import numpy as np
import ml_dtypes


def mxq(x, axis, fmt="e4m3"):
    dtype, down = {"e4m3": (ml_dtypes.float8_e4m3fn, 7), "e5m2": (ml_dtypes.float8_e5m2, 14)}[fmt]
    v = np.moveaxis(np.asarray(x, np.float32).astype(ml_dtypes.bfloat16).astype(np.float64), axis, -1)
    blocks = v.reshape(v.shape[:-1] + (-1, 32))
    amax = np.abs(blocks).max(-1, keepdims=True)
    byte = np.maximum(np.where(amax > 0, np.frexp(amax)[1] - 1 + 127, 0) - down, 1)
    scale = np.exp2(byte - 127.0)
    codes = (blocks / scale).astype(np.float32).astype(dtype).astype(np.float64)
    return np.moveaxis((codes * scale).reshape(v.shape), -1, axis)


WIDE = False


def mx_kscale(k):
    if not WIDE:
        return np.ones(k)
    levels = np.array([24, -24, 12, -12, 0])
    if k % 512:
        return np.exp2(np.random.permutation(np.resize(levels, k // 32))).repeat(32)
    a = np.empty((k // 512, 16))
    for p in range(k // 512):
        a[p, :8] = np.random.permutation(np.resize(levels, 8))
        for g in range(8):
            far = levels[np.abs(levels - a[p, g]) >= 10]
            a[p, g + 8] = far[np.random.randint(len(far))]
    return np.exp2(a.ravel()).repeat(32)


def f64(x):
    return np.asarray(x).astype(np.float64)


def striped(idx):
    return np.tile(idx.reshape(-1, 16).T, (8, 1)).astype(np.uint16)


def unstriped(offs):
    return offs[:16].T.reshape(-1).astype(np.int64)


E2M1 = np.array([0.0, 0.5, 1.0, 1.5, 2.0, 3.0, 4.0, 6.0, -0.0, -0.5, -1.0, -1.5, -2.0, -3.0, -4.0, -6.0])


def pack_weight(w, fmt):
    k, n = w.shape
    w = f64(np.asarray(w, np.float32).astype(ml_dtypes.bfloat16)).reshape(k // 32, 32, n)
    amax = np.abs(w).max(1)
    if fmt == "e4m3":
        byte = np.frexp(amax)[1] - 1 + 127 - 7
    else:
        mant, ex = np.frexp(amax / 6.0)
        byte = np.where(mant > 0.5, ex, ex - 1) + 127
    byte = np.clip(np.where(amax > 0, byte, 1), 1, 254)
    scaled = (w * np.exp2(127.0 - byte)[:, None, :]).reshape(k, n).astype(np.float32)
    by_word = np.ascontiguousarray(scaled.reshape(k // 512, 128, 4, n).transpose(0, 1, 3, 2))
    if fmt == "e4m3":
        words = by_word.astype(ml_dtypes.float8_e4m3fn).view(np.uint8)
    else:
        c = by_word.astype(ml_dtypes.float4_e2m1fn).view(np.uint8) & 0xF
        words = (c[..., 0::2] | (c[..., 1::2] << 4)).reshape(k // 512, 128, 2 * n)
    return np.ascontiguousarray(words), np.ascontiguousarray(byte.astype(np.uint8).reshape(k // 512, 16, n))


def unpack_weight(words, scales, fmt):
    g, _, n = scales.shape
    words = np.ascontiguousarray(words).reshape(g, 128, n, -1)
    if fmt == "e4m3":
        vals = words.view(ml_dtypes.float8_e4m3fn).astype(np.float64)
    else:
        nib = np.empty((g, 128, n, 4), np.uint8)
        nib[..., 0::2] = words & 0xF
        nib[..., 1::2] = words >> 4
        vals = E2M1[nib]
    vals = vals * np.repeat(np.exp2(scales.astype(np.float64) - 127.0), 8, axis=1)[..., None]
    return vals.transpose(0, 1, 3, 2).reshape(g * 512, n)


def pack_table4(v):
    words, scales = pack_weight(v, "e2m1")
    g, t = words.shape[0] // 2, v.shape[1]
    return np.ascontiguousarray(words.reshape(g, 2, 128, t, 2).transpose(0, 2, 3, 1, 4).reshape(g, 128, t, 4)), scales


def unpack_table4(words, scales):
    g, _, t, _ = words.shape
    return unpack_weight(words.reshape(g, 128, t, 2, 2).transpose(0, 3, 1, 2, 4).reshape(2 * g, 128, 2 * t), scales, "e2m1")


def gelu(f):
    return 0.5 * f * (1.0 + np.tanh(np.sqrt(2.0 / np.pi) * (f + 0.044715 * f**3)))


K, L, R, N, T, J = 512, 1024, 1024, 1024, 1024, 512


def setup_inputs():
    n = np.random.standard_normal
    s = mx_kscale(K)[:, None]
    s2 = mx_kscale(L)[:, None]
    u = mx_kscale(R)[:, None]
    en = n((R, N)) / np.sqrt(R) / u
    p_tab = pack_weight(n((K, T)) * s, "e4m3")
    p_tab2 = pack_table4(n((L, T)) * s2)
    p_wa = pack_weight(n((K, R)) / np.sqrt(K) / s, "e2m1")
    p_wb = pack_weight(n((L, R)) / np.sqrt(L) / s2, "e4m3")
    p_en8 = pack_weight(en[:512], "e4m3")
    p_en4 = pack_weight(en[512:], "e2m1")
    return {
        "tab_words": p_tab[0],
        "tab_scales": p_tab[1],
        "tab2_words": p_tab2[0],
        "tab2_scales": p_tab2[1],
        "wa_words": p_wa[0],
        "wa_scales": p_wa[1],
        "wb_words": p_wb[0],
        "wb_scales": p_wb[1],
        "sm": (np.random.uniform(0.5, 2.0, R) * u[:, 0]).astype(np.float32),
        "en8_words": p_en8[0],
        "en8_scales": p_en8[1],
        "en4_words": p_en4[0],
        "en4_scales": p_en4[1],
        "b": (0.3 * n(N)).astype(np.float32),
        "offs": striped(np.random.permutation(T)[:J]),
        "offs2": striped(np.random.permutation(T)[:J]),
    }


def reference(tab_words, tab_scales, tab2_words, tab2_scales, wa_words, wa_scales, wb_words, wb_scales, sm, en8_words, en8_scales, en4_words, en4_scales, b, offs, offs2):
    idx = unstriped(offs)
    idx2 = unstriped(offs2)
    tab_ = unpack_weight(tab_words, tab_scales, "e4m3")[:, idx]
    tab2_ = unpack_table4(tab2_words, tab2_scales)[:, idx2]
    wa_ = unpack_weight(wa_words, wa_scales, "e2m1")
    wb_ = unpack_weight(wb_words, wb_scales, "e4m3")
    ha = wa_.T @ tab_
    hb = wb_.T @ tab2_
    h = f64(sm)[:, None] * (ha - hb) ** 2
    h_ = mxq(h, 0, "e4m3")
    en8_ = unpack_weight(en8_words, en8_scales, "e4m3")
    en4_ = unpack_weight(en4_words, en4_scales, "e2m1")
    y = en8_.T @ h_[:512] + en4_.T @ h_[512:]
    return gelu(y + f64(b)[:, None])

@@ -1,0 +1,257 @@
+from contextlib import ExitStack
+
+import concourse.mybir as mybir
+
+K, L, R, N, T, J = 512, 1024, 1024, 1024, 1024, 512
+FLOPS = 2 * J * (K * R + L * R + R * N)
+
+F32 = mybir.dt.float32
+BF16 = mybir.dt.bfloat16
+I32 = mybir.dt.int32
+U32 = mybir.dt.uint32
+U16 = mybir.dt.uint16
+U8 = mybir.dt.uint8
+FP8X4 = mybir.dt.float8_e4m3fn_x4
+FP4X4 = mybir.dt.float4_e2m1fn_x4
+ACT = mybir.ActivationFunctionType
+ALU = mybir.AluOpType
+
+P = 128
+PASS = 512
+CHUNK = 128
+CHUNKS = J // CHUNK
+HALF = J // 2
+
+
+def tile_list_kg_sqd_mix_gelu_kernel(
+    tc, tab_words, tab_scales, tab2_words, tab2_scales, wa_words, wa_scales, wb_words, wb_scales,
+    sm, en8_words, en8_scales, en4_words, en4_scales, b, offs, offs2, out,
+):
+    nc = tc.nc
+    with ExitStack() as ctx:
+        keep = ctx.enter_context(tc.tile_pool(name="keep", bufs=1))
+        work = ctx.enter_context(tc.tile_pool(name="work", bufs=3))
+        psum = ctx.enter_context(tc.psum_pool(name="psum", bufs=2))
+        psum_y = ctx.enter_context(tc.psum_pool(name="psum_y", bufs=4))
+
+        idx = keep.tile([P, J // 16], U16, name="idx")
+        idx2 = keep.tile([P, J // 16], U16, name="idx2")
+        w_rows = keep.tile([P, R // 4], I32, name="w_rows", tag="rows", align_bytes=64)
+        tab_rows = keep.tile([P, T // 4], I32, name="tab_rows", align_bytes=64)
+        tab2_rows = keep.tile([P, T // 4], I32, name="tab2_rows", align_bytes=64)
+        en_rows = keep.tile([32, N // 4], I32, name="en_rows", align_bytes=64)
+        w_planes = keep.tile([P, 5, R // 4], I32, name="w_planes", align_bytes=64)
+        tab_planes = keep.tile([P, J], I32, name="tab_planes", align_bytes=64)
+        warm = keep.tile([P, 2], F32, name="warm")
+
+        nc.vector.memset(w_rows[:], 0)
+        nc.vector.memset(tab2_rows[:], 0)
+        nc.vector.memset(tab_rows[:], 0)
+        nc.vector.memset(warm[:], 0.0)
+        nc.vector.memset(w_planes[:], 0)
+        nc.vector.memset(tab_planes[:], 0)
+        nc.scalar.activation(warm[:, 1:2], warm[:, 0:1], ACT.Gelu_apprx_tanh)
+
+        wa_raw = keep.tile([P, R // 2], I32, name="wa_raw", tag="raw_a", align_bytes=64)
+        tab_win = keep.tile([P, T], I32, name="tab_win", align_bytes=64)
+        tab2_win = keep.tile([P, T], I32, name="tab2_win", align_bytes=64)
+        wb_hbm = wb_words.rearrange("a p n i -> p a (n i)")
+
+        nc.sync.dma_start(idx2[:], offs2)
+        nc.sync.dma_start(idx[:], offs)
+        nc.sync.dma_start(w_rows[0:64:4, :], wa_scales[0].bitcast(I32))
+        nc.sync.dma_start(w_rows[1:64:4, :], wb_scales[0].bitcast(I32))
+        nc.sync.dma_start(w_rows[2:64:4, :], wb_scales[1].bitcast(I32))
+        nc.sync.dma_start(tab2_rows[0:32, :], tab2_scales.rearrange("a q t -> q a t").bitcast(I32))
+        nc.sync.dma_start(tab_rows[0:32:2, :], tab_scales[0].bitcast(I32))
+        nc.sync.dma_start(tab2_win[:], tab2_words[0].rearrange("p t i -> p (t i)").bitcast(I32))
+        nc.sync.dma_start(tab_win[:], tab_words[0].rearrange("p t i -> p (t i)").bitcast(I32))
+        nc.sync.dma_start(wa_raw[:], wa_words[0].bitcast(I32))
+
+        sm_cols = keep.tile([P, 2, 4], F32, name="sm_cols")
+        bias = keep.tile([P, N // P], F32, name="bias")
+        nc.gpsimd.dma_start(en_rows[0:32:2, :], en8_scales[0].bitcast(I32))
+        nc.gpsimd.dma_start(en_rows[1:32:2, :], en4_scales[0].bitcast(I32))
+        nc.gpsimd.dma_start(sm_cols[:], sm.rearrange("(g p t) -> p g t", g=2, t=4))
+        with nc.allow_non_contiguous_dma(reason="one bias value for each partition"):
+            nc.gpsimd.dma_start(bias[:], b.rearrange("(s p) -> p s", p=P))
+
+        w_rows_t = keep.tile([P, R // 4], I32, name="w_rows_t", tag="rows_t", align_bytes=64)
+        nc.vector.tensor_copy(
+            w_rows_t[:].bitcast(U8).rearrange("p (g t c i) -> p g c t i", g=2, t=4, i=16),
+            w_rows[:].bitcast(U8).rearrange("p (g c i t) -> p g c t i", g=2, t=4, i=16),
+        )
+        for q in range(4):
+            nc.sync.dma_start(w_planes[32 * q : 32 * q + 4, 0:4, :], w_rows_t[16 * q : 16 * q + 16, :])
+        wb_raw0 = keep.tile([P, 2, PASS], I32, name="wb_raw0", tag="rows", align_bytes=64)
+        nc.sync.dma_start(wb_raw0[:], wb_hbm[:, :, 0 : 4 * PASS].bitcast(I32))
+
+        picked_rows = keep.tile([P, 2 * J // 4], I32, name="picked_rows", tag="picked", align_bytes=64)
+        nc.vector.tensor_copy(picked_rows[:].bitcast(U8)[:, J:], tab2_rows[:].bitcast(U8).indirect(idx2[:]))
+        nc.vector.tensor_copy(picked_rows[:].bitcast(U8)[:, :J], tab_rows[:].bitcast(U8).indirect(idx[:]))
+        for q in range(4):
+            nc.sync.dma_start(
+                tab_planes[32 * q : 32 * q + 4, :].rearrange("p (a n) -> p a n", a=2), picked_rows[8 * q : 8 * q + 8, :]
+            )
+        wb_raw1 = keep.tile([P, 2, PASS], I32, name="wb_raw1", tag="rows_t", align_bytes=64)
+        nc.sync.dma_start(wb_raw1[:], wb_hbm[:, :, 4 * PASS :].bitcast(I32))
+        for q in range(4):
+            nc.sync.dma_start(w_planes[32 * q : 32 * q + 4, 3:5, :], en_rows[8 * q : 8 * q + 8, :])
+
+        tab_codes = []
+        tab2_codes = []
+
+        def gather_half(half):
+            cols = slice(half * HALF // 16, (half + 1) * HALF // 16)
+            picked = keep.tile([P, HALF], U32, name=f"tab_codes{half}", align_bytes=64)
+            nc.vector.tensor_copy(picked[:], tab_win[:].bitcast(U32).indirect(idx[:, cols]))
+            pairs = keep.tile([P, HALF], U32, name=f"tab2_pairs{half}", align_bytes=64)
+            nc.vector.tensor_copy(pairs[:], tab2_win[:].bitcast(U32).indirect(idx2[:, cols]))
+            tab_codes.append(picked)
+            return pairs
+
+        def part_half(half, pairs):
+            parted = keep.tile([P, 2, HALF], U16, name=f"tab2_codes{half}", align_bytes=64)
+            nc.vector.tensor_copy(
+                parted[:].rearrange("p d (c i) -> p c d i", i=8),
+                pairs[:].bitcast(U16).rearrange("p (c i d) -> p c d i", d=2, i=8),
+            )
+            tab2_codes.append(parted)
+
+        wb_t = []
+
+        def reorder_wb(g, raw):
+            t = keep.tile([P, 2, PASS], I32, name=f"wb_t{g}", align_bytes=64)
+            nc.vector.tensor_copy(
+                t[:].rearrange("p a (t c i) -> p a c t i", t=4, i=4),
+                raw[:].rearrange("p a (c i t) -> p a c t i", t=4, i=4),
+            )
+            wb_t.append(t)
+
+        pairs0 = gather_half(0)
+        part_half(0, pairs0)
+        wa_t = keep.tile([P, R], U16, name="wa_t", align_bytes=64)
+        nc.vector.tensor_copy(
+            wa_t[:].rearrange("p (g t c i) -> p g c t i", g=2, t=4, i=8),
+            wa_raw[:].bitcast(U16).rearrange("p (g c i t) -> p g c t i", g=2, t=4, i=8),
+        )
+        en4_codes = keep.tile([P, N // 2], I32, name="en4_codes", tag="raw_a", align_bytes=64)
+        nc.sync.dma_start(en4_codes[:], en4_words[0].bitcast(I32))
+        en8_codes = keep.tile([P, N], I32, name="en8_codes", tag="picked", align_bytes=64)
+        nc.sync.dma_start(en8_codes[:], en8_words[0].rearrange("p n i -> p (n i)").bitcast(I32))
+        reorder_wb(0, wb_raw0)
+        pairs1 = gather_half(1)
+        reorder_wb(1, wb_raw1)
+        part_half(1, pairs1)
+
+        sm_wide = keep.tile([P, 2, CHUNK, 4], F32, name="sm_wide")
+        for g in range(2):
+            nc.scalar.copy(sm_wide[:, g], sm_cols[:, g, :].unsqueeze(1).to_broadcast([P, CHUNK, 4]))
+
+        w_scale = w_planes[:].rearrange("p k n -> p (k n)").bitcast(U8)
+        tab_scale = tab_planes[:].bitcast(U8)
+        en_scale = w_scale[:, 3 * R :]
+        en8_flat = en8_codes[:]
+        en4_flat = en4_codes[:].bitcast(U16)
+        out_v = out.rearrange("(s p) j -> p s j", p=P)
+
+        units = [(c, g) for c in range(CHUNKS) for g in range(2)]
+        state = {}
+
+        def project(u):
+            c, g = units[u]
+            half, j0 = divmod(c * CHUNK, HALF)
+            ha = psum.tile([P, PASS], F32, name="ha")
+            hb = psum.tile([P, PASS], F32, name="hb")
+            for t in range(4):
+                r0 = g * PASS + t * P
+                nc.tensor.matmul_mx(
+                    out=ha[:, t * P : (t + 1) * P],
+                    lhsT=wa_t[:, r0 : r0 + P].bitcast(FP4X4),
+                    lhsT_scale=w_scale[:, r0 : r0 + P],
+                    rhs=tab_codes[half][:, j0 : j0 + CHUNK].bitcast(FP8X4),
+                    rhs_scale=tab_scale[:, c * CHUNK : (c + 1) * CHUNK],
+                    start=True,
+                    stop=True,
+                )
+            for t in range(4):
+                r0 = g * PASS + t * P
+                for a in range(2):
+                    s0 = (2 * a + 1) * J + c * CHUNK
+                    nc.tensor.matmul_mx(
+                        out=hb[:, t * P : (t + 1) * P],
+                        lhsT=wb_t[g][:, a, t * P : (t + 1) * P].bitcast(FP8X4),
+                        lhsT_scale=w_scale[:, (1 + a) * R + r0 : (1 + a) * R + r0 + P],
+                        rhs=tab2_codes[half][:, a, j0 : j0 + CHUNK].bitcast(FP4X4),
+                        rhs_scale=tab_scale[:, s0 : s0 + CHUNK],
+                        start=(a == 0),
+                        stop=(a == 1),
+                    )
+            ha_sb = work.tile([P, CHUNK, 4], F32, name="ha_sb")
+            nc.scalar.copy(ha_sb[:], ha[:].rearrange("p (t j) -> p j t", t=4))
+            state[u] = (ha_sb, hb)
+
+        def difference(u):
+            ha_sb, hb = state[u]
+            diff = work.tile([P, CHUNK, 4], F32, name="diff")
+            nc.vector.tensor_tensor(diff[:], hb[:].rearrange("p (t j) -> p j t", t=4), ha_sb[:], ALU.subtract)
+            square = work.tile([P, CHUNK, 4], F32, name="square")
+            nc.scalar.activation(square[:], diff[:], ACT.Square)
+            state[u] = square
+
+        def smooth(u):
+            g = units[u][1]
+            h = work.tile([P, CHUNK, 4], BF16, name="h", align_bytes=64)
+            nc.vector.tensor_tensor(h[:], state[u][:], sm_wide[:, g], ALU.mult)
+            state[u] = h
+
+        def quantise(u):
+            codes = work.tile([P, CHUNK], U32, name="h_codes", bufs=4, align_bytes=64)
+            scales = work.tile([P, CHUNK], U8, name="h_scales", bufs=4, align_bytes=64)
+            nc.vector.quantize_mx(out=codes[:].bitcast(FP8X4), scales=scales[:], in_=state[u][:].rearrange("p j t -> p (j t)"))
+            state[u] = (codes, scales)
+
+        banks = {}
+
+        def score(u):
+            c, g = units[u]
+            codes, scales = state[u]
+            for half in range(2):
+                if g == 0:
+                    banks[half] = psum_y.tile([P, 4, CHUNK], F32, name="y")
+                for s in range(4):
+                    n0 = (4 * half + s) * P
+                    if g == 0:
+                        lhs = en8_flat[:, n0 : n0 + P].bitcast(FP8X4)
+                    else:
+                        lhs = en4_flat[:, n0 : n0 + P].bitcast(FP4X4)
+                    nc.tensor.matmul_mx(
+                        out=banks[half][:, s, :],
+                        lhsT=lhs,
+                        lhsT_scale=en_scale[:, g * N + n0 : g * N + n0 + P],
+                        rhs=codes[:].bitcast(FP8X4),
+                        rhs_scale=scales[:],
+                        start=(g == 0 and s == 0),
+                        stop=(g == 1 and s == 3),
+                    )
+                if g == 1:
+                    res = work.tile([P, 4, CHUNK], F32, name="res")
+                    for s in range(4):
+                        nc.scalar.activation(
+                            res[:, s, :], banks[half][:, s, :], ACT.Gelu_apprx_tanh,
+                            bias=bias[:, 4 * half + s : 4 * half + s + 1],
+                        )
+                    nc.sync.dma_start(out_v[:, 4 * half : 4 * half + 4, c * CHUNK : (c + 1) * CHUNK], res[:])
+
+        last = len(units)
+        project(0)
+        for step in range(last + 2):
+            if step + 1 < last:
+                project(step + 1)
+            if step < last:
+                difference(step)
+            if 0 <= step - 2:
+                quantise(step - 2)
+                score(step - 2)
+            if 0 <= step - 1 < last:
+                smooth(step - 1)

@@ -1,6 +1,7 @@
 from contextlib import ExitStack
 
 import concourse.mybir as mybir
+from concourse.masks import make_identity
 
 K, L, R, N, T, J = 512, 1024, 1024, 1024, 1024, 512
 FLOPS = 2 * J * (K * R + L * R + R * N)
@@ -36,67 +37,76 @@ def tile_list_kg_sqd_mix_gelu_kernel(
 
         idx = keep.tile([P, J // 16], U16, name="idx")
         idx2 = keep.tile([P, J // 16], U16, name="idx2")
-        w_rows = keep.tile([P, R // 4], I32, name="w_rows", tag="rows", align_bytes=64)
-        tab_rows = keep.tile([P, T // 4], I32, name="tab_rows", align_bytes=64)
+        w_rows = keep.tile([P, R // 4], I32, name="w_rows", align_bytes=64)
+        tab_rows = keep.tile([P, T // 4], I32, name="tab_rows", tag="late_wb", align_bytes=64)
         tab2_rows = keep.tile([P, T // 4], I32, name="tab2_rows", align_bytes=64)
         en_rows = keep.tile([32, N // 4], I32, name="en_rows", align_bytes=64)
-        w_planes = keep.tile([P, 5, R // 4], I32, name="w_planes", align_bytes=64)
-        tab_planes = keep.tile([P, J], I32, name="tab_planes", align_bytes=64)
+        w_planes = keep.tile([P, 4, R // 4], I32, name="w_planes", align_bytes=64)
+        tab_planes = keep.tile([P, (3 * J + 2 * N) // 4], I32, name="tab_planes", align_bytes=64)
         warm = keep.tile([P, 2], F32, name="warm")
+
+        vectors = keep.tile([P, PASS + P], F32, name="vectors")
+        ident = keep.tile([P, P], F32, name="ident")
 
         nc.vector.memset(w_rows[:], 0)
         nc.vector.memset(tab2_rows[:], 0)
         nc.vector.memset(tab_rows[:], 0)
         nc.vector.memset(warm[:], 0.0)
+        nc.vector.memset(vectors[:], 0.0)
         nc.vector.memset(w_planes[:], 0)
         nc.vector.memset(tab_planes[:], 0)
         nc.scalar.activation(warm[:, 1:2], warm[:, 0:1], ACT.Gelu_apprx_tanh)
 
-        wa_raw = keep.tile([P, R // 2], I32, name="wa_raw", tag="raw_a", align_bytes=64)
+        wa_raw = keep.tile([P, R // 2], I32, name="wa_raw", align_bytes=64)
         tab_win = keep.tile([P, T], I32, name="tab_win", align_bytes=64)
         tab2_win = keep.tile([P, T], I32, name="tab2_win", align_bytes=64)
         wb_hbm = wb_words.rearrange("a p n i -> p a (n i)")
 
+        def by_row(scales):
+            return scales.rearrange("(q r) n -> r q n", r=4).bitcast(I32)
+
         nc.sync.dma_start(idx2[:], offs2)
         nc.sync.dma_start(idx[:], offs)
-        nc.sync.dma_start(w_rows[0:64:4, :], wa_scales[0].bitcast(I32))
-        nc.sync.dma_start(w_rows[1:64:4, :], wb_scales[0].bitcast(I32))
-        nc.sync.dma_start(w_rows[2:64:4, :], wb_scales[1].bitcast(I32))
+        nc.sync.dma_start(w_rows[0:64:4, :], by_row(wa_scales[0]))
+        nc.sync.dma_start(w_rows[1:64:4, :], by_row(wb_scales[0]))
+        nc.sync.dma_start(w_rows[2:64:4, :], by_row(wb_scales[1]))
         nc.sync.dma_start(tab2_rows[0:32, :], tab2_scales.rearrange("a q t -> q a t").bitcast(I32))
         nc.sync.dma_start(tab_rows[0:32:2, :], tab_scales[0].bitcast(I32))
         nc.sync.dma_start(tab2_win[:], tab2_words[0].rearrange("p t i -> p (t i)").bitcast(I32))
         nc.sync.dma_start(tab_win[:], tab_words[0].rearrange("p t i -> p (t i)").bitcast(I32))
         nc.sync.dma_start(wa_raw[:], wa_words[0].bitcast(I32))
 
-        sm_cols = keep.tile([P, 2, 4], F32, name="sm_cols")
-        bias = keep.tile([P, N // P], F32, name="bias")
-        nc.gpsimd.dma_start(en_rows[0:32:2, :], en8_scales[0].bitcast(I32))
-        nc.gpsimd.dma_start(en_rows[1:32:2, :], en4_scales[0].bitcast(I32))
-        nc.gpsimd.dma_start(sm_cols[:], sm.rearrange("(g p t) -> p g t", g=2, t=4))
-        with nc.allow_non_contiguous_dma(reason="one bias value for each partition"):
-            nc.gpsimd.dma_start(bias[:], b.rearrange("(s p) -> p s", p=P))
+        make_identity(nc, ident[:])
+        nc.gpsimd.dma_start(vectors[0:2, 0:PASS], sm.rearrange("(g r) -> g r", g=2))
+        nc.gpsimd.dma_start(vectors[0:8, PASS:], b.rearrange("(s p) -> s p", p=P))
+        nc.gpsimd.dma_start(en_rows[0:32:2, :], by_row(en8_scales[0]))
+        nc.gpsimd.dma_start(en_rows[1:32:2, :], by_row(en4_scales[0]))
 
-        w_rows_t = keep.tile([P, R // 4], I32, name="w_rows_t", tag="rows_t", align_bytes=64)
+        w_rows_t = keep.tile([P, R // 4], I32, name="w_rows_t", align_bytes=64)
         nc.vector.tensor_copy(
             w_rows_t[:].bitcast(U8).rearrange("p (g t c i) -> p g c t i", g=2, t=4, i=16),
             w_rows[:].bitcast(U8).rearrange("p (g c i t) -> p g c t i", g=2, t=4, i=16),
         )
-        for q in range(4):
-            nc.sync.dma_start(w_planes[32 * q : 32 * q + 4, 0:4, :], w_rows_t[16 * q : 16 * q + 16, :])
-        wb_raw0 = keep.tile([P, 2, PASS], I32, name="wb_raw0", tag="rows", align_bytes=64)
-        nc.sync.dma_start(wb_raw0[:], wb_hbm[:, :, 0 : 4 * PASS].bitcast(I32))
+        for r in range(4):
+            nc.scalar.dma_start(w_planes[r:P:32, :, :], w_rows_t[16 * r : 16 * r + 16, :])
 
-        picked_rows = keep.tile([P, 2 * J // 4], I32, name="picked_rows", tag="picked", align_bytes=64)
-        nc.vector.tensor_copy(picked_rows[:].bitcast(U8)[:, J:], tab2_rows[:].bitcast(U8).indirect(idx2[:]))
-        nc.vector.tensor_copy(picked_rows[:].bitcast(U8)[:, :J], tab_rows[:].bitcast(U8).indirect(idx[:]))
-        for q in range(4):
+        picked_rows = keep.tile([P, 2 * J // 4], I32, name="picked_rows", tag="late_en", align_bytes=64)
+        nc.vector.tensor_copy(picked_rows[:].bitcast(U8)[:, :J], tab2_rows[:].bitcast(U8).indirect(idx2[:]))
+        nc.vector.tensor_copy(picked_rows[:].bitcast(U8)[:, J:], tab_rows[:].bitcast(U8).indirect(idx[:]))
+        for q in (0, 2, 1, 3):
             nc.sync.dma_start(
-                tab_planes[32 * q : 32 * q + 4, :].rearrange("p (a n) -> p a n", a=2), picked_rows[8 * q : 8 * q + 8, :]
+                tab_planes[32 * q : 32 * q + 4, 0:J].rearrange("p (a n) -> p a n", a=2), picked_rows[8 * q : 8 * q + 8, :]
             )
-        wb_raw1 = keep.tile([P, 2, PASS], I32, name="wb_raw1", tag="rows_t", align_bytes=64)
-        nc.sync.dma_start(wb_raw1[:], wb_hbm[:, :, 4 * PASS :].bitcast(I32))
-        for q in range(4):
-            nc.sync.dma_start(w_planes[32 * q : 32 * q + 4, 3:5, :], en_rows[8 * q : 8 * q + 8, :])
+        wb_raw = keep.tile([P, 2, 2, PASS], I32, name="wb_raw", tag="late_wb", align_bytes=64)
+        for g in range(2):
+            nc.sync.dma_start(wb_raw[:, g], wb_hbm[:, :, 4 * g * PASS : 4 * (g + 1) * PASS].bitcast(I32))
+        for r in range(4):
+            nc.sync.dma_start(
+                tab_planes[r:P:32, 3 * J // 4 :].rearrange("p (k n) -> p k n", k=2), en_rows[8 * r : 8 * r + 8, :]
+            )
+        en_codes = keep.tile([P, N + N // 2], I32, name="en_codes", tag="late_en", align_bytes=64)
+        nc.sync.dma_start(en_codes[:, :N], en8_words[0].rearrange("p n i -> p (n i)").bitcast(I32))
+        nc.sync.dma_start(en_codes[:, N:], en4_words[0].bitcast(I32))
 
         tab_codes = []
         tab2_codes = []
@@ -124,35 +134,38 @@ def tile_list_kg_sqd_mix_gelu_kernel(
             t = keep.tile([P, 2, PASS], I32, name=f"wb_t{g}", align_bytes=64)
             nc.vector.tensor_copy(
                 t[:].rearrange("p a (t c i) -> p a c t i", t=4, i=4),
-                raw[:].rearrange("p a (c i t) -> p a c t i", t=4, i=4),
+                raw.rearrange("p a (c i t) -> p a c t i", t=4, i=4),
             )
             wb_t.append(t)
 
         pairs0 = gather_half(0)
-        part_half(0, pairs0)
         wa_t = keep.tile([P, R], U16, name="wa_t", align_bytes=64)
         nc.vector.tensor_copy(
             wa_t[:].rearrange("p (g t c i) -> p g c t i", g=2, t=4, i=8),
             wa_raw[:].bitcast(U16).rearrange("p (g c i t) -> p g c t i", g=2, t=4, i=8),
         )
-        en4_codes = keep.tile([P, N // 2], I32, name="en4_codes", tag="raw_a", align_bytes=64)
-        nc.sync.dma_start(en4_codes[:], en4_words[0].bitcast(I32))
-        en8_codes = keep.tile([P, N], I32, name="en8_codes", tag="picked", align_bytes=64)
-        nc.sync.dma_start(en8_codes[:], en8_words[0].rearrange("p n i -> p (n i)").bitcast(I32))
-        reorder_wb(0, wb_raw0)
+        part_half(0, pairs0)
         pairs1 = gather_half(1)
-        reorder_wb(1, wb_raw1)
+        reorder_wb(0, wb_raw[:, 0])
         part_half(1, pairs1)
+        reorder_wb(1, wb_raw[:, 1])
 
+        turned = psum_y.tile([P, 4, CHUNK], F32, name="y")
+        for t in range(4):
+            nc.tensor.transpose(turned[:, t, :], vectors[:, t:PASS:4], ident[:])
+        turned_b = psum_y.tile([P, 4, CHUNK], F32, name="y")
+        nc.tensor.transpose(turned_b[:, 0, :], vectors[:, PASS:], ident[:])
         sm_wide = keep.tile([P, 2, CHUNK, 4], F32, name="sm_wide")
         for g in range(2):
-            nc.scalar.copy(sm_wide[:, g], sm_cols[:, g, :].unsqueeze(1).to_broadcast([P, CHUNK, 4]))
+            nc.scalar.copy(sm_wide[:, g], turned[:, :, g].unsqueeze(1).to_broadcast([P, CHUNK, 4]))
+        bias = keep.tile([P, N // P], F32, name="bias")
+        nc.scalar.copy(bias[:], turned_b[:, 0, 0 : N // P])
 
         w_scale = w_planes[:].rearrange("p k n -> p (k n)").bitcast(U8)
         tab_scale = tab_planes[:].bitcast(U8)
-        en_scale = w_scale[:, 3 * R :]
-        en8_flat = en8_codes[:]
-        en4_flat = en4_codes[:].bitcast(U16)
+        en_scale = tab_scale[:, 3 * J :]
+        en8_flat = en_codes[:, :N]
+        en4_flat = en_codes[:, N:].bitcast(U16)
         out_v = out.rearrange("(s p) j -> p s j", p=P)
 
         units = [(c, g) for c in range(CHUNKS) for g in range(2)]
@@ -170,14 +183,14 @@ def tile_list_kg_sqd_mix_gelu_kernel(
                     lhsT=wa_t[:, r0 : r0 + P].bitcast(FP4X4),
                     lhsT_scale=w_scale[:, r0 : r0 + P],
                     rhs=tab_codes[half][:, j0 : j0 + CHUNK].bitcast(FP8X4),
-                    rhs_scale=tab_scale[:, c * CHUNK : (c + 1) * CHUNK],
+                    rhs_scale=tab_scale[:, J + c * CHUNK : J + (c + 1) * CHUNK],
                     start=True,
                     stop=True,
                 )
             for t in range(4):
                 r0 = g * PASS + t * P
                 for a in range(2):
-                    s0 = (2 * a + 1) * J + c * CHUNK
+                    s0 = 2 * a * J + c * CHUNK
                     nc.tensor.matmul_mx(
                         out=hb[:, t * P : (t + 1) * P],
                         lhsT=wb_t[g][:, a, t * P : (t + 1) * P].bitcast(FP8X4),
@@ -187,7 +200,7 @@ def tile_list_kg_sqd_mix_gelu_kernel(
                         start=(a == 0),
                         stop=(a == 1),
                     )
-            ha_sb = work.tile([P, CHUNK, 4], F32, name="ha_sb")
+            ha_sb = work.tile([P, CHUNK, 4], F32, name="ha_sb", bufs=8)
             nc.scalar.copy(ha_sb[:], ha[:].rearrange("p (t j) -> p j t", t=4))
             state[u] = (ha_sb, hb)
 

@@ -1,7 +1,6 @@
 from contextlib import ExitStack
 
 import concourse.mybir as mybir
-from concourse.masks import make_identity
 
 K, L, R, N, T, J = 512, 1024, 1024, 1024, 1024, 512
 FLOPS = 2 * J * (K * R + L * R + R * N)
@@ -22,6 +21,9 @@ PASS = 512
 CHUNK = 128
 CHUNKS = J // CHUNK
 HALF = J // 2
+STAGE = 96
+SLOT = 2048
+HA_AHEAD = 3
 
 
 def tile_list_kg_sqd_mix_gelu_kernel(
@@ -31,183 +33,173 @@ def tile_list_kg_sqd_mix_gelu_kernel(
     nc = tc.nc
     with ExitStack() as ctx:
         keep = ctx.enter_context(tc.tile_pool(name="keep", bufs=1))
+        after_tab = ctx.enter_context(tc.tile_pool(name="after_tab", bufs=1))
         work = ctx.enter_context(tc.tile_pool(name="work", bufs=3))
         psum = ctx.enter_context(tc.psum_pool(name="psum", bufs=2))
         psum_y = ctx.enter_context(tc.psum_pool(name="psum_y", bufs=4))
 
         idx = keep.tile([P, J // 16], U16, name="idx")
         idx2 = keep.tile([P, J // 16], U16, name="idx2")
-        w_rows = keep.tile([P, R // 4], I32, name="w_rows", align_bytes=64)
-        tab_rows = keep.tile([P, T // 4], I32, name="tab_rows", tag="late_wb", align_bytes=64)
-        tab2_rows = keep.tile([P, T // 4], I32, name="tab2_rows", align_bytes=64)
-        en_rows = keep.tile([32, N // 4], I32, name="en_rows", align_bytes=64)
-        w_planes = keep.tile([P, 4, R // 4], I32, name="w_planes", align_bytes=64)
-        tab_planes = keep.tile([P, (3 * J + 2 * N) // 4], I32, name="tab_planes", align_bytes=64)
+        tab_rows = after_tab.tile([P, T // 4], I32, name="tab_rows", offset=3584, align_bytes=64)
+        tab2_rows = keep.tile([P, T // 4], I32, name="tab2_rows", tag="then_en_rows", align_bytes=64)
+        w_rows = keep.tile([P, 3 * PASS // 4], I32, name="w_rows", align_bytes=64)
+        staged = keep.tile([P, SLOT // 4], I32, name="staged", align_bytes=64)
+        planes = keep.tile([P, 2 * SLOT // 4], I32, name="planes", align_bytes=64)
+        en_planes = keep.tile([P, 2 * N // 4], I32, name="en_planes", align_bytes=64)
         warm = keep.tile([P, 2], F32, name="warm")
+        tab_win = keep.tile([P, T], I32, name="tab_win", tag="then_en8", align_bytes=64)
+        tab2_win = keep.tile([P, T], I32, name="tab2_win", align_bytes=64)
+        wa_raw = keep.tile([P, R // 2], I32, name="wa_raw", tag="then_en4", align_bytes=64)
+        wb_raw0 = keep.tile([P, 2, PASS], I32, name="wb_raw0", align_bytes=64)
+        wb_hbm = wb_words.rearrange("a p n i -> p a (n i)")
+        sm_sb = keep.tile([P, 2, 4], F32, name="sm_sb")
 
-        vectors = keep.tile([P, PASS + P], F32, name="vectors")
-        ident = keep.tile([P, P], F32, name="ident")
-
-        nc.vector.memset(w_rows[:], 0)
-        nc.vector.memset(tab2_rows[:], 0)
         nc.vector.memset(tab_rows[:], 0)
-        nc.vector.memset(warm[:], 0.0)
-        nc.vector.memset(vectors[:], 0.0)
-        nc.vector.memset(w_planes[:], 0)
-        nc.vector.memset(tab_planes[:], 0)
+        nc.vector.memset(tab2_rows[0:STAGE, :], 0)
+        nc.vector.memset(w_rows[0:STAGE, :], 0)
+        nc.gpsimd.memset(warm[:], 0.0)
+        nc.gpsimd.memset(planes[:], 0)
+        nc.gpsimd.memset(en_planes[:], 0)
         nc.scalar.activation(warm[:, 1:2], warm[:, 0:1], ACT.Gelu_apprx_tanh)
 
-        wa_raw = keep.tile([P, R // 2], I32, name="wa_raw", align_bytes=64)
-        tab_win = keep.tile([P, T], I32, name="tab_win", align_bytes=64)
-        tab2_win = keep.tile([P, T], I32, name="tab2_win", align_bytes=64)
-        wb_hbm = wb_words.rearrange("a p n i -> p a (n i)")
-
-        def by_row(scales):
-            return scales.rearrange("(q r) n -> r q n", r=4).bitcast(I32)
-
         nc.sync.dma_start(idx2[:], offs2)
+        nc.sync.dma_start(tab2_rows[STAGE:, :], tab2_scales.rearrange("a q t -> q a t").bitcast(I32))
+        nc.sync.dma_start(w_rows[STAGE:, : R // 4], wb_scales.rearrange("a q n -> q a n").bitcast(I32))
+        nc.sync.dma_start(w_rows[STAGE:, R // 4 :], wa_scales[0].rearrange("q (g n) -> (q g) n", g=2).bitcast(I32))
         nc.sync.dma_start(idx[:], offs)
-        nc.sync.dma_start(w_rows[0:64:4, :], by_row(wa_scales[0]))
-        nc.sync.dma_start(w_rows[1:64:4, :], by_row(wb_scales[0]))
-        nc.sync.dma_start(w_rows[2:64:4, :], by_row(wb_scales[1]))
-        nc.sync.dma_start(tab2_rows[0:32, :], tab2_scales.rearrange("a q t -> q a t").bitcast(I32))
-        nc.sync.dma_start(tab_rows[0:32:2, :], tab_scales[0].bitcast(I32))
-        nc.sync.dma_start(tab2_win[:], tab2_words[0].rearrange("p t i -> p (t i)").bitcast(I32))
         nc.sync.dma_start(tab_win[:], tab_words[0].rearrange("p t i -> p (t i)").bitcast(I32))
         nc.sync.dma_start(wa_raw[:], wa_words[0].bitcast(I32))
+        nc.sync.dma_start(tab2_win[:], tab2_words[0].rearrange("p t i -> p (t i)").bitcast(I32))
+        for q in range(4):
+            nc.sync.dma_start(tab_rows[32 * q : 32 * q + 4, :], tab_scales[0, 4 * q : 4 * q + 4, :].bitcast(I32))
+        nc.sync.dma_start(wb_raw0[:], wb_hbm[:, :, : 4 * PASS].bitcast(I32))
+        nc.sync.dma_start(sm_sb[:], sm.rearrange("(g p t) -> p g t", g=2, t=4))
 
-        make_identity(nc, ident[:])
-        nc.gpsimd.dma_start(vectors[0:2, 0:PASS], sm.rearrange("(g r) -> g r", g=2))
-        nc.gpsimd.dma_start(vectors[0:8, PASS:], b.rearrange("(s p) -> s p", p=P))
-        nc.gpsimd.dma_start(en_rows[0:32:2, :], by_row(en8_scales[0]))
-        nc.gpsimd.dma_start(en_rows[1:32:2, :], by_row(en4_scales[0]))
-
-        w_rows_t = keep.tile([P, R // 4], I32, name="w_rows_t", align_bytes=64)
+        picked2 = keep.tile([P, J // 4], I32, name="picked2", tag="then_wb1", align_bytes=64)
+        nc.vector.tensor_copy(picked2[:].bitcast(U8), tab2_rows[:].bitcast(U8).indirect(idx2[:]))
         nc.vector.tensor_copy(
-            w_rows_t[:].bitcast(U8).rearrange("p (g t c i) -> p g c t i", g=2, t=4, i=16),
-            w_rows[:].bitcast(U8).rearrange("p (g c i t) -> p g c t i", g=2, t=4, i=16),
+            staged[:, : 3 * PASS // 4].bitcast(U8).rearrange("p (g t c i) -> p c g t i", g=3, t=4, i=16),
+            w_rows[:].bitcast(U8).rearrange("p (g c i t) -> p c g t i", g=3, t=4, i=16),
         )
-        for r in range(4):
-            nc.scalar.dma_start(w_planes[r:P:32, :, :], w_rows_t[16 * r : 16 * r + 16, :])
-
-        picked_rows = keep.tile([P, 2 * J // 4], I32, name="picked_rows", tag="late_en", align_bytes=64)
-        nc.vector.tensor_copy(picked_rows[:].bitcast(U8)[:, :J], tab2_rows[:].bitcast(U8).indirect(idx2[:]))
-        nc.vector.tensor_copy(picked_rows[:].bitcast(U8)[:, J:], tab_rows[:].bitcast(U8).indirect(idx[:]))
+        nc.vector.tensor_copy(staged[STAGE:, 3 * PASS // 4 :], picked2[STAGE:, :])
         for q in (0, 2, 1, 3):
             nc.sync.dma_start(
-                tab_planes[32 * q : 32 * q + 4, 0:J].rearrange("p (a n) -> p a n", a=2), picked_rows[8 * q : 8 * q + 8, :]
+                planes[32 * q : 32 * q + 4, :].rearrange("p (k n) -> p k n", k=2),
+                staged[STAGE + 8 * q : STAGE + 8 * q + 8, :],
             )
-        wb_raw = keep.tile([P, 2, 2, PASS], I32, name="wb_raw", tag="late_wb", align_bytes=64)
-        for g in range(2):
-            nc.sync.dma_start(wb_raw[:, g], wb_hbm[:, :, 4 * g * PASS : 4 * (g + 1) * PASS].bitcast(I32))
-        for r in range(4):
+        wb_raw1 = keep.tile([P, 2, PASS], I32, name="wb_raw1", tag="then_wb1", align_bytes=64)
+        nc.sync.dma_start(wb_raw1[:], wb_hbm[:, :, 4 * PASS :].bitcast(I32))
+        wb_raw = [wb_raw0, wb_raw1]
+
+        en_rows = keep.tile([32, N // 4], I32, name="en_rows", tag="then_en_rows", align_bytes=64)
+        nc.sync.dma_start(en_rows[0:32:2, :], en8_scales[0].bitcast(I32))
+        nc.sync.dma_start(en_rows[1:32:2, :], en4_scales[0].bitcast(I32))
+        for q in (0, 2, 1, 3):
             nc.sync.dma_start(
-                tab_planes[r:P:32, 3 * J // 4 :].rearrange("p (k n) -> p k n", k=2), en_rows[8 * r : 8 * r + 8, :]
+                en_planes[32 * q : 32 * q + 4, :].rearrange("p (k n) -> p k n", k=2), en_rows[8 * q : 8 * q + 8, :]
             )
-        en_codes = keep.tile([P, N + N // 2], I32, name="en_codes", tag="late_en", align_bytes=64)
-        nc.sync.dma_start(en_codes[:, :N], en8_words[0].rearrange("p n i -> p (n i)").bitcast(I32))
-        nc.sync.dma_start(en_codes[:, N:], en4_words[0].bitcast(I32))
 
-        tab_codes = []
-        tab2_codes = []
-
-        def gather_half(half):
-            cols = slice(half * HALF // 16, (half + 1) * HALF // 16)
-            picked = keep.tile([P, HALF], U32, name=f"tab_codes{half}", align_bytes=64)
-            nc.vector.tensor_copy(picked[:], tab_win[:].bitcast(U32).indirect(idx[:, cols]))
-            pairs = keep.tile([P, HALF], U32, name=f"tab2_pairs{half}", align_bytes=64)
-            nc.vector.tensor_copy(pairs[:], tab2_win[:].bitcast(U32).indirect(idx2[:, cols]))
-            tab_codes.append(picked)
-            return pairs
-
-        def part_half(half, pairs):
-            parted = keep.tile([P, 2, HALF], U16, name=f"tab2_codes{half}", align_bytes=64)
-            nc.vector.tensor_copy(
-                parted[:].rearrange("p d (c i) -> p c d i", i=8),
-                pairs[:].bitcast(U16).rearrange("p (c i d) -> p c d i", d=2, i=8),
-            )
-            tab2_codes.append(parted)
-
-        wb_t = []
-
-        def reorder_wb(g, raw):
-            t = keep.tile([P, 2, PASS], I32, name=f"wb_t{g}", align_bytes=64)
-            nc.vector.tensor_copy(
-                t[:].rearrange("p a (t c i) -> p a c t i", t=4, i=4),
-                raw.rearrange("p a (c i t) -> p a c t i", t=4, i=4),
-            )
-            wb_t.append(t)
-
-        pairs0 = gather_half(0)
+        tab_codes = keep.tile([P, J], U32, name="tab_codes", align_bytes=64)
+        nc.vector.tensor_copy(tab_codes[:], tab_win[:].bitcast(U32).indirect(idx[:]))
         wa_t = keep.tile([P, R], U16, name="wa_t", align_bytes=64)
         nc.vector.tensor_copy(
             wa_t[:].rearrange("p (g t c i) -> p g c t i", g=2, t=4, i=8),
             wa_raw[:].bitcast(U16).rearrange("p (g c i t) -> p g c t i", g=2, t=4, i=8),
         )
-        part_half(0, pairs0)
-        pairs1 = gather_half(1)
-        reorder_wb(0, wb_raw[:, 0])
-        part_half(1, pairs1)
-        reorder_wb(1, wb_raw[:, 1])
+        tab_plane = keep.tile([P, J], U8, name="tab_plane", align_bytes=64)
+        nc.vector.tensor_copy(tab_plane[:], tab_rows[:].bitcast(U8).indirect(idx[:]))
 
-        turned = psum_y.tile([P, 4, CHUNK], F32, name="y")
-        for t in range(4):
-            nc.tensor.transpose(turned[:, t, :], vectors[:, t:PASS:4], ident[:])
-        turned_b = psum_y.tile([P, 4, CHUNK], F32, name="y")
-        nc.tensor.transpose(turned_b[:, 0, :], vectors[:, PASS:], ident[:])
-        sm_wide = keep.tile([P, 2, CHUNK, 4], F32, name="sm_wide")
-        for g in range(2):
-            nc.scalar.copy(sm_wide[:, g], turned[:, :, g].unsqueeze(1).to_broadcast([P, CHUNK, 4]))
-        bias = keep.tile([P, N // P], F32, name="bias")
-        nc.scalar.copy(bias[:], turned_b[:, 0, 0 : N // P])
+        en8_codes = keep.tile([P, N], I32, name="en8_codes", tag="then_en8", align_bytes=64)
+        nc.sync.dma_start(en8_codes[:], en8_words[0].rearrange("p n i -> p (n i)").bitcast(I32))
+        en4_codes = keep.tile([P, N // 2], I32, name="en4_codes", tag="then_en4", align_bytes=64)
+        nc.sync.dma_start(en4_codes[:], en4_words[0].bitcast(I32))
 
-        w_scale = w_planes[:].rearrange("p k n -> p (k n)").bitcast(U8)
-        tab_scale = tab_planes[:].bitcast(U8)
-        en_scale = tab_scale[:, 3 * J :]
-        en8_flat = en_codes[:, :N]
-        en4_flat = en_codes[:, N:].bitcast(U16)
+        bias = after_tab.tile([P, N // P], F32, name="bias", offset=4096, align_bytes=64)
+        with nc.allow_non_contiguous_dma(reason="one bias value for each partition and tile of 128 rows"):
+            nc.sync.dma_start(bias[:], b.rearrange("(s p) -> p s", p=P))
+        pairs = after_tab.tile([P, J], U32, name="tab2_pairs", offset=4160, align_bytes=64)
+
+        tab2_codes = []
+        wb_t = []
+
+        def gather_tab2(half):
+            cols = slice(half * HALF // 16, (half + 1) * HALF // 16)
+            nc.vector.tensor_copy(pairs[:, half * HALF : (half + 1) * HALF], tab2_win[:].bitcast(U32).indirect(idx2[:, cols]))
+
+        def part_tab2(half):
+            parted = keep.tile([P, 2, HALF], U16, name=f"tab2_codes{half}", align_bytes=64)
+            nc.vector.tensor_copy(
+                parted[:].rearrange("p d (c i) -> p c d i", i=8),
+                pairs[:, half * HALF : (half + 1) * HALF].bitcast(U16).rearrange("p (c i d) -> p c d i", d=2, i=8),
+            )
+            tab2_codes.append(parted)
+
+        def reorder_wb(g):
+            if g == 0:
+                t = after_tab.tile([P, 2, PASS], I32, name="wb_t0", offset=0, align_bytes=64)
+            else:
+                t = keep.tile([P, 2, PASS], I32, name="wb_t1", align_bytes=64)
+            nc.vector.tensor_copy(
+                t[:].rearrange("p a (t c i) -> p a c t i", t=4, i=4),
+                wb_raw[g][:].rearrange("p a (c i t) -> p a c t i", t=4, i=4),
+            )
+            wb_t.append(t)
+
+        gather_tab2(0)
+        reorder_wb(0)
+        part_tab2(0)
+        reorder_wb(1)
+        gather_tab2(1)
+
+        scale = planes[:].bitcast(U8)
+        en_scale = en_planes[:].bitcast(U8)
         out_v = out.rearrange("(s p) j -> p s j", p=P)
 
         units = [(c, g) for c in range(CHUNKS) for g in range(2)]
+        ha_of = {}
         state = {}
 
-        def project(u):
+        def project_a(u):
             c, g = units[u]
-            half, j0 = divmod(c * CHUNK, HALF)
             ha = psum.tile([P, PASS], F32, name="ha")
-            hb = psum.tile([P, PASS], F32, name="hb")
             for t in range(4):
                 r0 = g * PASS + t * P
+                s0 = g * SLOT + R + t * P
                 nc.tensor.matmul_mx(
                     out=ha[:, t * P : (t + 1) * P],
                     lhsT=wa_t[:, r0 : r0 + P].bitcast(FP4X4),
-                    lhsT_scale=w_scale[:, r0 : r0 + P],
-                    rhs=tab_codes[half][:, j0 : j0 + CHUNK].bitcast(FP8X4),
-                    rhs_scale=tab_scale[:, J + c * CHUNK : J + (c + 1) * CHUNK],
+                    lhsT_scale=scale[:, s0 : s0 + P],
+                    rhs=tab_codes[:, c * CHUNK : (c + 1) * CHUNK].bitcast(FP8X4),
+                    rhs_scale=tab_plane[:, c * CHUNK : (c + 1) * CHUNK],
                     start=True,
                     stop=True,
                 )
+            ha_sb = work.tile([P, CHUNK, 4], F32, name="ha_sb", bufs=8)
+            nc.scalar.copy(ha_sb[:], ha[:].rearrange("p (t j) -> p j t", t=4))
+            ha_of[u] = ha_sb
+
+        def project_b(u):
+            c, g = units[u]
+            half, j0 = divmod(c * CHUNK, HALF)
+            hb = psum.tile([P, PASS], F32, name="hb")
             for t in range(4):
-                r0 = g * PASS + t * P
                 for a in range(2):
-                    s0 = 2 * a * J + c * CHUNK
+                    w0 = a * SLOT + g * PASS + t * P
+                    s0 = a * SLOT + R + PASS + c * CHUNK
                     nc.tensor.matmul_mx(
                         out=hb[:, t * P : (t + 1) * P],
                         lhsT=wb_t[g][:, a, t * P : (t + 1) * P].bitcast(FP8X4),
-                        lhsT_scale=w_scale[:, (1 + a) * R + r0 : (1 + a) * R + r0 + P],
+                        lhsT_scale=scale[:, w0 : w0 + P],
                         rhs=tab2_codes[half][:, a, j0 : j0 + CHUNK].bitcast(FP4X4),
-                        rhs_scale=tab_scale[:, s0 : s0 + CHUNK],
+                        rhs_scale=scale[:, s0 : s0 + CHUNK],
                         start=(a == 0),
                         stop=(a == 1),
                     )
-            ha_sb = work.tile([P, CHUNK, 4], F32, name="ha_sb", bufs=8)
-            nc.scalar.copy(ha_sb[:], ha[:].rearrange("p (t j) -> p j t", t=4))
-            state[u] = (ha_sb, hb)
+            state[u] = hb
 
         def difference(u):
-            ha_sb, hb = state[u]
             diff = work.tile([P, CHUNK, 4], F32, name="diff")
-            nc.vector.tensor_tensor(diff[:], hb[:].rearrange("p (t j) -> p j t", t=4), ha_sb[:], ALU.subtract)
+            nc.vector.tensor_tensor(diff[:], state[u][:].rearrange("p (t j) -> p j t", t=4), ha_of[u][:], ALU.subtract)
             square = work.tile([P, CHUNK, 4], F32, name="square")
             nc.scalar.activation(square[:], diff[:], ACT.Square)
             state[u] = square
@@ -215,7 +207,7 @@ def tile_list_kg_sqd_mix_gelu_kernel(
         def smooth(u):
             g = units[u][1]
             h = work.tile([P, CHUNK, 4], BF16, name="h", align_bytes=64)
-            nc.vector.tensor_tensor(h[:], state[u][:], sm_wide[:, g], ALU.mult)
+            nc.vector.tensor_tensor(h[:], state[u][:], sm_sb[:, g].unsqueeze(1).to_broadcast([P, CHUNK, 4]), ALU.mult)
             state[u] = h
 
         def quantise(u):
@@ -235,9 +227,9 @@ def tile_list_kg_sqd_mix_gelu_kernel(
                 for s in range(4):
                     n0 = (4 * half + s) * P
                     if g == 0:
-                        lhs = en8_flat[:, n0 : n0 + P].bitcast(FP8X4)
+                        lhs = en8_codes[:, n0 : n0 + P].bitcast(FP8X4)
                     else:
-                        lhs = en4_flat[:, n0 : n0 + P].bitcast(FP4X4)
+                        lhs = en4_codes[:].bitcast(U16)[:, n0 : n0 + P].bitcast(FP4X4)
                     nc.tensor.matmul_mx(
                         out=banks[half][:, s, :],
                         lhsT=lhs,
@@ -257,12 +249,18 @@ def tile_list_kg_sqd_mix_gelu_kernel(
                     nc.sync.dma_start(out_v[:, 4 * half : 4 * half + 4, c * CHUNK : (c + 1) * CHUNK], res[:])
 
         last = len(units)
-        project(0)
+        for u in range(HA_AHEAD):
+            project_a(u)
+        project_b(0)
         for step in range(last + 2):
             if step + 1 < last:
-                project(step + 1)
+                project_b(step + 1)
+            if step + HA_AHEAD < last:
+                project_a(step + HA_AHEAD)
             if step < last:
                 difference(step)
+            if step == 0:
+                part_tab2(1)
             if 0 <= step - 2:
                 quantise(step - 2)
                 score(step - 2)

@@ -217,36 +217,43 @@ def tile_list_kg_sqd_mix_gelu_kernel(
             state[u] = (codes, scales)
 
         banks = {}
+        closed = []
 
         def score(u):
             c, g = units[u]
             codes, scales = state[u]
-            for half in range(2):
+            width = 2 if c == CHUNKS - 1 else 4
+            for part in range(8 // width):
                 if g == 0:
-                    banks[half] = psum_y.tile([P, 4, CHUNK], F32, name="y")
-                for s in range(4):
-                    n0 = (4 * half + s) * P
+                    if part < 2:
+                        banks[part] = psum_y.tile([P, width, CHUNK], F32, name="y")
+                    else:
+                        banks[part] = psum.tile([P, width, CHUNK], F32, name="ha")
+                for s in range(width):
+                    n0 = (width * part + s) * P
                     if g == 0:
                         lhs = en8_codes[:, n0 : n0 + P].bitcast(FP8X4)
                     else:
                         lhs = en4_codes[:].bitcast(U16)[:, n0 : n0 + P].bitcast(FP4X4)
                     nc.tensor.matmul_mx(
-                        out=banks[half][:, s, :],
+                        out=banks[part][:, s, :],
                         lhsT=lhs,
                         lhsT_scale=en_scale[:, g * N + n0 : g * N + n0 + P],
                         rhs=codes[:].bitcast(FP8X4),
                         rhs_scale=scales[:],
                         start=(g == 0 and s == 0),
-                        stop=(g == 1 and s == 3),
+                        stop=(g == 1 and s == width - 1),
                     )
                 if g == 1:
-                    res = work.tile([P, 4, CHUNK], F32, name="res")
-                    for s in range(4):
-                        nc.scalar.activation(
-                            res[:, s, :], banks[half][:, s, :], ACT.Gelu_apprx_tanh,
-                            bias=bias[:, 4 * half + s : 4 * half + s + 1],
-                        )
-                    nc.sync.dma_start(out_v[:, 4 * half : 4 * half + 4, c * CHUNK : (c + 1) * CHUNK], res[:])
+                    closed.append((c, part, width, banks[part]))
+
+        def finish():
+            c, part, width, bank = closed.pop(0)
+            res = work.tile([P, width, CHUNK], F32, name="res", bufs=6)
+            for s in range(width):
+                row = width * part + s
+                nc.scalar.activation(res[:, s, :], bank[:, s, :], ACT.Gelu_apprx_tanh, bias=bias[:, row : row + 1])
+            nc.sync.dma_start(out_v[:, width * part : width * (part + 1), c * CHUNK : (c + 1) * CHUNK], res[:])
 
         last = len(units)
         for u in range(HA_AHEAD):
@@ -266,3 +273,7 @@ def tile_list_kg_sqd_mix_gelu_kernel(
                 score(step - 2)
             if 0 <= step - 1 < last:
                 smooth(step - 1)
+            if closed:
+                finish()
+        for left in range(len(closed)):
+            finish()

@@ -23,7 +23,7 @@ CHUNKS = J // CHUNK
 HALF = J // 2
 STAGE = 96
 SLOT = 2048
-HA_AHEAD = 3
+HA_AHEAD = 5
 
 
 def tile_list_kg_sqd_mix_gelu_kernel(
@@ -34,25 +34,25 @@ def tile_list_kg_sqd_mix_gelu_kernel(
     with ExitStack() as ctx:
         keep = ctx.enter_context(tc.tile_pool(name="keep", bufs=1))
         after_tab = ctx.enter_context(tc.tile_pool(name="after_tab", bufs=1))
+        after_rows = ctx.enter_context(tc.tile_pool(name="after_rows", bufs=1))
+        after_wa = ctx.enter_context(tc.tile_pool(name="after_wa", bufs=1))
         work = ctx.enter_context(tc.tile_pool(name="work", bufs=3))
-        psum = ctx.enter_context(tc.psum_pool(name="psum", bufs=2))
+        psum = ctx.enter_context(tc.psum_pool(name="psum", bufs=4))
         psum_y = ctx.enter_context(tc.psum_pool(name="psum_y", bufs=4))
 
         idx = keep.tile([P, J // 16], U16, name="idx")
         idx2 = keep.tile([P, J // 16], U16, name="idx2")
         tab_rows = after_tab.tile([P, T // 4], I32, name="tab_rows", offset=3584, align_bytes=64)
-        tab2_rows = keep.tile([P, T // 4], I32, name="tab2_rows", tag="then_en_rows", align_bytes=64)
+        tab2_rows = after_rows.tile([P, T // 4], I32, name="tab2_rows", offset=3584, align_bytes=64)
         w_rows = keep.tile([P, 3 * PASS // 4], I32, name="w_rows", align_bytes=64)
         staged = keep.tile([P, SLOT // 4], I32, name="staged", align_bytes=64)
         planes = keep.tile([P, 2 * SLOT // 4], I32, name="planes", align_bytes=64)
         en_planes = keep.tile([P, 2 * N // 4], I32, name="en_planes", align_bytes=64)
         warm = keep.tile([P, 2], F32, name="warm")
-        tab_win = keep.tile([P, T], I32, name="tab_win", tag="then_en8", align_bytes=64)
+        tab_win = keep.tile([P, T], I32, name="tab_win", align_bytes=64)
         tab2_win = keep.tile([P, T], I32, name="tab2_win", align_bytes=64)
-        wa_raw = keep.tile([P, R // 2], I32, name="wa_raw", tag="then_en4", align_bytes=64)
-        wb_raw0 = keep.tile([P, 2, PASS], I32, name="wb_raw0", align_bytes=64)
+        wa_raw = after_wa.tile([P, R // 2], I32, name="wa_raw", offset=3072, align_bytes=64)
         wb_hbm = wb_words.rearrange("a p n i -> p a (n i)")
-        sm_sb = keep.tile([P, 2, 4], F32, name="sm_sb")
 
         nc.vector.memset(tab_rows[:], 0)
         nc.vector.memset(tab2_rows[0:STAGE, :], 0)
@@ -72,16 +72,18 @@ def tile_list_kg_sqd_mix_gelu_kernel(
         nc.sync.dma_start(tab2_win[:], tab2_words[0].rearrange("p t i -> p (t i)").bitcast(I32))
         for q in range(4):
             nc.sync.dma_start(tab_rows[32 * q : 32 * q + 4, :], tab_scales[0, 4 * q : 4 * q + 4, :].bitcast(I32))
-        nc.sync.dma_start(wb_raw0[:], wb_hbm[:, :, : 4 * PASS].bitcast(I32))
-        nc.sync.dma_start(sm_sb[:], sm.rearrange("(g p t) -> p g t", g=2, t=4))
 
         picked2 = keep.tile([P, J // 4], I32, name="picked2", tag="then_wb1", align_bytes=64)
         nc.vector.tensor_copy(picked2[:].bitcast(U8), tab2_rows[:].bitcast(U8).indirect(idx2[:]))
+        wb_raw0 = after_rows.tile([P, 2, PASS], I32, name="wb_raw0", offset=0, align_bytes=64)
+        sm_sb = after_rows.tile([P, 2, 4], F32, name="sm_sb", offset=4096, align_bytes=64)
+        nc.sync.dma_start(wb_raw0[:], wb_hbm[:, :, : 4 * PASS].bitcast(I32))
+        nc.sync.dma_start(sm_sb[:], sm.rearrange("(g p t) -> p g t", g=2, t=4))
         nc.vector.tensor_copy(
             staged[:, : 3 * PASS // 4].bitcast(U8).rearrange("p (g t c i) -> p c g t i", g=3, t=4, i=16),
             w_rows[:].bitcast(U8).rearrange("p (g c i t) -> p c g t i", g=3, t=4, i=16),
         )
-        nc.vector.tensor_copy(staged[STAGE:, 3 * PASS // 4 :], picked2[STAGE:, :])
+        nc.vector.tensor_copy(staged[:, 3 * PASS // 4 :], picked2[:])
         for q in (0, 2, 1, 3):
             nc.sync.dma_start(
                 planes[32 * q : 32 * q + 4, :].rearrange("p (k n) -> p k n", k=2),
@@ -91,7 +93,7 @@ def tile_list_kg_sqd_mix_gelu_kernel(
         nc.sync.dma_start(wb_raw1[:], wb_hbm[:, :, 4 * PASS :].bitcast(I32))
         wb_raw = [wb_raw0, wb_raw1]
 
-        en_rows = keep.tile([32, N // 4], I32, name="en_rows", tag="then_en_rows", align_bytes=64)
+        en_rows = after_rows.tile([32, N // 4], I32, name="en_rows", offset=4160, align_bytes=64)
         nc.sync.dma_start(en_rows[0:32:2, :], en8_scales[0].bitcast(I32))
         nc.sync.dma_start(en_rows[1:32:2, :], en4_scales[0].bitcast(I32))
         for q in (0, 2, 1, 3):
@@ -99,8 +101,16 @@ def tile_list_kg_sqd_mix_gelu_kernel(
                 en_planes[32 * q : 32 * q + 4, :].rearrange("p (k n) -> p k n", k=2), en_rows[8 * q : 8 * q + 8, :]
             )
 
-        tab_codes = keep.tile([P, J], U32, name="tab_codes", align_bytes=64)
-        nc.vector.tensor_copy(tab_codes[:], tab_win[:].bitcast(U32).indirect(idx[:]))
+        tab_codes = [
+            keep.tile([P, HALF], U32, name="tab_codes0", align_bytes=64),
+            after_tab.tile([P, HALF], U32, name="tab_codes1", offset=4160, align_bytes=64),
+        ]
+
+        def gather_tab(half):
+            cols = slice(half * HALF // 16, (half + 1) * HALF // 16)
+            nc.vector.tensor_copy(tab_codes[half][:], tab_win[:].bitcast(U32).indirect(idx[:, cols]))
+
+        gather_tab(0)
         wa_t = keep.tile([P, R], U16, name="wa_t", align_bytes=64)
         nc.vector.tensor_copy(
             wa_t[:].rearrange("p (g t c i) -> p g c t i", g=2, t=4, i=8),
@@ -109,28 +119,31 @@ def tile_list_kg_sqd_mix_gelu_kernel(
         tab_plane = keep.tile([P, J], U8, name="tab_plane", align_bytes=64)
         nc.vector.tensor_copy(tab_plane[:], tab_rows[:].bitcast(U8).indirect(idx[:]))
 
-        en8_codes = keep.tile([P, N], I32, name="en8_codes", tag="then_en8", align_bytes=64)
+        en8_codes = after_wa.tile([P, N], I32, name="en8_codes", offset=0, align_bytes=64)
         nc.sync.dma_start(en8_codes[:], en8_words[0].rearrange("p n i -> p (n i)").bitcast(I32))
-        en4_codes = keep.tile([P, N // 2], I32, name="en4_codes", tag="then_en4", align_bytes=64)
+        en4_codes = after_wa.tile([P, N // 2], I32, name="en4_codes", offset=4096, align_bytes=64)
         nc.sync.dma_start(en4_codes[:], en4_words[0].bitcast(I32))
 
         bias = after_tab.tile([P, N // P], F32, name="bias", offset=4096, align_bytes=64)
         with nc.allow_non_contiguous_dma(reason="one bias value for each partition and tile of 128 rows"):
             nc.sync.dma_start(bias[:], b.rearrange("(s p) -> p s", p=P))
-        pairs = after_tab.tile([P, J], U32, name="tab2_pairs", offset=4160, align_bytes=64)
+        pairs = [
+            after_tab.tile([P, HALF], U32, name="tab2_pairs0", offset=4160, align_bytes=64),
+            after_rows.tile([P, HALF], U32, name="tab2_pairs1", offset=0, align_bytes=64),
+        ]
 
         tab2_codes = []
         wb_t = []
 
         def gather_tab2(half):
             cols = slice(half * HALF // 16, (half + 1) * HALF // 16)
-            nc.vector.tensor_copy(pairs[:, half * HALF : (half + 1) * HALF], tab2_win[:].bitcast(U32).indirect(idx2[:, cols]))
+            nc.vector.tensor_copy(pairs[half][:], tab2_win[:].bitcast(U32).indirect(idx2[:, cols]))
 
         def part_tab2(half):
             parted = keep.tile([P, 2, HALF], U16, name=f"tab2_codes{half}", align_bytes=64)
             nc.vector.tensor_copy(
                 parted[:].rearrange("p d (c i) -> p c d i", i=8),
-                pairs[:, half * HALF : (half + 1) * HALF].bitcast(U16).rearrange("p (c i d) -> p c d i", d=2, i=8),
+                pairs[half][:].bitcast(U16).rearrange("p (c i d) -> p c d i", d=2, i=8),
             )
             tab2_codes.append(parted)
 
@@ -148,6 +161,7 @@ def tile_list_kg_sqd_mix_gelu_kernel(
         gather_tab2(0)
         reorder_wb(0)
         part_tab2(0)
+        gather_tab(1)
         reorder_wb(1)
         gather_tab2(1)
 
@@ -161,7 +175,8 @@ def tile_list_kg_sqd_mix_gelu_kernel(
 
         def project_a(u):
             c, g = units[u]
-            ha = psum.tile([P, PASS], F32, name="ha")
+            half, j0 = divmod(c * CHUNK, HALF)
+            ha = psum.tile([P, PASS], F32, name="ha", tag="first")
             for t in range(4):
                 r0 = g * PASS + t * P
                 s0 = g * SLOT + R + t * P
@@ -169,7 +184,7 @@ def tile_list_kg_sqd_mix_gelu_kernel(
                     out=ha[:, t * P : (t + 1) * P],
                     lhsT=wa_t[:, r0 : r0 + P].bitcast(FP4X4),
                     lhsT_scale=scale[:, s0 : s0 + P],
-                    rhs=tab_codes[:, c * CHUNK : (c + 1) * CHUNK].bitcast(FP8X4),
+                    rhs=tab_codes[half][:, j0 : j0 + CHUNK].bitcast(FP8X4),
                     rhs_scale=tab_plane[:, c * CHUNK : (c + 1) * CHUNK],
                     start=True,
                     stop=True,
@@ -181,7 +196,7 @@ def tile_list_kg_sqd_mix_gelu_kernel(
         def project_b(u):
             c, g = units[u]
             half, j0 = divmod(c * CHUNK, HALF)
-            hb = psum.tile([P, PASS], F32, name="hb")
+            hb = psum.tile([P, PASS], F32, name="hb", tag="first")
             for t in range(4):
                 for a in range(2):
                     w0 = a * SLOT + g * PASS + t * P
@@ -200,7 +215,7 @@ def tile_list_kg_sqd_mix_gelu_kernel(
         def difference(u):
             diff = work.tile([P, CHUNK, 4], F32, name="diff")
             nc.vector.tensor_tensor(diff[:], state[u][:].rearrange("p (t j) -> p j t", t=4), ha_of[u][:], ALU.subtract)
-            square = work.tile([P, CHUNK, 4], F32, name="square")
+            square = work.tile([P, CHUNK, 4], F32, name="square", bufs=4)
             nc.scalar.activation(square[:], diff[:], ACT.Square)
             state[u] = square
 
@@ -228,7 +243,7 @@ def tile_list_kg_sqd_mix_gelu_kernel(
                     if part < 2:
                         banks[part] = psum_y.tile([P, width, CHUNK], F32, name="y")
                     else:
-                        banks[part] = psum.tile([P, width, CHUNK], F32, name="ha")
+                        banks[part] = psum.tile([P, width, CHUNK], F32, name="y_last", tag="first")
                 for s in range(width):
                     n0 = (width * part + s) * P
                     if g == 0:
@@ -256,23 +271,27 @@ def tile_list_kg_sqd_mix_gelu_kernel(
             nc.sync.dma_start(out_v[:, width * part : width * (part + 1), c * CHUNK : (c + 1) * CHUNK], res[:])
 
         last = len(units)
-        for u in range(HA_AHEAD):
-            project_a(u)
+        project_a(0)
+        project_a(1)
         project_b(0)
-        for step in range(last + 2):
-            if step + 1 < last:
-                project_b(step + 1)
-            if step + HA_AHEAD < last:
-                project_a(step + HA_AHEAD)
+        project_a(2)
+        project_b(1)
+        project_a(3)
+        project_a(4)
+        for step in range(last + 3):
             if step < last:
                 difference(step)
+            if step + 2 < last:
+                project_b(step + 2)
+            if step + HA_AHEAD < last:
+                project_a(step + HA_AHEAD)
             if step == 0:
                 part_tab2(1)
-            if 0 <= step - 2:
-                quantise(step - 2)
-                score(step - 2)
-            if 0 <= step - 1 < last:
-                smooth(step - 1)
+            if 0 <= step - 3:
+                quantise(step - 3)
+                score(step - 3)
+            if 0 <= step - 2 < last:
+                smooth(step - 2)
             if closed:
                 finish()
         for left in range(len(closed)):

@@ -18,12 +18,15 @@ ALU = mybir.AluOpType
 
 P = 128
 PASS = 512
-CHUNK = 128
-CHUNKS = J // CHUNK
+BANK = 512
 HALF = J // 2
 STAGE = 96
-SLOT = 2048
-HA_AHEAD = 5
+SLOT_A = 1024
+SLOT_B = 1536
+AHEAD = 2
+CHUNKS = [(0, 256), (256, 128), (384, 128)]
+SUM_BANKS = [(0, 1, 2, 3), (4, 5), (6, 7)]
+SQUARE_ON_VECTOR = ()
 
 
 def tile_list_kg_sqd_mix_gelu_kernel(
@@ -33,266 +36,264 @@ def tile_list_kg_sqd_mix_gelu_kernel(
     nc = tc.nc
     with ExitStack() as ctx:
         keep = ctx.enter_context(tc.tile_pool(name="keep", bufs=1))
-        after_tab = ctx.enter_context(tc.tile_pool(name="after_tab", bufs=1))
-        after_rows = ctx.enter_context(tc.tile_pool(name="after_rows", bufs=1))
+        after_a = ctx.enter_context(tc.tile_pool(name="after_a", bufs=1))
+        after_b = ctx.enter_context(tc.tile_pool(name="after_b", bufs=1))
+        after_wb_rows = ctx.enter_context(tc.tile_pool(name="after_wb_rows", bufs=1))
         after_wa = ctx.enter_context(tc.tile_pool(name="after_wa", bufs=1))
-        work = ctx.enter_context(tc.tile_pool(name="work", bufs=3))
-        psum = ctx.enter_context(tc.psum_pool(name="psum", bufs=4))
-        psum_y = ctx.enter_context(tc.psum_pool(name="psum_y", bufs=4))
+        work = ctx.enter_context(tc.tile_pool(name="work", bufs=4))
+        psum = ctx.enter_context(tc.psum_pool(name="psum", bufs=1))
 
         idx = keep.tile([P, J // 16], U16, name="idx")
         idx2 = keep.tile([P, J // 16], U16, name="idx2")
-        tab_rows = after_tab.tile([P, T // 4], I32, name="tab_rows", offset=3584, align_bytes=64)
-        tab2_rows = after_rows.tile([P, T // 4], I32, name="tab2_rows", offset=3584, align_bytes=64)
-        w_rows = keep.tile([P, 3 * PASS // 4], I32, name="w_rows", align_bytes=64)
-        staged = keep.tile([P, SLOT // 4], I32, name="staged", align_bytes=64)
-        planes = keep.tile([P, 2 * SLOT // 4], I32, name="planes", align_bytes=64)
+        tab_rows = keep.tile([P, T // 4], I32, name="tab_rows", align_bytes=64)
+        wa_rows = keep.tile([P, PASS // 4], I32, name="wa_rows", align_bytes=64)
+        tab2_rows = keep.tile([P, T // 4], I32, name="tab2_rows", align_bytes=64)
+        wb_rows = after_wb_rows.tile([P, R // 4], I32, name="wb_rows", offset=0, align_bytes=64)
+        staged_a = keep.tile([P, SLOT_A // 4], I32, name="staged_a", align_bytes=64)
+        planes_a = keep.tile([P, 2 * SLOT_A // 4], I32, name="planes_a", align_bytes=64)
+        planes_b = keep.tile([P, 2 * SLOT_B // 4], I32, name="planes_b", align_bytes=64)
         en_planes = keep.tile([P, 2 * N // 4], I32, name="en_planes", align_bytes=64)
         warm = keep.tile([P, 2], F32, name="warm")
         tab_win = keep.tile([P, T], I32, name="tab_win", align_bytes=64)
         tab2_win = keep.tile([P, T], I32, name="tab2_win", align_bytes=64)
-        wa_raw = after_wa.tile([P, R // 2], I32, name="wa_raw", offset=3072, align_bytes=64)
+        wa_raw = after_wa.tile([P, R // 2], I32, name="wa_raw", offset=0, align_bytes=64)
+        sm_sb = keep.tile([P, 8], F32, name="sm_sb")
         wb_hbm = wb_words.rearrange("a p n i -> p a (n i)")
 
-        nc.vector.memset(tab_rows[:], 0)
-        nc.vector.memset(tab2_rows[0:STAGE, :], 0)
-        nc.vector.memset(w_rows[0:STAGE, :], 0)
-        nc.gpsimd.memset(warm[:], 0.0)
-        nc.gpsimd.memset(planes[:], 0)
-        nc.gpsimd.memset(en_planes[:], 0)
-        nc.scalar.activation(warm[:, 1:2], warm[:, 0:1], ACT.Gelu_apprx_tanh)
+        nc.vector.memset(warm[:], 0.0)
+        for rows in (tab_rows, wa_rows, tab2_rows, wb_rows):
+            nc.vector.memset(rows[0:STAGE, :], 0)
+        nc.vector.memset(en_planes[:], 0)
+        nc.gpsimd.memset(planes_a[:], 0)
+        nc.gpsimd.memset(planes_b[:], 0)
+        nc.scalar.activation(warm[:, 1:2], warm[:, 0:1], ACT.Sqrt)
 
-        nc.sync.dma_start(idx2[:], offs2)
-        nc.sync.dma_start(tab2_rows[STAGE:, :], tab2_scales.rearrange("a q t -> q a t").bitcast(I32))
-        nc.sync.dma_start(w_rows[STAGE:, : R // 4], wb_scales.rearrange("a q n -> q a n").bitcast(I32))
-        nc.sync.dma_start(w_rows[STAGE:, R // 4 :], wa_scales[0].rearrange("q (g n) -> (q g) n", g=2).bitcast(I32))
         nc.sync.dma_start(idx[:], offs)
+        nc.sync.dma_start(tab_rows[STAGE:, :], tab_scales[0].bitcast(I32).unsqueeze(1).to_broadcast([16, 2, T // 4]))
+        nc.sync.dma_start(wa_rows[STAGE:, :], wa_scales[0].rearrange("q (g n) -> (q g) n", g=2).bitcast(I32))
+        nc.sync.dma_start(sm_sb[:].rearrange("p (g t) -> p g t", g=2), sm.rearrange("(g p t) -> p g t", g=2, t=4))
         nc.sync.dma_start(tab_win[:], tab_words[0].rearrange("p t i -> p (t i)").bitcast(I32))
         nc.sync.dma_start(wa_raw[:], wa_words[0].bitcast(I32))
+        nc.sync.dma_start(idx2[:], offs2)
+        nc.sync.dma_start(tab2_rows[STAGE:, :], tab2_scales.rearrange("a q t -> q a t").bitcast(I32))
+        nc.sync.dma_start(wb_rows[STAGE:, :], wb_scales.rearrange("a q n -> q a n").bitcast(I32))
         nc.sync.dma_start(tab2_win[:], tab2_words[0].rearrange("p t i -> p (t i)").bitcast(I32))
-        for q in range(4):
-            nc.sync.dma_start(tab_rows[32 * q : 32 * q + 4, :], tab_scales[0, 4 * q : 4 * q + 4, :].bitcast(I32))
 
-        picked2 = keep.tile([P, J // 4], I32, name="picked2", tag="then_wb1", align_bytes=64)
+        sign = keep.tile([P, 8], BF16, name="sign")
+        size = keep.tile([P, 8], F32, name="size")
+        root = keep.tile([P, 8], F32, name="root")
+        nc.scalar.activation(sign[:], sm_sb[:], ACT.Sign)
+        nc.scalar.activation(size[:], sm_sb[:], ACT.Abs)
+        nc.scalar.activation(root[:], size[:], ACT.Sqrt)
+        nc.scalar.activation(warm[:, 0:1], root[:, 0:1], ACT.Gelu_apprx_tanh)
+
+        def place(planes, staged):
+            for q in (0, 2, 1, 3):
+                nc.sync.dma_start(
+                    planes[32 * q : 32 * q + 4, :].rearrange("p (k n) -> p k n", k=2), staged[8 * q : 8 * q + 8, :]
+                )
+
+        def deal_scales(dst, src, groups):
+            nc.vector.tensor_copy(
+                dst.bitcast(U8).rearrange("p (g t c i) -> p c g t i", g=groups, t=4, i=16),
+                src.bitcast(U8).rearrange("p (g c i t) -> p c g t i", g=groups, t=4, i=16),
+            )
+
+        picked = after_a.tile([P, J // 4], I32, name="picked", offset=4096 - 256, align_bytes=64)
+        nc.vector.tensor_copy(picked[:].bitcast(U8), tab_rows[:].bitcast(U8).indirect(idx[:]))
+        deal_scales(staged_a[:, : PASS // 4], wa_rows[:], 1)
+        nc.vector.tensor_copy(staged_a[:, PASS // 4 :], picked[:])
+        place(planes_a, staged_a[STAGE:, :])
+        wb_raw = []
+        for g in range(2):
+            raw = after_a.tile([P, 2, PASS], I32, name=f"wb_raw{g}", offset=4096 * g, align_bytes=64)
+            nc.sync.dma_start(raw[:], wb_hbm[:, :, 4 * PASS * g : 4 * PASS * (g + 1)].bitcast(I32))
+            wb_raw.append(raw)
+
+        picked2 = after_b.tile([P, J // 4], I32, name="picked2", offset=4096 - 64, align_bytes=64)
         nc.vector.tensor_copy(picked2[:].bitcast(U8), tab2_rows[:].bitcast(U8).indirect(idx2[:]))
-        wb_raw0 = after_rows.tile([P, 2, PASS], I32, name="wb_raw0", offset=0, align_bytes=64)
-        sm_sb = after_rows.tile([P, 2, 4], F32, name="sm_sb", offset=4096, align_bytes=64)
-        nc.sync.dma_start(wb_raw0[:], wb_hbm[:, :, : 4 * PASS].bitcast(I32))
-        nc.sync.dma_start(sm_sb[:], sm.rearrange("(g p t) -> p g t", g=2, t=4))
-        nc.vector.tensor_copy(
-            staged[:, : 3 * PASS // 4].bitcast(U8).rearrange("p (g t c i) -> p c g t i", g=3, t=4, i=16),
-            w_rows[:].bitcast(U8).rearrange("p (g c i t) -> p c g t i", g=3, t=4, i=16),
-        )
-        nc.vector.tensor_copy(staged[:, 3 * PASS // 4 :], picked2[:])
-        for q in (0, 2, 1, 3):
-            nc.sync.dma_start(
-                planes[32 * q : 32 * q + 4, :].rearrange("p (k n) -> p k n", k=2),
-                staged[STAGE + 8 * q : STAGE + 8 * q + 8, :],
-            )
-        wb_raw1 = keep.tile([P, 2, PASS], I32, name="wb_raw1", tag="then_wb1", align_bytes=64)
-        nc.sync.dma_start(wb_raw1[:], wb_hbm[:, :, 4 * PASS :].bitcast(I32))
-        wb_raw = [wb_raw0, wb_raw1]
-
-        en_rows = after_rows.tile([32, N // 4], I32, name="en_rows", offset=4160, align_bytes=64)
-        nc.sync.dma_start(en_rows[0:32:2, :], en8_scales[0].bitcast(I32))
-        nc.sync.dma_start(en_rows[1:32:2, :], en4_scales[0].bitcast(I32))
-        for q in (0, 2, 1, 3):
-            nc.sync.dma_start(
-                en_planes[32 * q : 32 * q + 4, :].rearrange("p (k n) -> p k n", k=2), en_rows[8 * q : 8 * q + 8, :]
-            )
-
-        tab_codes = [
-            keep.tile([P, HALF], U32, name="tab_codes0", align_bytes=64),
-            after_tab.tile([P, HALF], U32, name="tab_codes1", offset=4160, align_bytes=64),
-        ]
-
-        def gather_tab(half):
-            cols = slice(half * HALF // 16, (half + 1) * HALF // 16)
-            nc.vector.tensor_copy(tab_codes[half][:], tab_win[:].bitcast(U32).indirect(idx[:, cols]))
-
-        gather_tab(0)
+        tab_codes = keep.tile([P, J], U32, name="tab_codes", align_bytes=64)
+        nc.vector.tensor_copy(tab_codes[:], tab_win[:].bitcast(U32).indirect(idx[:]))
         wa_t = keep.tile([P, R], U16, name="wa_t", align_bytes=64)
         nc.vector.tensor_copy(
             wa_t[:].rearrange("p (g t c i) -> p g c t i", g=2, t=4, i=8),
             wa_raw[:].bitcast(U16).rearrange("p (g c i t) -> p g c t i", g=2, t=4, i=8),
         )
-        tab_plane = keep.tile([P, J], U8, name="tab_plane", align_bytes=64)
-        nc.vector.tensor_copy(tab_plane[:], tab_rows[:].bitcast(U8).indirect(idx[:]))
 
-        en8_codes = after_wa.tile([P, N], I32, name="en8_codes", offset=0, align_bytes=64)
+        staged_b = after_wa.tile([P, SLOT_B // 4], I32, name="staged_b", offset=0, align_bytes=64)
+        deal_scales(staged_b[:, : R // 4], wb_rows[:], 2)
+        nc.vector.tensor_copy(staged_b[:, R // 4 :], picked2[:])
+        place(planes_b, staged_b[STAGE:, :])
+
+        en_rows = after_wb_rows.tile([32, N // 4], I32, name="en_rows", offset=0, align_bytes=64)
+        nc.sync.dma_start(en_rows[0:32:2, :], en8_scales[0].bitcast(I32))
+        nc.sync.dma_start(en_rows[1:32:2, :], en4_scales[0].bitcast(I32))
+        en8_codes = after_b.tile([P, N], I32, name="en8_codes", offset=0, align_bytes=64)
         nc.sync.dma_start(en8_codes[:], en8_words[0].rearrange("p n i -> p (n i)").bitcast(I32))
-        en4_codes = after_wa.tile([P, N // 2], I32, name="en4_codes", offset=4096, align_bytes=64)
+        en4_codes = after_b.tile([P, N // 2], I32, name="en4_codes", offset=4096 + 128, align_bytes=64)
         nc.sync.dma_start(en4_codes[:], en4_words[0].bitcast(I32))
-
-        bias = after_tab.tile([P, N // P], F32, name="bias", offset=4096, align_bytes=64)
+        bias = after_b.tile([P, N // P], F32, name="bias", offset=4096, align_bytes=64)
         with nc.allow_non_contiguous_dma(reason="one bias value for each partition and tile of 128 rows"):
             nc.sync.dma_start(bias[:], b.rearrange("(s p) -> p s", p=P))
-        pairs = [
-            after_tab.tile([P, HALF], U32, name="tab2_pairs0", offset=4160, align_bytes=64),
-            after_rows.tile([P, HALF], U32, name="tab2_pairs1", offset=0, align_bytes=64),
-        ]
+        place(en_planes, en_rows)
+
+        scale_a = planes_a[:].bitcast(U8)
+        scale_b = planes_b[:].bitcast(U8)
+        en_scale = en_planes[:].bitcast(U8)
+        out_v = out.rearrange("(s p) j -> p s j", p=P)
+
+        head = []
+        for g in range(2):
+            rows = keep.tile([P, 4, J], F32, name=f"head{g}")
+            for t in range(4):
+                ha = psum.tile([P, BANK], F32, name="ha", tag=f"bank{t}")
+                s0 = g * SLOT_A + t * P
+                nc.tensor.matmul_mx(
+                    out=ha[:],
+                    lhsT=wa_t[:, g * PASS + t * P : g * PASS + (t + 1) * P].bitcast(FP4X4),
+                    lhsT_scale=scale_a[:, s0 : s0 + P],
+                    rhs=tab_codes[:].bitcast(FP8X4),
+                    rhs_scale=scale_a[:, g * SLOT_A + PASS : (g + 1) * SLOT_A],
+                    start=True,
+                    stop=True,
+                )
+                nc.scalar.activation(rows[:, t, :], ha[:], ACT.Copy, scale=root[:, 4 * g + t : 4 * g + t + 1])
+            head.append(rows)
 
         tab2_codes = []
         wb_t = []
 
-        def gather_tab2(half):
-            cols = slice(half * HALF // 16, (half + 1) * HALF // 16)
-            nc.vector.tensor_copy(pairs[half][:], tab2_win[:].bitcast(U32).indirect(idx2[:, cols]))
-
-        def part_tab2(half):
-            parted = keep.tile([P, 2, HALF], U16, name=f"tab2_codes{half}", align_bytes=64)
+        def gather_tab2(part):
+            cols = slice(part * HALF // 16, (part + 1) * HALF // 16)
+            pairs = keep.tile([P, HALF], U32, name=f"tab2_pairs{part}", align_bytes=64)
+            nc.vector.tensor_copy(pairs[:], tab2_win[:].bitcast(U32).indirect(idx2[:, cols]))
+            parted = keep.tile([P, 2, HALF], U16, name=f"tab2_codes{part}", align_bytes=64)
             nc.vector.tensor_copy(
                 parted[:].rearrange("p d (c i) -> p c d i", i=8),
-                pairs[half][:].bitcast(U16).rearrange("p (c i d) -> p c d i", d=2, i=8),
+                pairs[:].bitcast(U16).rearrange("p (c i d) -> p c d i", d=2, i=8),
             )
             tab2_codes.append(parted)
 
         def reorder_wb(g):
-            if g == 0:
-                t = after_tab.tile([P, 2, PASS], I32, name="wb_t0", offset=0, align_bytes=64)
-            else:
-                t = keep.tile([P, 2, PASS], I32, name="wb_t1", align_bytes=64)
+            dealt = keep.tile([P, 2, PASS], I32, name=f"wb_t{g}", align_bytes=64)
             nc.vector.tensor_copy(
-                t[:].rearrange("p a (t c i) -> p a c t i", t=4, i=4),
+                dealt[:].rearrange("p a (t c i) -> p a c t i", t=4, i=4),
                 wb_raw[g][:].rearrange("p a (c i t) -> p a c t i", t=4, i=4),
             )
-            wb_t.append(t)
+            wb_t.append(dealt)
 
         gather_tab2(0)
         reorder_wb(0)
-        part_tab2(0)
-        gather_tab(1)
         reorder_wb(1)
         gather_tab2(1)
 
-        scale = planes[:].bitcast(U8)
-        en_scale = en_planes[:].bitcast(U8)
-        out_v = out.rearrange("(s p) j -> p s j", p=P)
+        ring = []
 
-        units = [(c, g) for c in range(CHUNKS) for g in range(2)]
-        ha_of = {}
-        state = {}
+        def project(j0, width, g):
+            part, c0 = divmod(j0, HALF)
+            per_bank = BANK // width
+            sums = []
+            for t0 in range(0, 4, per_bank):
+                hb = psum.tile([P, per_bank, width], F32, name="hb", tag=f"bank{4 + len(ring) % 4}")
+                ring.append(hb)
+                for t in range(t0, t0 + per_bank):
+                    for n0 in range(0, width, P):
+                        for a in range(2):
+                            w0 = a * SLOT_B + g * PASS + t * P
+                            s0 = a * SLOT_B + R + j0 + n0
+                            nc.tensor.matmul_mx(
+                                out=hb[:, t - t0, n0 : n0 + P],
+                                lhsT=wb_t[g][:, a, t * P : (t + 1) * P].bitcast(FP8X4),
+                                lhsT_scale=scale_b[:, w0 : w0 + P],
+                                rhs=tab2_codes[part][:, a, c0 + n0 : c0 + n0 + P].bitcast(FP4X4),
+                                rhs_scale=scale_b[:, s0 : s0 + P],
+                                start=(a == 0),
+                                stop=(a == 1),
+                            )
+                sums.extend(hb[:, t - t0, :] for t in range(t0, t0 + per_bank))
+            return sums
 
-        def project_a(u):
-            c, g = units[u]
-            half, j0 = divmod(c * CHUNK, HALF)
-            ha = psum.tile([P, PASS], F32, name="ha", tag="first")
+        def difference(sums, j0, width, g):
+            diff = work.tile([P, 4, width], F32, name="diff")
             for t in range(4):
-                r0 = g * PASS + t * P
-                s0 = g * SLOT + R + t * P
-                nc.tensor.matmul_mx(
-                    out=ha[:, t * P : (t + 1) * P],
-                    lhsT=wa_t[:, r0 : r0 + P].bitcast(FP4X4),
-                    lhsT_scale=scale[:, s0 : s0 + P],
-                    rhs=tab_codes[half][:, j0 : j0 + CHUNK].bitcast(FP8X4),
-                    rhs_scale=tab_plane[:, c * CHUNK : (c + 1) * CHUNK],
-                    start=True,
-                    stop=True,
+                nc.vector.scalar_tensor_tensor(
+                    diff[:, t, :], sums[t], root[:, 4 * g + t : 4 * g + t + 1],
+                    head[g][:, t, j0 : j0 + width], ALU.mult, ALU.subtract,
                 )
-            ha_sb = work.tile([P, CHUNK, 4], F32, name="ha_sb", bufs=8)
-            nc.scalar.copy(ha_sb[:], ha[:].rearrange("p (t j) -> p j t", t=4))
-            ha_of[u] = ha_sb
+            return diff
 
-        def project_b(u):
-            c, g = units[u]
-            half, j0 = divmod(c * CHUNK, HALF)
-            hb = psum.tile([P, PASS], F32, name="hb", tag="first")
-            for t in range(4):
-                for a in range(2):
-                    w0 = a * SLOT + g * PASS + t * P
-                    s0 = a * SLOT + R + PASS + c * CHUNK
-                    nc.tensor.matmul_mx(
-                        out=hb[:, t * P : (t + 1) * P],
-                        lhsT=wb_t[g][:, a, t * P : (t + 1) * P].bitcast(FP8X4),
-                        lhsT_scale=scale[:, w0 : w0 + P],
-                        rhs=tab2_codes[half][:, a, j0 : j0 + CHUNK].bitcast(FP4X4),
-                        rhs_scale=scale[:, s0 : s0 + CHUNK],
-                        start=(a == 0),
-                        stop=(a == 1),
+        def quantised(diff, width, g, on_vector):
+            square = work.tile([P, width, 4], BF16, name="square", align_bytes=64)
+            woven = square[:].rearrange("p (c i) t -> p c t i", i=4)
+            planar = diff[:].rearrange("p t (c i) -> p c t i", i=4)
+            if on_vector:
+                nc.vector.tensor_tensor(woven, planar, planar, ALU.mult)
+            else:
+                nc.scalar.activation(woven, planar, ACT.Square)
+            h = work.tile([P, width, 4], BF16, name="h", align_bytes=64)
+            nc.vector.tensor_tensor(
+                h[:], square[:], sign[:, 4 * g : 4 * g + 4].unsqueeze(1).to_broadcast([P, width, 4]), ALU.mult
+            )
+            codes = work.tile([P, width], U32, name="h_codes", align_bytes=64)
+            scales = work.tile([P, width], U8, name="h_scales", align_bytes=64)
+            nc.vector.quantize_mx(out=codes[:].bitcast(FP8X4), scales=scales[:], in_=h[:].rearrange("p j t -> p (j t)"))
+            return codes, scales
+
+        def score(c, halves):
+            j0, width = CHUNKS[c]
+            per_bank = N // P // len(SUM_BANKS[c])
+            banks = []
+            for s0 in range(0, N // P, per_bank):
+                bank = psum.tile([P, per_bank, width], F32, name="y", tag=f"bank{SUM_BANKS[c][s0 // per_bank]}")
+                for g in range(2):
+                    codes, scales = halves[g]
+                    for s in range(per_bank):
+                        n0 = (s0 + s) * P
+                        step = width if g == 0 else P
+                        for c0 in range(0, width, step):
+                            if g == 0:
+                                lhs = en8_codes[:, n0 : n0 + P].bitcast(FP8X4)
+                            else:
+                                lhs = en4_codes[:].bitcast(U16)[:, n0 : n0 + P].bitcast(FP4X4)
+                            nc.tensor.matmul_mx(
+                                out=bank[:, s, c0 : c0 + step],
+                                lhsT=lhs,
+                                lhsT_scale=en_scale[:, g * N + n0 : g * N + n0 + P],
+                                rhs=codes[:, c0 : c0 + step].bitcast(FP8X4),
+                                rhs_scale=scales[:, c0 : c0 + step],
+                                start=(g == 0 and s == 0),
+                                stop=(g == 1 and s == per_bank - 1 and c0 + step == width),
+                            )
+                banks.append(bank)
+            return banks
+
+        def finish(c, banks):
+            j0, width = CHUNKS[c]
+            per_bank = N // P // len(banks)
+            for s0 in range(0, N // P, 2):
+                res = work.tile([P, 2, width], F32, name="res", bufs=8)
+                for s in range(s0, s0 + 2):
+                    nc.scalar.activation(
+                        res[:, s - s0, :], banks[s // per_bank][:, s % per_bank, :], ACT.Gelu_apprx_tanh, bias=bias[:, s : s + 1]
                     )
-            state[u] = hb
+                nc.sync.dma_start(out_v[:, s0 : s0 + 2, j0 : j0 + width], res[:])
 
-        def difference(u):
-            diff = work.tile([P, CHUNK, 4], F32, name="diff")
-            nc.vector.tensor_tensor(diff[:], state[u][:].rearrange("p (t j) -> p j t", t=4), ha_of[u][:], ALU.subtract)
-            square = work.tile([P, CHUNK, 4], F32, name="square", bufs=4)
-            nc.scalar.activation(square[:], diff[:], ACT.Square)
-            state[u] = square
-
-        def smooth(u):
-            g = units[u][1]
-            h = work.tile([P, CHUNK, 4], BF16, name="h", align_bytes=64)
-            nc.vector.tensor_tensor(h[:], state[u][:], sm_sb[:, g].unsqueeze(1).to_broadcast([P, CHUNK, 4]), ALU.mult)
-            state[u] = h
-
-        def quantise(u):
-            codes = work.tile([P, CHUNK], U32, name="h_codes", bufs=4, align_bytes=64)
-            scales = work.tile([P, CHUNK], U8, name="h_scales", bufs=4, align_bytes=64)
-            nc.vector.quantize_mx(out=codes[:].bitcast(FP8X4), scales=scales[:], in_=state[u][:].rearrange("p j t -> p (j t)"))
-            state[u] = (codes, scales)
-
-        banks = {}
-        closed = []
-
-        def score(u):
-            c, g = units[u]
-            codes, scales = state[u]
-            width = 2 if c == CHUNKS - 1 else 4
-            for part in range(8 // width):
-                if g == 0:
-                    if part < 2:
-                        banks[part] = psum_y.tile([P, width, CHUNK], F32, name="y")
-                    else:
-                        banks[part] = psum.tile([P, width, CHUNK], F32, name="y_last", tag="first")
-                for s in range(width):
-                    n0 = (width * part + s) * P
-                    if g == 0:
-                        lhs = en8_codes[:, n0 : n0 + P].bitcast(FP8X4)
-                    else:
-                        lhs = en4_codes[:].bitcast(U16)[:, n0 : n0 + P].bitcast(FP4X4)
-                    nc.tensor.matmul_mx(
-                        out=banks[part][:, s, :],
-                        lhsT=lhs,
-                        lhsT_scale=en_scale[:, g * N + n0 : g * N + n0 + P],
-                        rhs=codes[:].bitcast(FP8X4),
-                        rhs_scale=scales[:],
-                        start=(g == 0 and s == 0),
-                        stop=(g == 1 and s == width - 1),
-                    )
+        units = [(c, g) for c in range(len(CHUNKS)) for g in range(2)]
+        sums = {u: project(*CHUNKS[units[u][0]], units[u][1]) for u in range(AHEAD)}
+        diffs = {}
+        quants = {}
+        scored = []
+        for step in range(len(units) + 1):
+            if step < len(units):
+                c, g = units[step]
+                diffs[step] = difference(sums[step], *CHUNKS[c], g)
+            if step + AHEAD < len(units):
+                c, g = units[step + AHEAD]
+                sums[step + AHEAD] = project(*CHUNKS[c], g)
+            if step > 0:
+                c, g = units[step - 1]
+                quants[c, g] = quantised(diffs[step - 1], CHUNKS[c][1], g, (c, g) in SQUARE_ON_VECTOR)
                 if g == 1:
-                    closed.append((c, part, width, banks[part]))
-
-        def finish():
-            c, part, width, bank = closed.pop(0)
-            res = work.tile([P, width, CHUNK], F32, name="res", bufs=6)
-            for s in range(width):
-                row = width * part + s
-                nc.scalar.activation(res[:, s, :], bank[:, s, :], ACT.Gelu_apprx_tanh, bias=bias[:, row : row + 1])
-            nc.sync.dma_start(out_v[:, width * part : width * (part + 1), c * CHUNK : (c + 1) * CHUNK], res[:])
-
-        last = len(units)
-        project_a(0)
-        project_a(1)
-        project_b(0)
-        project_a(2)
-        project_b(1)
-        project_a(3)
-        project_a(4)
-        for step in range(last + 3):
-            if step < last:
-                difference(step)
-            if step + 2 < last:
-                project_b(step + 2)
-            if step + HA_AHEAD < last:
-                project_a(step + HA_AHEAD)
-            if step == 0:
-                part_tab2(1)
-            if 0 <= step - 3:
-                quantise(step - 3)
-                score(step - 3)
-            if 0 <= step - 2 < last:
-                smooth(step - 2)
-            if closed:
-                finish()
-        for left in range(len(closed)):
-            finish()
+                    scored.append(score(c, [quants[c, 0], quants[c, 1]]))
+        for c, banks in enumerate(scored):
+            finish(c, banks)

@@ -21,12 +21,11 @@ PASS = 512
 BANK = 512
 HALF = J // 2
 STAGE = 96
-SLOT_A = 1024
 SLOT_B = 1536
-AHEAD = 2
-CHUNKS = [(0, 256), (256, 128), (384, 128)]
-SUM_BANKS = [(0, 1, 2, 3), (4, 5), (6, 7)]
-SQUARE_ON_VECTOR = ()
+AHEAD = 3
+CHUNKS = [(0, 128), (128, 128), (256, 128), (384, 128)]
+SUM_BANKS = [(0, 1), (2, 3), (4, 5), (6, 7)]
+SQUARE_ON_VECTOR = ((3, 1),)
 
 
 def tile_list_kg_sqd_mix_gelu_kernel(
@@ -38,53 +37,49 @@ def tile_list_kg_sqd_mix_gelu_kernel(
         keep = ctx.enter_context(tc.tile_pool(name="keep", bufs=1))
         after_a = ctx.enter_context(tc.tile_pool(name="after_a", bufs=1))
         after_b = ctx.enter_context(tc.tile_pool(name="after_b", bufs=1))
-        after_wb_rows = ctx.enter_context(tc.tile_pool(name="after_wb_rows", bufs=1))
-        after_wa = ctx.enter_context(tc.tile_pool(name="after_wa", bufs=1))
         work = ctx.enter_context(tc.tile_pool(name="work", bufs=4))
         psum = ctx.enter_context(tc.psum_pool(name="psum", bufs=1))
 
         idx = keep.tile([P, J // 16], U16, name="idx")
         idx2 = keep.tile([P, J // 16], U16, name="idx2")
         tab_rows = keep.tile([P, T // 4], I32, name="tab_rows", align_bytes=64)
-        wa_rows = keep.tile([P, PASS // 4], I32, name="wa_rows", align_bytes=64)
-        tab2_rows = keep.tile([P, T // 4], I32, name="tab2_rows", align_bytes=64)
-        wb_rows = after_wb_rows.tile([P, R // 4], I32, name="wb_rows", offset=0, align_bytes=64)
-        staged_a = keep.tile([P, SLOT_A // 4], I32, name="staged_a", align_bytes=64)
-        planes_a = keep.tile([P, 2 * SLOT_A // 4], I32, name="planes_a", align_bytes=64)
+        first = after_a.tile([P, 560], I32, name="first", offset=4096 - 64, align_bytes=64)
+        wa_rows = first[:, : PASS // 4]
+        staged_a = keep.tile([P, PASS // 4], I32, name="staged_a", align_bytes=64)
+        staged_b = keep.tile([P, SLOT_B // 4], I32, name="staged_b", align_bytes=64)
+        planes_a = keep.tile([P, R // 4], I32, name="planes_a", align_bytes=64)
         planes_b = keep.tile([P, 2 * SLOT_B // 4], I32, name="planes_b", align_bytes=64)
         en_planes = keep.tile([P, 2 * N // 4], I32, name="en_planes", align_bytes=64)
         warm = keep.tile([P, 2], F32, name="warm")
         tab_win = keep.tile([P, T], I32, name="tab_win", align_bytes=64)
-        tab2_win = keep.tile([P, T], I32, name="tab2_win", align_bytes=64)
-        wa_raw = after_wa.tile([P, R // 2], I32, name="wa_raw", offset=0, align_bytes=64)
+        wa_raw = keep.tile([P, R // 2], I32, name="wa_raw", align_bytes=64)
         sm_sb = keep.tile([P, 8], F32, name="sm_sb")
         wb_hbm = wb_words.rearrange("a p n i -> p a (n i)")
 
         nc.vector.memset(warm[:], 0.0)
-        for rows in (tab_rows, wa_rows, tab2_rows, wb_rows):
-            nc.vector.memset(rows[0:STAGE, :], 0)
-        nc.vector.memset(en_planes[:], 0)
-        nc.gpsimd.memset(planes_a[:], 0)
-        nc.gpsimd.memset(planes_b[:], 0)
+        nc.vector.memset(wa_rows[0:STAGE, :], 0)
+        for planes in (planes_a, planes_b, en_planes):
+            nc.vector.memset(planes[:], 0)
         nc.scalar.activation(warm[:, 1:2], warm[:, 0:1], ACT.Sqrt)
 
-        nc.sync.dma_start(idx[:], offs)
-        nc.sync.dma_start(tab_rows[STAGE:, :], tab_scales[0].bitcast(I32).unsqueeze(1).to_broadcast([16, 2, T // 4]))
         nc.sync.dma_start(wa_rows[STAGE:, :], wa_scales[0].rearrange("q (g n) -> (q g) n", g=2).bitcast(I32))
+        nc.sync.dma_start(idx[:], offs)
         nc.sync.dma_start(sm_sb[:].rearrange("p (g t) -> p g t", g=2), sm.rearrange("(g p t) -> p g t", g=2, t=4))
+        for q in (0, 2, 1, 3):
+            nc.sync.dma_start(
+                tab_rows[32 * q : 32 * q + 32, :],
+                tab_scales[0, 4 * q : 4 * q + 4, :].bitcast(I32).unsqueeze(0).to_broadcast([8, 4, T // 4]),
+            )
         nc.sync.dma_start(tab_win[:], tab_words[0].rearrange("p t i -> p (t i)").bitcast(I32))
         nc.sync.dma_start(wa_raw[:], wa_words[0].bitcast(I32))
         nc.sync.dma_start(idx2[:], offs2)
-        nc.sync.dma_start(tab2_rows[STAGE:, :], tab2_scales.rearrange("a q t -> q a t").bitcast(I32))
-        nc.sync.dma_start(wb_rows[STAGE:, :], wb_scales.rearrange("a q n -> q a n").bitcast(I32))
-        nc.sync.dma_start(tab2_win[:], tab2_words[0].rearrange("p t i -> p (t i)").bitcast(I32))
 
         sign = keep.tile([P, 8], BF16, name="sign")
         size = keep.tile([P, 8], F32, name="size")
         root = keep.tile([P, 8], F32, name="root")
-        nc.scalar.activation(sign[:], sm_sb[:], ACT.Sign)
         nc.scalar.activation(size[:], sm_sb[:], ACT.Abs)
         nc.scalar.activation(root[:], size[:], ACT.Sqrt)
+        nc.scalar.activation(sign[:], sm_sb[:], ACT.Sign)
         nc.scalar.activation(warm[:, 0:1], root[:, 0:1], ACT.Gelu_apprx_tanh)
 
         def place(planes, staged):
@@ -99,33 +94,46 @@ def tile_list_kg_sqd_mix_gelu_kernel(
                 src.bitcast(U8).rearrange("p (g c i t) -> p c g t i", g=groups, t=4, i=16),
             )
 
-        picked = after_a.tile([P, J // 4], I32, name="picked", offset=4096 - 256, align_bytes=64)
-        nc.vector.tensor_copy(picked[:].bitcast(U8), tab_rows[:].bitcast(U8).indirect(idx[:]))
-        deal_scales(staged_a[:, : PASS // 4], wa_rows[:], 1)
-        nc.vector.tensor_copy(staged_a[:, PASS // 4 :], picked[:])
+        deal_scales(staged_a[:], wa_rows, 1)
         place(planes_a, staged_a[STAGE:, :])
-        wb_raw = []
+        tab2_rows = after_a.tile([P, T // 4], I32, name="tab2_rows", offset=4096, align_bytes=64)
+        wb_rows = after_a.tile([P, R // 4], I32, name="wb_rows", offset=5120, align_bytes=64)
+        nc.sync.dma_start(tab2_rows[STAGE:, :], tab2_scales.rearrange("a q t -> q a t").bitcast(I32))
+        nc.sync.dma_start(wb_rows[STAGE:, :], wb_scales.rearrange("a q n -> q a n").bitcast(I32))
+        for rows in (tab2_rows, wb_rows):
+            nc.gpsimd.memset(rows[0:STAGE, :], 0)
+        tab2_win = after_a.tile([P, T], I32, name="tab2_win", offset=0, align_bytes=64)
+        nc.sync.dma_start(tab2_win[:], tab2_words[0].rearrange("p t i -> p (t i)").bitcast(I32))
+        wb_both = after_a.tile([P, 2, 2, PASS], I32, name="wb_both", offset=6144, align_bytes=64)
+        wb_raw = [wb_both[:, g] for g in range(2)]
         for g in range(2):
-            raw = after_a.tile([P, 2, PASS], I32, name=f"wb_raw{g}", offset=4096 * g, align_bytes=64)
-            nc.sync.dma_start(raw[:], wb_hbm[:, :, 4 * PASS * g : 4 * PASS * (g + 1)].bitcast(I32))
-            wb_raw.append(raw)
+            nc.sync.dma_start(wb_raw[g], wb_hbm[:, :, 4 * PASS * g : 4 * PASS * (g + 1)].bitcast(I32))
 
-        picked2 = after_b.tile([P, J // 4], I32, name="picked2", offset=4096 - 64, align_bytes=64)
-        nc.vector.tensor_copy(picked2[:].bitcast(U8), tab2_rows[:].bitcast(U8).indirect(idx2[:]))
-        tab_codes = keep.tile([P, J], U32, name="tab_codes", align_bytes=64)
-        nc.vector.tensor_copy(tab_codes[:], tab_win[:].bitcast(U32).indirect(idx[:]))
+        tab_plane = keep.tile([P, J], U8, name="tab_plane", align_bytes=64)
+        nc.vector.tensor_copy(tab_plane[:], tab_rows[:].bitcast(U8).indirect(idx[:]))
+        tab_codes = []
+
+        def gather_tab(part):
+            cols = slice(part * HALF // 16, (part + 1) * HALF // 16)
+            codes = keep.tile([P, HALF], U32, name=f"tab_codes{part}", align_bytes=64)
+            nc.vector.tensor_copy(codes[:], tab_win[:].bitcast(U32).indirect(idx[:, cols]))
+            tab_codes.append(codes)
+
+        gather_tab(0)
         wa_t = keep.tile([P, R], U16, name="wa_t", align_bytes=64)
         nc.vector.tensor_copy(
             wa_t[:].rearrange("p (g t c i) -> p g c t i", g=2, t=4, i=8),
             wa_raw[:].bitcast(U16).rearrange("p (g c i t) -> p g c t i", g=2, t=4, i=8),
         )
+        gather_tab(1)
 
-        staged_b = after_wa.tile([P, SLOT_B // 4], I32, name="staged_b", offset=0, align_bytes=64)
+        picked2 = after_b.tile([P, J // 4], I32, name="picked2", offset=4096 - 64, align_bytes=64)
+        nc.vector.tensor_copy(picked2[:].bitcast(U8), tab2_rows[:].bitcast(U8).indirect(idx2[:]))
         deal_scales(staged_b[:, : R // 4], wb_rows[:], 2)
         nc.vector.tensor_copy(staged_b[:, R // 4 :], picked2[:])
         place(planes_b, staged_b[STAGE:, :])
 
-        en_rows = after_wb_rows.tile([32, N // 4], I32, name="en_rows", offset=0, align_bytes=64)
+        en_rows = after_a.tile([32, N // 4], I32, name="en_rows", offset=5120, align_bytes=64)
         nc.sync.dma_start(en_rows[0:32:2, :], en8_scales[0].bitcast(I32))
         nc.sync.dma_start(en_rows[1:32:2, :], en4_scales[0].bitcast(I32))
         en8_codes = after_b.tile([P, N], I32, name="en8_codes", offset=0, align_bytes=64)
@@ -142,23 +150,33 @@ def tile_list_kg_sqd_mix_gelu_kernel(
         en_scale = en_planes[:].bitcast(U8)
         out_v = out.rearrange("(s p) j -> p s j", p=P)
 
-        head = []
-        for g in range(2):
-            rows = keep.tile([P, 4, J], F32, name=f"head{g}")
-            for t in range(4):
-                ha = psum.tile([P, BANK], F32, name="ha", tag=f"bank{t}")
-                s0 = g * SLOT_A + t * P
-                nc.tensor.matmul_mx(
-                    out=ha[:],
-                    lhsT=wa_t[:, g * PASS + t * P : g * PASS + (t + 1) * P].bitcast(FP4X4),
-                    lhsT_scale=scale_a[:, s0 : s0 + P],
-                    rhs=tab_codes[:].bitcast(FP8X4),
-                    rhs_scale=scale_a[:, g * SLOT_A + PASS : (g + 1) * SLOT_A],
-                    start=True,
-                    stop=True,
-                )
-                nc.scalar.activation(rows[:, t, :], ha[:], ACT.Copy, scale=root[:, 4 * g + t : 4 * g + t + 1])
-            head.append(rows)
+        head = {}
+
+        def project_head(part):
+            j0 = part * HALF
+            for g in range(2):
+                rows = keep.tile([P, 4, HALF], F32, name=f"head{part}{g}")
+                for t0 in (0, 2):
+                    ha = psum.tile([P, 2, HALF], F32, name="ha", tag=f"bank{2 * g + t0 // 2}")
+                    for t in (t0, t0 + 1):
+                        s0 = g * PASS + t * P
+                        nc.tensor.matmul_mx(
+                            out=ha[:, t - t0, :],
+                            lhsT=wa_t[:, g * PASS + t * P : g * PASS + (t + 1) * P].bitcast(FP4X4),
+                            lhsT_scale=scale_a[:, s0 : s0 + P],
+                            rhs=tab_codes[part][:].bitcast(FP8X4),
+                            rhs_scale=tab_plane[:, j0 : j0 + HALF],
+                            start=True,
+                            stop=True,
+                        )
+                    for t in (t0, t0 + 1):
+                        nc.scalar.activation(
+                            rows[:, t, :], ha[:, t - t0, :], ACT.Copy, scale=root[:, 4 * g + t : 4 * g + t + 1]
+                        )
+                head[part, g] = rows
+
+        project_head(0)
+        project_head(1)
 
         tab2_codes = []
         wb_t = []
@@ -178,7 +196,7 @@ def tile_list_kg_sqd_mix_gelu_kernel(
             dealt = keep.tile([P, 2, PASS], I32, name=f"wb_t{g}", align_bytes=64)
             nc.vector.tensor_copy(
                 dealt[:].rearrange("p a (t c i) -> p a c t i", t=4, i=4),
-                wb_raw[g][:].rearrange("p a (c i t) -> p a c t i", t=4, i=4),
+                wb_raw[g].rearrange("p a (c i t) -> p a c t i", t=4, i=4),
             )
             wb_t.append(dealt)
 
@@ -218,7 +236,7 @@ def tile_list_kg_sqd_mix_gelu_kernel(
             for t in range(4):
                 nc.vector.scalar_tensor_tensor(
                     diff[:, t, :], sums[t], root[:, 4 * g + t : 4 * g + t + 1],
-                    head[g][:, t, j0 : j0 + width], ALU.mult, ALU.subtract,
+                    head[j0 // HALF, g][:, t, j0 % HALF : j0 % HALF + width], ALU.mult, ALU.subtract,
                 )
             return diff
 

@@ -1,6 +1,7 @@
 from contextlib import ExitStack
 
 import concourse.mybir as mybir
+from concourse.masks import make_identity
 
 K, L, R, N, T, J = 512, 1024, 1024, 1024, 1024, 512
 FLOPS = 2 * J * (K * R + L * R + R * N)
@@ -24,7 +25,7 @@ STAGE = 96
 SLOT_B = 1536
 AHEAD = 3
 CHUNKS = [(0, 128), (128, 128), (256, 128), (384, 128)]
-SUM_BANKS = [(0, 1), (2, 3), (4, 5), (6, 7)]
+GROUPS = [((0,), (0, 1)), ((1,), (2, 3)), ((2,), (4, 5)), ((3,), (6, 0, 1, 7))]
 SQUARE_ON_VECTOR = ((3, 1),)
 
 
@@ -43,7 +44,7 @@ def tile_list_kg_sqd_mix_gelu_kernel(
         idx = keep.tile([P, J // 16], U16, name="idx")
         idx2 = keep.tile([P, J // 16], U16, name="idx2")
         tab_rows = keep.tile([P, T // 4], I32, name="tab_rows", align_bytes=64)
-        first = after_a.tile([P, 560], I32, name="first", offset=4096 - 64, align_bytes=64)
+        first = after_a.tile([P, 688], I32, name="first", offset=4096 - 64, align_bytes=64)
         wa_rows = first[:, : PASS // 4]
         staged_a = keep.tile([P, PASS // 4], I32, name="staged_a", align_bytes=64)
         staged_b = keep.tile([P, SLOT_B // 4], I32, name="staged_b", align_bytes=64)
@@ -53,10 +54,13 @@ def tile_list_kg_sqd_mix_gelu_kernel(
         warm = keep.tile([P, 2], F32, name="warm")
         tab_win = keep.tile([P, T], I32, name="tab_win", align_bytes=64)
         wa_raw = keep.tile([P, R // 2], I32, name="wa_raw", align_bytes=64)
-        sm_sb = keep.tile([P, 8], F32, name="sm_sb")
+        vectors = keep.tile([P, PASS], F32, name="vectors")
+        identity = keep.tile([P, P], F32, name="identity")
         wb_hbm = wb_words.rearrange("a p n i -> p a (n i)")
 
         nc.vector.memset(warm[:], 0.0)
+        nc.vector.memset(vectors[0:STAGE, :], 0.0)
+        make_identity(nc, identity[:])
         nc.vector.memset(wa_rows[0:STAGE, :], 0)
         for planes in (planes_a, planes_b, en_planes):
             nc.vector.memset(planes[:], 0)
@@ -64,7 +68,7 @@ def tile_list_kg_sqd_mix_gelu_kernel(
 
         nc.sync.dma_start(wa_rows[STAGE:, :], wa_scales[0].rearrange("q (g n) -> (q g) n", g=2).bitcast(I32))
         nc.sync.dma_start(idx[:], offs)
-        nc.sync.dma_start(sm_sb[:].rearrange("p (g t) -> p g t", g=2), sm.rearrange("(g p t) -> p g t", g=2, t=4))
+        nc.sync.dma_start(vectors[STAGE:, :PASS], sm.rearrange("(g r) -> g r", g=2).unsqueeze(0).to_broadcast([16, 2, PASS]))
         for q in (0, 2, 1, 3):
             nc.sync.dma_start(
                 tab_rows[32 * q : 32 * q + 32, :],
@@ -77,9 +81,13 @@ def tile_list_kg_sqd_mix_gelu_kernel(
         sign = keep.tile([P, 8], BF16, name="sign")
         size = keep.tile([P, 8], F32, name="size")
         root = keep.tile([P, 8], F32, name="root")
-        nc.scalar.activation(size[:], sm_sb[:], ACT.Abs)
+        sm_turned = psum.tile([P, 4, P], F32, name="sm_turned", tag="bank4")
+        for t in range(4):
+            nc.tensor.transpose(sm_turned[:, t, :], vectors[:, t:PASS:4], identity[:])
+        sm_dealt = sm_turned[:, :, STAGE : STAGE + 2].rearrange("p t g -> p g t")
+        nc.scalar.activation(size[:].rearrange("p (g t) -> p g t", g=2), sm_dealt, ACT.Abs)
         nc.scalar.activation(root[:], size[:], ACT.Sqrt)
-        nc.scalar.activation(sign[:], sm_sb[:], ACT.Sign)
+        nc.scalar.activation(sign[:].rearrange("p (g t) -> p g t", g=2), sm_dealt, ACT.Sign)
         nc.scalar.activation(warm[:, 0:1], root[:, 0:1], ACT.Gelu_apprx_tanh)
 
         def place(planes, staged):
@@ -100,11 +108,18 @@ def tile_list_kg_sqd_mix_gelu_kernel(
         wb_rows = after_a.tile([P, R // 4], I32, name="wb_rows", offset=5120, align_bytes=64)
         nc.sync.dma_start(tab2_rows[STAGE:, :], tab2_scales.rearrange("a q t -> q a t").bitcast(I32))
         nc.sync.dma_start(wb_rows[STAGE:, :], wb_scales.rearrange("a q n -> q a n").bitcast(I32))
+        b_rows = after_a.tile([P, P], F32, name="b_rows", offset=6144, align_bytes=64)
+        nc.sync.dma_start(b_rows[STAGE:, :], b.rearrange("(s p) -> s p", p=P).unsqueeze(0).to_broadcast([4, N // P, P]))
+        nc.gpsimd.memset(b_rows[0:STAGE, :], 0.0)
+        b_turned = psum.tile([P, P], F32, name="b_turned", tag="bank5")
+        nc.tensor.transpose(b_turned[:], b_rows[:], identity[:])
+        bias = keep.tile([P, N // P], F32, name="bias")
+        nc.scalar.copy(bias[:], b_turned[:, STAGE : STAGE + N // P])
         for rows in (tab2_rows, wb_rows):
             nc.gpsimd.memset(rows[0:STAGE, :], 0)
         tab2_win = after_a.tile([P, T], I32, name="tab2_win", offset=0, align_bytes=64)
         nc.sync.dma_start(tab2_win[:], tab2_words[0].rearrange("p t i -> p (t i)").bitcast(I32))
-        wb_both = after_a.tile([P, 2, 2, PASS], I32, name="wb_both", offset=6144, align_bytes=64)
+        wb_both = after_a.tile([P, 2, 2, PASS], I32, name="wb_both", offset=6656, align_bytes=64)
         wb_raw = [wb_both[:, g] for g in range(2)]
         for g in range(2):
             nc.sync.dma_start(wb_raw[g], wb_hbm[:, :, 4 * PASS * g : 4 * PASS * (g + 1)].bitcast(I32))
@@ -140,9 +155,6 @@ def tile_list_kg_sqd_mix_gelu_kernel(
         nc.sync.dma_start(en8_codes[:], en8_words[0].rearrange("p n i -> p (n i)").bitcast(I32))
         en4_codes = after_b.tile([P, N // 2], I32, name="en4_codes", offset=4096 + 128, align_bytes=64)
         nc.sync.dma_start(en4_codes[:], en4_words[0].bitcast(I32))
-        bias = after_b.tile([P, N // P], F32, name="bias", offset=4096, align_bytes=64)
-        with nc.allow_non_contiguous_dma(reason="one bias value for each partition and tile of 128 rows"):
-            nc.sync.dma_start(bias[:], b.rearrange("(s p) -> p s", p=P))
         place(en_planes, en_rows)
 
         scale_a = planes_a[:].bitcast(U8)
@@ -257,36 +269,38 @@ def tile_list_kg_sqd_mix_gelu_kernel(
             nc.vector.quantize_mx(out=codes[:].bitcast(FP8X4), scales=scales[:], in_=h[:].rearrange("p j t -> p (j t)"))
             return codes, scales
 
-        def score(c, halves):
-            j0, width = CHUNKS[c]
-            per_bank = N // P // len(SUM_BANKS[c])
-            banks = []
-            for s0 in range(0, N // P, per_bank):
-                bank = psum.tile([P, per_bank, width], F32, name="y", tag=f"bank{SUM_BANKS[c][s0 // per_bank]}")
-                for g in range(2):
-                    codes, scales = halves[g]
-                    for s in range(per_bank):
-                        n0 = (s0 + s) * P
-                        step = width if g == 0 else P
-                        for c0 in range(0, width, step):
-                            if g == 0:
-                                lhs = en8_codes[:, n0 : n0 + P].bitcast(FP8X4)
-                            else:
-                                lhs = en4_codes[:].bitcast(U16)[:, n0 : n0 + P].bitcast(FP4X4)
-                            nc.tensor.matmul_mx(
-                                out=bank[:, s, c0 : c0 + step],
-                                lhsT=lhs,
-                                lhsT_scale=en_scale[:, g * N + n0 : g * N + n0 + P],
-                                rhs=codes[:, c0 : c0 + step].bitcast(FP8X4),
-                                rhs_scale=scales[:, c0 : c0 + step],
-                                start=(g == 0 and s == 0),
-                                stop=(g == 1 and s == per_bank - 1 and c0 + step == width),
-                            )
-                banks.append(bank)
-            return banks
+        group_of = {c: (chunks, banks) for chunks, banks in GROUPS for c in chunks}
+        sums_of = {}
 
-        def finish(c, banks):
-            j0, width = CHUNKS[c]
+        def score(c, g, codes, scales):
+            chunks, banks = group_of[c]
+            width = CHUNKS[c][1]
+            per_bank = N // P // len(banks)
+            if c == chunks[0] and g == 0:
+                sums_of[chunks] = [
+                    psum.tile([P, per_bank, len(chunks) * width], F32, name="y", tag=f"bank{bank}") for bank in banks
+                ]
+            c0 = (c - chunks[0]) * width
+            for s in range(N // P):
+                n0 = s * P
+                if g == 0:
+                    lhs = en8_codes[:, n0 : n0 + P].bitcast(FP8X4)
+                else:
+                    lhs = en4_codes[:].bitcast(U16)[:, n0 : n0 + P].bitcast(FP4X4)
+                nc.tensor.matmul_mx(
+                    out=sums_of[chunks][s // per_bank][:, s % per_bank, c0 : c0 + width],
+                    lhsT=lhs,
+                    lhsT_scale=en_scale[:, g * N + n0 : g * N + n0 + P],
+                    rhs=codes[:].bitcast(FP8X4),
+                    rhs_scale=scales[:],
+                    start=(c == chunks[0] and g == 0 and s % per_bank == 0),
+                    stop=(c == chunks[-1] and g == 1 and s % per_bank == per_bank - 1),
+                )
+
+        def finish(chunks):
+            j0 = CHUNKS[chunks[0]][0]
+            width = len(chunks) * CHUNKS[chunks[0]][1]
+            banks = sums_of[chunks]
             per_bank = N // P // len(banks)
             for s0 in range(0, N // P, 2):
                 res = work.tile([P, 2, width], F32, name="res", bufs=8)
@@ -299,8 +313,6 @@ def tile_list_kg_sqd_mix_gelu_kernel(
         units = [(c, g) for c in range(len(CHUNKS)) for g in range(2)]
         sums = {u: project(*CHUNKS[units[u][0]], units[u][1]) for u in range(AHEAD)}
         diffs = {}
-        quants = {}
-        scored = []
         for step in range(len(units) + 1):
             if step < len(units):
                 c, g = units[step]
@@ -310,8 +322,6 @@ def tile_list_kg_sqd_mix_gelu_kernel(
                 sums[step + AHEAD] = project(*CHUNKS[c], g)
             if step > 0:
                 c, g = units[step - 1]
-                quants[c, g] = quantised(diffs[step - 1], CHUNKS[c][1], g, (c, g) in SQUARE_ON_VECTOR)
-                if g == 1:
-                    scored.append(score(c, [quants[c, 0], quants[c, 1]]))
-        for c, banks in enumerate(scored):
-            finish(c, banks)
+                score(c, g, *quantised(diffs[step - 1], CHUNKS[c][1], g, (c, g) in SQUARE_ON_VECTOR))
+        for chunks, banks in GROUPS:
+            finish(chunks)

@@ -26,7 +26,7 @@ SLOT_B = 1536
 AHEAD = 3
 CHUNKS = [(0, 128), (128, 128), (256, 128), (384, 128)]
 GROUPS = [((0,), (0, 1)), ((1,), (2, 3)), ((2,), (4, 5)), ((3,), (6, 0, 1, 7))]
-SQUARE_ON_VECTOR = ((3, 1),)
+SQUARE_ON_VECTOR = ((1, 1), (2, 1), (3, 1))
 
 
 def tile_list_kg_sqd_mix_gelu_kernel(

@@ -26,7 +26,7 @@ SLOT_B = 1536
 AHEAD = 3
 CHUNKS = [(0, 128), (128, 128), (256, 128), (384, 128)]
 GROUPS = [((0,), (0, 1)), ((1,), (2, 3)), ((2,), (4, 5)), ((3,), (6, 0, 1, 7))]
-SQUARE_ON_VECTOR = ((1, 1), (2, 1), (3, 1))
+SQUARE_ON_VECTOR = ((3, 0), (3, 1))
 
 
 def tile_list_kg_sqd_mix_gelu_kernel(
@@ -126,21 +126,13 @@ def tile_list_kg_sqd_mix_gelu_kernel(
 
         tab_plane = keep.tile([P, J], U8, name="tab_plane", align_bytes=64)
         nc.vector.tensor_copy(tab_plane[:], tab_rows[:].bitcast(U8).indirect(idx[:]))
-        tab_codes = []
-
-        def gather_tab(part):
-            cols = slice(part * HALF // 16, (part + 1) * HALF // 16)
-            codes = keep.tile([P, HALF], U32, name=f"tab_codes{part}", align_bytes=64)
-            nc.vector.tensor_copy(codes[:], tab_win[:].bitcast(U32).indirect(idx[:, cols]))
-            tab_codes.append(codes)
-
-        gather_tab(0)
+        tab_codes = keep.tile([P, J], U32, name="tab_codes", align_bytes=64)
+        nc.vector.tensor_copy(tab_codes[:], tab_win[:].bitcast(U32).indirect(idx[:]))
         wa_t = keep.tile([P, R], U16, name="wa_t", align_bytes=64)
         nc.vector.tensor_copy(
             wa_t[:].rearrange("p (g t c i) -> p g c t i", g=2, t=4, i=8),
             wa_raw[:].bitcast(U16).rearrange("p (g c i t) -> p g c t i", g=2, t=4, i=8),
         )
-        gather_tab(1)
 
         picked2 = after_b.tile([P, J // 4], I32, name="picked2", offset=4096 - 64, align_bytes=64)
         nc.vector.tensor_copy(picked2[:].bitcast(U8), tab2_rows[:].bitcast(U8).indirect(idx2[:]))
@@ -162,33 +154,23 @@ def tile_list_kg_sqd_mix_gelu_kernel(
         en_scale = en_planes[:].bitcast(U8)
         out_v = out.rearrange("(s p) j -> p s j", p=P)
 
-        head = {}
-
-        def project_head(part):
-            j0 = part * HALF
-            for g in range(2):
-                rows = keep.tile([P, 4, HALF], F32, name=f"head{part}{g}")
-                for t0 in (0, 2):
-                    ha = psum.tile([P, 2, HALF], F32, name="ha", tag=f"bank{2 * g + t0 // 2}")
-                    for t in (t0, t0 + 1):
-                        s0 = g * PASS + t * P
-                        nc.tensor.matmul_mx(
-                            out=ha[:, t - t0, :],
-                            lhsT=wa_t[:, g * PASS + t * P : g * PASS + (t + 1) * P].bitcast(FP4X4),
-                            lhsT_scale=scale_a[:, s0 : s0 + P],
-                            rhs=tab_codes[part][:].bitcast(FP8X4),
-                            rhs_scale=tab_plane[:, j0 : j0 + HALF],
-                            start=True,
-                            stop=True,
-                        )
-                    for t in (t0, t0 + 1):
-                        nc.scalar.activation(
-                            rows[:, t, :], ha[:, t - t0, :], ACT.Copy, scale=root[:, 4 * g + t : 4 * g + t + 1]
-                        )
-                head[part, g] = rows
-
-        project_head(0)
-        project_head(1)
+        head = []
+        for g in range(2):
+            rows = keep.tile([P, 4, J], F32, name=f"head{g}")
+            for t in range(4):
+                ha = psum.tile([P, BANK], F32, name="ha", tag=f"bank{t}")
+                s0 = g * PASS + t * P
+                nc.tensor.matmul_mx(
+                    out=ha[:],
+                    lhsT=wa_t[:, s0 : s0 + P].bitcast(FP4X4),
+                    lhsT_scale=scale_a[:, s0 : s0 + P],
+                    rhs=tab_codes[:].bitcast(FP8X4),
+                    rhs_scale=tab_plane[:],
+                    start=True,
+                    stop=True,
+                )
+                nc.scalar.activation(rows[:, t, :], ha[:], ACT.Copy, scale=root[:, 4 * g + t : 4 * g + t + 1])
+            head.append(rows)
 
         tab2_codes = []
         wb_t = []
@@ -248,14 +230,14 @@ def tile_list_kg_sqd_mix_gelu_kernel(
             for t in range(4):
                 nc.vector.scalar_tensor_tensor(
                     diff[:, t, :], sums[t], root[:, 4 * g + t : 4 * g + t + 1],
-                    head[j0 // HALF, g][:, t, j0 % HALF : j0 % HALF + width], ALU.mult, ALU.subtract,
+                    head[g][:, t, j0 : j0 + width], ALU.mult, ALU.subtract,
                 )
             return diff
 
         def quantised(diff, width, g, on_vector):
             square = work.tile([P, width, 4], BF16, name="square", align_bytes=64)
-            woven = square[:].rearrange("p (c i) t -> p c t i", i=4)
-            planar = diff[:].rearrange("p t (c i) -> p c t i", i=4)
+            woven = square[:].rearrange("p (c i) t -> p c t i", i=2)
+            planar = diff[:].rearrange("p t (c i) -> p c t i", i=2)
             if on_vector:
                 nc.vector.tensor_tensor(woven, planar, planar, ALU.mult)
             else:

@@ -25,7 +25,7 @@ STAGE = 96
 SLOT_B = 1536
 AHEAD = 3
 CHUNKS = [(0, 128), (128, 128), (256, 128), (384, 128)]
-GROUPS = [((0,), (0, 1)), ((1,), (2, 3)), ((2,), (4, 5)), ((3,), (6, 0, 1, 7))]
+GROUPS = [((0, 1), (0, 1, 2, 3)), ((2,), (4, 5)), ((3,), (6, 0, 1, 7))]
 SQUARE_ON_VECTOR = ((3, 0), (3, 1))
 
 

@@ -1,7 +1,6 @@
 from contextlib import ExitStack
 
 import concourse.mybir as mybir
-from concourse.masks import make_identity
 
 K, L, R, N, T, J = 512, 1024, 1024, 1024, 1024, 512
 FLOPS = 2 * J * (K * R + L * R + R * N)
@@ -22,7 +21,7 @@ PASS = 512
 BANK = 512
 HALF = J // 2
 STAGE = 96
-SLOT_B = 1536
+SLOT = 1024
 AHEAD = 3
 CHUNKS = [(0, 128), (128, 128), (256, 128), (384, 128)]
 GROUPS = [((0, 1), (0, 1, 2, 3)), ((2,), (4, 5)), ((3,), (6, 0, 1, 7))]
@@ -43,32 +42,33 @@ def tile_list_kg_sqd_mix_gelu_kernel(
 
         idx = keep.tile([P, J // 16], U16, name="idx")
         idx2 = keep.tile([P, J // 16], U16, name="idx2")
-        tab_rows = keep.tile([P, T // 4], I32, name="tab_rows", align_bytes=64)
-        first = after_a.tile([P, 688], I32, name="first", offset=4096 - 64, align_bytes=64)
+        first = after_a.tile([P, 2 * T + PASS], I32, name="first", offset=0, align_bytes=64)
         wa_rows = first[:, : PASS // 4]
+        wb_rows = keep.tile([P, PASS // 4], I32, name="wb_rows", align_bytes=64)
         staged_a = keep.tile([P, PASS // 4], I32, name="staged_a", align_bytes=64)
-        staged_b = keep.tile([P, SLOT_B // 4], I32, name="staged_b", align_bytes=64)
+        tab_rows = keep.tile([P, T // 4], I32, name="tab_rows", align_bytes=64)
+        tab2_rows = keep.tile([P, T // 4], I32, name="tab2_rows", align_bytes=64)
+        staged = keep.tile([P, SLOT // 4], I32, name="staged", align_bytes=64)
         planes_a = keep.tile([P, R // 4], I32, name="planes_a", align_bytes=64)
-        planes_b = keep.tile([P, 2 * SLOT_B // 4], I32, name="planes_b", align_bytes=64)
+        planes_b = keep.tile([P, 4 * SLOT // 4], I32, name="planes_b", align_bytes=64)
         en_planes = keep.tile([P, 2 * N // 4], I32, name="en_planes", align_bytes=64)
         warm = keep.tile([P, 2], F32, name="warm")
         tab_win = keep.tile([P, T], I32, name="tab_win", align_bytes=64)
         wa_raw = keep.tile([P, R // 2], I32, name="wa_raw", align_bytes=64)
-        vectors = keep.tile([P, PASS], F32, name="vectors")
-        identity = keep.tile([P, P], F32, name="identity")
+        sm_dealt = keep.tile([P, 2, 4], F32, name="sm_dealt")
         wb_hbm = wb_words.rearrange("a p n i -> p a (n i)")
 
         nc.vector.memset(warm[:], 0.0)
-        nc.vector.memset(vectors[0:STAGE, :], 0.0)
-        make_identity(nc, identity[:])
+        nc.vector.memset(tab2_rows[:], 0)
         nc.vector.memset(wa_rows[0:STAGE, :], 0)
-        for planes in (planes_a, planes_b, en_planes):
-            nc.vector.memset(planes[:], 0)
+        nc.vector.memset(wb_rows[64:, :], 0)
+        nc.vector.memset(planes_a[:], 0)
+        nc.vector.memset(planes_b[:], 0)
         nc.scalar.activation(warm[:, 1:2], warm[:, 0:1], ACT.Sqrt)
 
         nc.sync.dma_start(wa_rows[STAGE:, :], wa_scales[0].rearrange("q (g n) -> (q g) n", g=2).bitcast(I32))
         nc.sync.dma_start(idx[:], offs)
-        nc.sync.dma_start(vectors[STAGE:, :PASS], sm.rearrange("(g r) -> g r", g=2).unsqueeze(0).to_broadcast([16, 2, PASS]))
+        nc.sync.dma_start(sm_dealt[:], sm.rearrange("(g p t) -> p g t", g=2, t=4))
         for q in (0, 2, 1, 3):
             nc.sync.dma_start(
                 tab_rows[32 * q : 32 * q + 32, :],
@@ -77,49 +77,40 @@ def tile_list_kg_sqd_mix_gelu_kernel(
         nc.sync.dma_start(tab_win[:], tab_words[0].rearrange("p t i -> p (t i)").bitcast(I32))
         nc.sync.dma_start(wa_raw[:], wa_words[0].bitcast(I32))
         nc.sync.dma_start(idx2[:], offs2)
+        nc.sync.dma_start(tab2_rows[0:64:2, :], tab2_scales.rearrange("a q t -> q a t").bitcast(I32))
+        for g, queue in enumerate((nc.sync, nc.gpsimd)):
+            queue.dma_start(
+                wb_rows[g:64:2, :], wb_scales[:, :, g * PASS : (g + 1) * PASS].rearrange("a q n -> q a n").bitcast(I32)
+            )
+
+        nc.gpsimd.memset(en_planes[:], 0)
 
         sign = keep.tile([P, 8], BF16, name="sign")
         size = keep.tile([P, 8], F32, name="size")
         root = keep.tile([P, 8], F32, name="root")
-        sm_turned = psum.tile([P, 4, P], F32, name="sm_turned", tag="bank4")
-        for t in range(4):
-            nc.tensor.transpose(sm_turned[:, t, :], vectors[:, t:PASS:4], identity[:])
-        sm_dealt = sm_turned[:, :, STAGE : STAGE + 2].rearrange("p t g -> p g t")
-        nc.scalar.activation(size[:].rearrange("p (g t) -> p g t", g=2), sm_dealt, ACT.Abs)
+        nc.scalar.activation(size[:].rearrange("p (g t) -> p g t", g=2), sm_dealt[:], ACT.Abs)
         nc.scalar.activation(root[:], size[:], ACT.Sqrt)
-        nc.scalar.activation(sign[:].rearrange("p (g t) -> p g t", g=2), sm_dealt, ACT.Sign)
+        nc.scalar.activation(sign[:].rearrange("p (g t) -> p g t", g=2), sm_dealt[:], ACT.Sign)
         nc.scalar.activation(warm[:, 0:1], root[:, 0:1], ACT.Gelu_apprx_tanh)
 
-        def place(planes, staged):
+        def place(planes, rows, pieces):
             for q in (0, 2, 1, 3):
                 nc.sync.dma_start(
-                    planes[32 * q : 32 * q + 4, :].rearrange("p (k n) -> p k n", k=2), staged[8 * q : 8 * q + 8, :]
+                    planes[32 * q : 32 * q + 4, :].rearrange("p (k n) -> p k n", k=pieces),
+                    rows[4 * pieces * q : 4 * pieces * (q + 1), :],
                 )
 
-        def deal_scales(dst, src, groups):
+        def deal_scales(dst, src):
             nc.vector.tensor_copy(
-                dst.bitcast(U8).rearrange("p (g t c i) -> p c g t i", g=groups, t=4, i=16),
-                src.bitcast(U8).rearrange("p (g c i t) -> p c g t i", g=groups, t=4, i=16),
+                dst.bitcast(U8).rearrange("p (t c i) -> p c t i", t=4, i=16),
+                src.bitcast(U8).rearrange("p (c i t) -> p c t i", t=4, i=16),
             )
 
-        deal_scales(staged_a[:], wa_rows, 1)
-        place(planes_a, staged_a[STAGE:, :])
-        tab2_rows = after_a.tile([P, T // 4], I32, name="tab2_rows", offset=4096, align_bytes=64)
-        wb_rows = after_a.tile([P, R // 4], I32, name="wb_rows", offset=5120, align_bytes=64)
-        nc.sync.dma_start(tab2_rows[STAGE:, :], tab2_scales.rearrange("a q t -> q a t").bitcast(I32))
-        nc.sync.dma_start(wb_rows[STAGE:, :], wb_scales.rearrange("a q n -> q a n").bitcast(I32))
-        b_rows = after_a.tile([P, P], F32, name="b_rows", offset=6144, align_bytes=64)
-        nc.sync.dma_start(b_rows[STAGE:, :], b.rearrange("(s p) -> s p", p=P).unsqueeze(0).to_broadcast([4, N // P, P]))
-        nc.gpsimd.memset(b_rows[0:STAGE, :], 0.0)
-        b_turned = psum.tile([P, P], F32, name="b_turned", tag="bank5")
-        nc.tensor.transpose(b_turned[:], b_rows[:], identity[:])
-        bias = keep.tile([P, N // P], F32, name="bias")
-        nc.scalar.copy(bias[:], b_turned[:, STAGE : STAGE + N // P])
-        for rows in (tab2_rows, wb_rows):
-            nc.gpsimd.memset(rows[0:STAGE, :], 0)
+        deal_scales(staged_a[:], wa_rows)
+        place(planes_a, staged_a[STAGE:, :], 2)
         tab2_win = after_a.tile([P, T], I32, name="tab2_win", offset=0, align_bytes=64)
         nc.sync.dma_start(tab2_win[:], tab2_words[0].rearrange("p t i -> p (t i)").bitcast(I32))
-        wb_both = after_a.tile([P, 2, 2, PASS], I32, name="wb_both", offset=6656, align_bytes=64)
+        wb_both = after_a.tile([P, 2, 2, PASS], I32, name="wb_both", offset=4 * T, align_bytes=64)
         wb_raw = [wb_both[:, g] for g in range(2)]
         for g in range(2):
             nc.sync.dma_start(wb_raw[g], wb_hbm[:, :, 4 * PASS * g : 4 * PASS * (g + 1)].bitcast(I32))
@@ -134,20 +125,24 @@ def tile_list_kg_sqd_mix_gelu_kernel(
             wa_raw[:].bitcast(U16).rearrange("p (g c i t) -> p g c t i", g=2, t=4, i=8),
         )
 
-        picked2 = after_b.tile([P, J // 4], I32, name="picked2", offset=4096 - 64, align_bytes=64)
-        nc.vector.tensor_copy(picked2[:].bitcast(U8), tab2_rows[:].bitcast(U8).indirect(idx2[:]))
-        deal_scales(staged_b[:, : R // 4], wb_rows[:], 2)
-        nc.vector.tensor_copy(staged_b[:, R // 4 :], picked2[:])
-        place(planes_b, staged_b[STAGE:, :])
+        held = after_b.tile([P, 3072], I32, name="held", offset=0, align_bytes=64)
+        picked2 = held[:, : J // 4]
+        nc.vector.tensor_copy(picked2.bitcast(U8), tab2_rows[:].bitcast(U8).indirect(idx2[:]))
+        deal_scales(staged[:, : PASS // 4], wb_rows[:])
+        nc.vector.tensor_copy(staged[0:64, PASS // 4 :], picked2[0:64, :])
+        place(planes_b, staged[0:64, :], 4)
 
-        en_rows = after_a.tile([32, N // 4], I32, name="en_rows", offset=5120, align_bytes=64)
+        en_rows = after_b.tile([32, N // 4], I32, name="en_rows", offset=4096, align_bytes=64)
         nc.sync.dma_start(en_rows[0:32:2, :], en8_scales[0].bitcast(I32))
         nc.sync.dma_start(en_rows[1:32:2, :], en4_scales[0].bitcast(I32))
-        en8_codes = after_b.tile([P, N], I32, name="en8_codes", offset=0, align_bytes=64)
+        en8_codes = after_b.tile([P, N], I32, name="en8_codes", offset=5120, align_bytes=64)
         nc.sync.dma_start(en8_codes[:], en8_words[0].rearrange("p n i -> p (n i)").bitcast(I32))
-        en4_codes = after_b.tile([P, N // 2], I32, name="en4_codes", offset=4096 + 128, align_bytes=64)
+        en4_codes = after_b.tile([P, N // 2], I32, name="en4_codes", offset=9216, align_bytes=64)
         nc.sync.dma_start(en4_codes[:], en4_words[0].bitcast(I32))
-        place(en_planes, en_rows)
+        place(en_planes, en_rows, 2)
+        bias = after_b.tile([P, N // P], F32, name="bias", offset=11264, align_bytes=64)
+        with nc.allow_non_contiguous_dma(reason="one bias value a partition and row tile"):
+            nc.sync.dma_start(bias[:], b.rearrange("(s p) -> p s", p=P))
 
         scale_a = planes_a[:].bitcast(U8)
         scale_b = planes_b[:].bitcast(U8)
@@ -211,8 +206,8 @@ def tile_list_kg_sqd_mix_gelu_kernel(
                 for t in range(t0, t0 + per_bank):
                     for n0 in range(0, width, P):
                         for a in range(2):
-                            w0 = a * SLOT_B + g * PASS + t * P
-                            s0 = a * SLOT_B + R + j0 + n0
+                            w0 = (2 * a + g) * SLOT + t * P
+                            s0 = 2 * a * SLOT + PASS + j0 + n0
                             nc.tensor.matmul_mx(
                                 out=hb[:, t - t0, n0 : n0 + P],
                                 lhsT=wb_t[g][:, a, t * P : (t + 1) * P].bitcast(FP8X4),

@@ -21,7 +21,7 @@ PASS = 512
 BANK = 512
 HALF = J // 2
 STAGE = 96
-SLOT = 1024
+SLOT_B = 1536
 AHEAD = 3
 CHUNKS = [(0, 128), (128, 128), (256, 128), (384, 128)]
 GROUPS = [((0, 1), (0, 1, 2, 3)), ((2,), (4, 5)), ((3,), (6, 0, 1, 7))]
@@ -44,13 +44,13 @@ def tile_list_kg_sqd_mix_gelu_kernel(
         idx2 = keep.tile([P, J // 16], U16, name="idx2")
         first = after_a.tile([P, 2 * T + PASS], I32, name="first", offset=0, align_bytes=64)
         wa_rows = first[:, : PASS // 4]
-        wb_rows = keep.tile([P, PASS // 4], I32, name="wb_rows", align_bytes=64)
+        wb_rows = keep.tile([P, R // 4], I32, name="wb_rows", align_bytes=64)
         staged_a = keep.tile([P, PASS // 4], I32, name="staged_a", align_bytes=64)
         tab_rows = keep.tile([P, T // 4], I32, name="tab_rows", align_bytes=64)
         tab2_rows = keep.tile([P, T // 4], I32, name="tab2_rows", align_bytes=64)
-        staged = keep.tile([P, SLOT // 4], I32, name="staged", align_bytes=64)
+        staged = keep.tile([P, SLOT_B // 4], I32, name="staged", align_bytes=64)
         planes_a = keep.tile([P, R // 4], I32, name="planes_a", align_bytes=64)
-        planes_b = keep.tile([P, 4 * SLOT // 4], I32, name="planes_b", align_bytes=64)
+        planes_b = keep.tile([P, 2 * SLOT_B // 4], I32, name="planes_b", align_bytes=64)
         en_planes = keep.tile([P, 2 * N // 4], I32, name="en_planes", align_bytes=64)
         warm = keep.tile([P, 2], F32, name="warm")
         tab_win = keep.tile([P, T], I32, name="tab_win", align_bytes=64)
@@ -58,10 +58,11 @@ def tile_list_kg_sqd_mix_gelu_kernel(
         sm_dealt = keep.tile([P, 2, 4], F32, name="sm_dealt")
         wb_hbm = wb_words.rearrange("a p n i -> p a (n i)")
 
+        nc.gpsimd.memset(en_planes[:], 0)
         nc.vector.memset(warm[:], 0.0)
-        nc.vector.memset(tab2_rows[:], 0)
+        nc.vector.memset(tab2_rows[0:STAGE, :], 0)
         nc.vector.memset(wa_rows[0:STAGE, :], 0)
-        nc.vector.memset(wb_rows[64:, :], 0)
+        nc.vector.memset(wb_rows[0:STAGE, :], 0)
         nc.vector.memset(planes_a[:], 0)
         nc.vector.memset(planes_b[:], 0)
         nc.scalar.activation(warm[:, 1:2], warm[:, 0:1], ACT.Sqrt)
@@ -77,13 +78,8 @@ def tile_list_kg_sqd_mix_gelu_kernel(
         nc.sync.dma_start(tab_win[:], tab_words[0].rearrange("p t i -> p (t i)").bitcast(I32))
         nc.sync.dma_start(wa_raw[:], wa_words[0].bitcast(I32))
         nc.sync.dma_start(idx2[:], offs2)
-        nc.sync.dma_start(tab2_rows[0:64:2, :], tab2_scales.rearrange("a q t -> q a t").bitcast(I32))
-        for g, queue in enumerate((nc.sync, nc.gpsimd)):
-            queue.dma_start(
-                wb_rows[g:64:2, :], wb_scales[:, :, g * PASS : (g + 1) * PASS].rearrange("a q n -> q a n").bitcast(I32)
-            )
-
-        nc.gpsimd.memset(en_planes[:], 0)
+        nc.sync.dma_start(tab2_rows[STAGE:, :], tab2_scales.rearrange("a q t -> q a t").bitcast(I32))
+        nc.sync.dma_start(wb_rows[STAGE:, :], wb_scales.rearrange("a q n -> q a n").bitcast(I32))
 
         sign = keep.tile([P, 8], BF16, name="sign")
         size = keep.tile([P, 8], F32, name="size")
@@ -100,13 +96,13 @@ def tile_list_kg_sqd_mix_gelu_kernel(
                     rows[4 * pieces * q : 4 * pieces * (q + 1), :],
                 )
 
-        def deal_scales(dst, src):
+        def deal_scales(dst, src, groups):
             nc.vector.tensor_copy(
-                dst.bitcast(U8).rearrange("p (t c i) -> p c t i", t=4, i=16),
-                src.bitcast(U8).rearrange("p (c i t) -> p c t i", t=4, i=16),
+                dst.bitcast(U8).rearrange("p (g t c i) -> p c g t i", g=groups, t=4, i=16),
+                src.bitcast(U8).rearrange("p (g c i t) -> p c g t i", g=groups, t=4, i=16),
             )
 
-        deal_scales(staged_a[:], wa_rows)
+        deal_scales(staged_a[:], wa_rows, 1)
         place(planes_a, staged_a[STAGE:, :], 2)
         tab2_win = after_a.tile([P, T], I32, name="tab2_win", offset=0, align_bytes=64)
         nc.sync.dma_start(tab2_win[:], tab2_words[0].rearrange("p t i -> p (t i)").bitcast(I32))
@@ -128,9 +124,9 @@ def tile_list_kg_sqd_mix_gelu_kernel(
         held = after_b.tile([P, 3072], I32, name="held", offset=0, align_bytes=64)
         picked2 = held[:, : J // 4]
         nc.vector.tensor_copy(picked2.bitcast(U8), tab2_rows[:].bitcast(U8).indirect(idx2[:]))
-        deal_scales(staged[:, : PASS // 4], wb_rows[:])
-        nc.vector.tensor_copy(staged[0:64, PASS // 4 :], picked2[0:64, :])
-        place(planes_b, staged[0:64, :], 4)
+        deal_scales(staged[:, : R // 4], wb_rows[:], 2)
+        nc.vector.tensor_copy(staged[STAGE:, R // 4 :], picked2[STAGE:, :])
+        place(planes_b, staged[STAGE:, :], 2)
 
         en_rows = after_b.tile([32, N // 4], I32, name="en_rows", offset=4096, align_bytes=64)
         nc.sync.dma_start(en_rows[0:32:2, :], en8_scales[0].bitcast(I32))
@@ -206,8 +202,8 @@ def tile_list_kg_sqd_mix_gelu_kernel(
                 for t in range(t0, t0 + per_bank):
                     for n0 in range(0, width, P):
                         for a in range(2):
-                            w0 = (2 * a + g) * SLOT + t * P
-                            s0 = 2 * a * SLOT + PASS + j0 + n0
+                            w0 = a * SLOT_B + g * PASS + t * P
+                            s0 = a * SLOT_B + R + j0 + n0
                             nc.tensor.matmul_mx(
                                 out=hb[:, t - t0, n0 : n0 + P],
                                 lhsT=wb_t[g][:, a, t * P : (t + 1) * P].bitcast(FP8X4),

@@ -1,6 +1,7 @@
 from contextlib import ExitStack
 
 import concourse.mybir as mybir
+from concourse.masks import make_identity
 
 K, L, R, N, T, J = 512, 1024, 1024, 1024, 1024, 512
 FLOPS = 2 * J * (K * R + L * R + R * N)
@@ -20,9 +21,11 @@ P = 128
 PASS = 512
 BANK = 512
 HALF = J // 2
+RUN = 4
 STAGE = 96
 SLOT_B = 1536
-AHEAD = 3
+AHEAD = 2
+SPANS = [(0, 1), (2,), (3,)]
 CHUNKS = [(0, 128), (128, 128), (256, 128), (384, 128)]
 GROUPS = [((0, 1), (0, 1, 2, 3)), ((2,), (4, 5)), ((3,), (6, 0, 1, 7))]
 SQUARE_ON_VECTOR = ((3, 0), (3, 1))
@@ -42,34 +45,32 @@ def tile_list_kg_sqd_mix_gelu_kernel(
 
         idx = keep.tile([P, J // 16], U16, name="idx")
         idx2 = keep.tile([P, J // 16], U16, name="idx2")
-        first = after_a.tile([P, 2 * T + PASS], I32, name="first", offset=0, align_bytes=64)
-        wa_rows = first[:, : PASS // 4]
-        wb_rows = keep.tile([P, R // 4], I32, name="wb_rows", align_bytes=64)
-        staged_a = keep.tile([P, PASS // 4], I32, name="staged_a", align_bytes=64)
         tab_rows = keep.tile([P, T // 4], I32, name="tab_rows", align_bytes=64)
-        tab2_rows = keep.tile([P, T // 4], I32, name="tab2_rows", align_bytes=64)
-        staged = keep.tile([P, SLOT_B // 4], I32, name="staged", align_bytes=64)
+        first = after_a.tile([P, 688], I32, name="first", offset=4096 - 64, align_bytes=64)
+        wa_rows = first[:, : PASS // 4]
+        staged_a = keep.tile([P, PASS // 4], I32, name="staged_a", align_bytes=64)
+        staged_b = keep.tile([P, SLOT_B // 4], I32, name="staged_b", align_bytes=64)
         planes_a = keep.tile([P, R // 4], I32, name="planes_a", align_bytes=64)
         planes_b = keep.tile([P, 2 * SLOT_B // 4], I32, name="planes_b", align_bytes=64)
         en_planes = keep.tile([P, 2 * N // 4], I32, name="en_planes", align_bytes=64)
         warm = keep.tile([P, 2], F32, name="warm")
         tab_win = keep.tile([P, T], I32, name="tab_win", align_bytes=64)
         wa_raw = keep.tile([P, R // 2], I32, name="wa_raw", align_bytes=64)
-        sm_dealt = keep.tile([P, 2, 4], F32, name="sm_dealt")
+        vectors = keep.tile([P, PASS], F32, name="vectors")
+        identity = keep.tile([P, P], F32, name="identity")
         wb_hbm = wb_words.rearrange("a p n i -> p a (n i)")
 
-        nc.gpsimd.memset(en_planes[:], 0)
         nc.vector.memset(warm[:], 0.0)
-        nc.vector.memset(tab2_rows[0:STAGE, :], 0)
+        nc.vector.memset(vectors[0:STAGE, :], 0.0)
+        make_identity(nc, identity[:])
         nc.vector.memset(wa_rows[0:STAGE, :], 0)
-        nc.vector.memset(wb_rows[0:STAGE, :], 0)
-        nc.vector.memset(planes_a[:], 0)
-        nc.vector.memset(planes_b[:], 0)
+        for planes in (planes_a, planes_b, en_planes):
+            nc.vector.memset(planes[:], 0)
         nc.scalar.activation(warm[:, 1:2], warm[:, 0:1], ACT.Sqrt)
 
         nc.sync.dma_start(wa_rows[STAGE:, :], wa_scales[0].rearrange("q (g n) -> (q g) n", g=2).bitcast(I32))
         nc.sync.dma_start(idx[:], offs)
-        nc.sync.dma_start(sm_dealt[:], sm.rearrange("(g p t) -> p g t", g=2, t=4))
+        nc.sync.dma_start(vectors[STAGE:, :PASS], sm.rearrange("(g r) -> g r", g=2).unsqueeze(0).to_broadcast([16, 2, PASS]))
         for q in (0, 2, 1, 3):
             nc.sync.dma_start(
                 tab_rows[32 * q : 32 * q + 32, :],
@@ -78,22 +79,23 @@ def tile_list_kg_sqd_mix_gelu_kernel(
         nc.sync.dma_start(tab_win[:], tab_words[0].rearrange("p t i -> p (t i)").bitcast(I32))
         nc.sync.dma_start(wa_raw[:], wa_words[0].bitcast(I32))
         nc.sync.dma_start(idx2[:], offs2)
-        nc.sync.dma_start(tab2_rows[STAGE:, :], tab2_scales.rearrange("a q t -> q a t").bitcast(I32))
-        nc.sync.dma_start(wb_rows[STAGE:, :], wb_scales.rearrange("a q n -> q a n").bitcast(I32))
 
         sign = keep.tile([P, 8], BF16, name="sign")
         size = keep.tile([P, 8], F32, name="size")
         root = keep.tile([P, 8], F32, name="root")
-        nc.scalar.activation(size[:].rearrange("p (g t) -> p g t", g=2), sm_dealt[:], ACT.Abs)
+        sm_turned = psum.tile([P, 4, P], F32, name="sm_turned", tag="bank4")
+        for t in range(4):
+            nc.tensor.transpose(sm_turned[:, t, :], vectors[:, t:PASS:4], identity[:])
+        sm_dealt = sm_turned[:, :, STAGE : STAGE + 2].rearrange("p t g -> p g t")
+        nc.scalar.activation(size[:].rearrange("p (g t) -> p g t", g=2), sm_dealt, ACT.Abs)
         nc.scalar.activation(root[:], size[:], ACT.Sqrt)
-        nc.scalar.activation(sign[:].rearrange("p (g t) -> p g t", g=2), sm_dealt[:], ACT.Sign)
+        nc.scalar.activation(sign[:].rearrange("p (g t) -> p g t", g=2), sm_dealt, ACT.Sign)
         nc.scalar.activation(warm[:, 0:1], root[:, 0:1], ACT.Gelu_apprx_tanh)
 
-        def place(planes, rows, pieces):
+        def place(planes, staged):
             for q in (0, 2, 1, 3):
                 nc.sync.dma_start(
-                    planes[32 * q : 32 * q + 4, :].rearrange("p (k n) -> p k n", k=pieces),
-                    rows[4 * pieces * q : 4 * pieces * (q + 1), :],
+                    planes[32 * q : 32 * q + 4, :].rearrange("p (k n) -> p k n", k=2), staged[8 * q : 8 * q + 8, :]
                 )
 
         def deal_scales(dst, src, groups):
@@ -103,10 +105,23 @@ def tile_list_kg_sqd_mix_gelu_kernel(
             )
 
         deal_scales(staged_a[:], wa_rows, 1)
-        place(planes_a, staged_a[STAGE:, :], 2)
+        place(planes_a, staged_a[STAGE:, :])
+        tab2_rows = after_a.tile([P, T // 4], I32, name="tab2_rows", offset=4096, align_bytes=64)
+        wb_rows = after_a.tile([P, R // 4], I32, name="wb_rows", offset=5120, align_bytes=64)
+        nc.sync.dma_start(tab2_rows[STAGE:, :], tab2_scales.rearrange("a q t -> q a t").bitcast(I32))
+        nc.sync.dma_start(wb_rows[STAGE:, :], wb_scales.rearrange("a q n -> q a n").bitcast(I32))
+        b_rows = after_a.tile([P, P], F32, name="b_rows", offset=6144, align_bytes=64)
+        nc.sync.dma_start(b_rows[STAGE:, :], b.rearrange("(s p) -> s p", p=P).unsqueeze(0).to_broadcast([4, N // P, P]))
+        nc.gpsimd.memset(b_rows[0:STAGE, :], 0.0)
+        b_turned = psum.tile([P, P], F32, name="b_turned", tag="bank5")
+        nc.tensor.transpose(b_turned[:], b_rows[:], identity[:])
+        bias = keep.tile([P, N // P], F32, name="bias")
+        nc.scalar.copy(bias[:], b_turned[:, STAGE : STAGE + N // P])
+        for rows in (tab2_rows, wb_rows):
+            nc.gpsimd.memset(rows[0:STAGE, :], 0)
         tab2_win = after_a.tile([P, T], I32, name="tab2_win", offset=0, align_bytes=64)
         nc.sync.dma_start(tab2_win[:], tab2_words[0].rearrange("p t i -> p (t i)").bitcast(I32))
-        wb_both = after_a.tile([P, 2, 2, PASS], I32, name="wb_both", offset=4 * T, align_bytes=64)
+        wb_both = after_a.tile([P, 2, 2, PASS], I32, name="wb_both", offset=6656, align_bytes=64)
         wb_raw = [wb_both[:, g] for g in range(2)]
         for g in range(2):
             nc.sync.dma_start(wb_raw[g], wb_hbm[:, :, 4 * PASS * g : 4 * PASS * (g + 1)].bitcast(I32))
@@ -121,24 +136,20 @@ def tile_list_kg_sqd_mix_gelu_kernel(
             wa_raw[:].bitcast(U16).rearrange("p (g c i t) -> p g c t i", g=2, t=4, i=8),
         )
 
-        held = after_b.tile([P, 3072], I32, name="held", offset=0, align_bytes=64)
-        picked2 = held[:, : J // 4]
-        nc.vector.tensor_copy(picked2.bitcast(U8), tab2_rows[:].bitcast(U8).indirect(idx2[:]))
-        deal_scales(staged[:, : R // 4], wb_rows[:], 2)
-        nc.vector.tensor_copy(staged[STAGE:, R // 4 :], picked2[STAGE:, :])
-        place(planes_b, staged[STAGE:, :], 2)
+        picked2 = after_b.tile([P, J // 4], I32, name="picked2", offset=4096 - 64, align_bytes=64)
+        nc.vector.tensor_copy(picked2[:].bitcast(U8), tab2_rows[:].bitcast(U8).indirect(idx2[:]))
+        deal_scales(staged_b[:, : R // 4], wb_rows[:], 2)
+        nc.vector.tensor_copy(staged_b[:, R // 4 :], picked2[:])
+        place(planes_b, staged_b[STAGE:, :])
 
-        en_rows = after_b.tile([32, N // 4], I32, name="en_rows", offset=4096, align_bytes=64)
+        en_rows = after_a.tile([32, N // 4], I32, name="en_rows", offset=5120, align_bytes=64)
         nc.sync.dma_start(en_rows[0:32:2, :], en8_scales[0].bitcast(I32))
         nc.sync.dma_start(en_rows[1:32:2, :], en4_scales[0].bitcast(I32))
-        en8_codes = after_b.tile([P, N], I32, name="en8_codes", offset=5120, align_bytes=64)
+        en8_codes = after_b.tile([P, N], I32, name="en8_codes", offset=0, align_bytes=64)
         nc.sync.dma_start(en8_codes[:], en8_words[0].rearrange("p n i -> p (n i)").bitcast(I32))
-        en4_codes = after_b.tile([P, N // 2], I32, name="en4_codes", offset=9216, align_bytes=64)
+        en4_codes = after_b.tile([P, N // 2], I32, name="en4_codes", offset=4096 + 128, align_bytes=64)
         nc.sync.dma_start(en4_codes[:], en4_words[0].bitcast(I32))
-        place(en_planes, en_rows, 2)
-        bias = after_b.tile([P, N // P], F32, name="bias", offset=11264, align_bytes=64)
-        with nc.allow_non_contiguous_dma(reason="one bias value a partition and row tile"):
-            nc.sync.dma_start(bias[:], b.rearrange("(s p) -> p s", p=P))
+        place(en_planes, en_rows)
 
         scale_a = planes_a[:].bitcast(U8)
         scale_b = planes_b[:].bitcast(U8)
@@ -217,18 +228,18 @@ def tile_list_kg_sqd_mix_gelu_kernel(
             return sums
 
         def difference(sums, j0, width, g):
-            diff = work.tile([P, 4, width], F32, name="diff")
+            diff = work.tile([P, width // RUN, 4, RUN], F32, name="diff")
             for t in range(4):
                 nc.vector.scalar_tensor_tensor(
-                    diff[:, t, :], sums[t], root[:, 4 * g + t : 4 * g + t + 1],
-                    head[g][:, t, j0 : j0 + width], ALU.mult, ALU.subtract,
+                    diff[:, :, t, :], sums[t].rearrange("p (c i) -> p c i", i=RUN), root[:, 4 * g + t : 4 * g + t + 1],
+                    head[g][:, t, j0 : j0 + width].rearrange("p (c i) -> p c i", i=RUN), ALU.mult, ALU.subtract,
                 )
             return diff
 
         def quantised(diff, width, g, on_vector):
             square = work.tile([P, width, 4], BF16, name="square", align_bytes=64)
-            woven = square[:].rearrange("p (c i) t -> p c t i", i=2)
-            planar = diff[:].rearrange("p t (c i) -> p c t i", i=2)
+            woven = square[:].rearrange("p (c i) t -> p c t i", i=RUN)
+            planar = diff
             if on_vector:
                 nc.vector.tensor_tensor(woven, planar, planar, ALU.mult)
             else:
@@ -283,18 +294,25 @@ def tile_list_kg_sqd_mix_gelu_kernel(
                     )
                 nc.sync.dma_start(out_v[:, s0 : s0 + 2, j0 : j0 + width], res[:])
 
-        units = [(c, g) for c in range(len(CHUNKS)) for g in range(2)]
-        sums = {u: project(*CHUNKS[units[u][0]], units[u][1]) for u in range(AHEAD)}
+        spans = [(chunks, g) for chunks in SPANS for g in range(2)]
+
+        def columns(chunks):
+            return CHUNKS[chunks[0]][0], len(chunks) * CHUNKS[chunks[0]][1]
+
+        sums = {u: project(*columns(spans[u][0]), spans[u][1]) for u in range(AHEAD)}
         diffs = {}
-        for step in range(len(units) + 1):
-            if step < len(units):
-                c, g = units[step]
-                diffs[step] = difference(sums[step], *CHUNKS[c], g)
-            if step + AHEAD < len(units):
-                c, g = units[step + AHEAD]
-                sums[step + AHEAD] = project(*CHUNKS[c], g)
+        for step in range(len(spans) + 1):
+            if step < len(spans):
+                chunks, g = spans[step]
+                diffs[step] = difference(sums[step], *columns(chunks), g)
+            if step + AHEAD < len(spans):
+                chunks, g = spans[step + AHEAD]
+                sums[step + AHEAD] = project(*columns(chunks), g)
             if step > 0:
-                c, g = units[step - 1]
-                score(c, g, *quantised(diffs[step - 1], CHUNKS[c][1], g, (c, g) in SQUARE_ON_VECTOR))
+                chunks, g = spans[step - 1]
+                for i, c in enumerate(chunks):
+                    width = CHUNKS[c][1]
+                    part = diffs[step - 1][:, i * width // RUN : (i + 1) * width // RUN]
+                    score(c, g, *quantised(part, width, g, (c, g) in SQUARE_ON_VECTOR))
         for chunks, banks in GROUPS:
             finish(chunks)

@@ -28,7 +28,6 @@ AHEAD = 2
 SPANS = [(0, 1), (2,), (3,)]
 CHUNKS = [(0, 128), (128, 128), (256, 128), (384, 128)]
 GROUPS = [((0, 1), (0, 1, 2, 3)), ((2,), (4, 5)), ((3,), (6, 0, 1, 7))]
-SQUARE_ON_VECTOR = ((3, 0), (3, 1))
 
 
 def tile_list_kg_sqd_mix_gelu_kernel(
@@ -40,31 +39,35 @@ def tile_list_kg_sqd_mix_gelu_kernel(
         keep = ctx.enter_context(tc.tile_pool(name="keep", bufs=1))
         after_a = ctx.enter_context(tc.tile_pool(name="after_a", bufs=1))
         after_b = ctx.enter_context(tc.tile_pool(name="after_b", bufs=1))
+        after_c = ctx.enter_context(tc.tile_pool(name="after_c", bufs=1))
         work = ctx.enter_context(tc.tile_pool(name="work", bufs=4))
         psum = ctx.enter_context(tc.psum_pool(name="psum", bufs=1))
 
         idx = keep.tile([P, J // 16], U16, name="idx")
         idx2 = keep.tile([P, J // 16], U16, name="idx2")
         tab_rows = keep.tile([P, T // 4], I32, name="tab_rows", align_bytes=64)
-        first = after_a.tile([P, 688], I32, name="first", offset=4096 - 64, align_bytes=64)
+        first = after_a.tile([P, 2208], I32, name="first", offset=4096 - 64, align_bytes=64)
         wa_rows = first[:, : PASS // 4]
+        tab2_rows = after_b.tile([P, T // 4], I32, name="tab2_rows", offset=0, align_bytes=64)[:]
         staged_a = keep.tile([P, PASS // 4], I32, name="staged_a", align_bytes=64)
-        staged_b = keep.tile([P, SLOT_B // 4], I32, name="staged_b", align_bytes=64)
         planes_a = keep.tile([P, R // 4], I32, name="planes_a", align_bytes=64)
         planes_b = keep.tile([P, 2 * SLOT_B // 4], I32, name="planes_b", align_bytes=64)
         en_planes = keep.tile([P, 2 * N // 4], I32, name="en_planes", align_bytes=64)
         warm = keep.tile([P, 2], F32, name="warm")
         tab_win = keep.tile([P, T], I32, name="tab_win", align_bytes=64)
-        wa_raw = keep.tile([P, R // 2], I32, name="wa_raw", align_bytes=64)
+        wa_raw = after_c.tile([P, R // 2], I32, name="wa_raw", offset=3072, align_bytes=64)
         vectors = keep.tile([P, PASS], F32, name="vectors")
         identity = keep.tile([P, P], F32, name="identity")
         wb_hbm = wb_words.rearrange("a p n i -> p a (n i)")
 
+        nc.gpsimd.dma_start(tab2_rows[STAGE:, :], tab2_scales.rearrange("a q t -> q a t").bitcast(I32))
         nc.vector.memset(warm[:], 0.0)
         nc.vector.memset(vectors[0:STAGE, :], 0.0)
+        nc.gpsimd.memset(en_planes[:], 0)
         make_identity(nc, identity[:])
         nc.vector.memset(wa_rows[0:STAGE, :], 0)
-        for planes in (planes_a, planes_b, en_planes):
+        nc.vector.memset(tab2_rows[0:STAGE, :], 0)
+        for planes in (planes_a, planes_b):
             nc.vector.memset(planes[:], 0)
         nc.scalar.activation(warm[:, 1:2], warm[:, 0:1], ACT.Sqrt)
 
@@ -106,22 +109,20 @@ def tile_list_kg_sqd_mix_gelu_kernel(
 
         deal_scales(staged_a[:], wa_rows, 1)
         place(planes_a, staged_a[STAGE:, :])
-        tab2_rows = after_a.tile([P, T // 4], I32, name="tab2_rows", offset=4096, align_bytes=64)
-        wb_rows = after_a.tile([P, R // 4], I32, name="wb_rows", offset=5120, align_bytes=64)
-        nc.sync.dma_start(tab2_rows[STAGE:, :], tab2_scales.rearrange("a q t -> q a t").bitcast(I32))
+        tab2_win = after_a.tile([P, T], I32, name="tab2_win", offset=0, align_bytes=64)
+        nc.sync.dma_start(tab2_win[:], tab2_words[0].rearrange("p t i -> p (t i)").bitcast(I32))
+        second = after_a.tile([P, 3328], I32, name="second", offset=12800, align_bytes=64)
+        wb_rows = second[:, : R // 4]
         nc.sync.dma_start(wb_rows[STAGE:, :], wb_scales.rearrange("a q n -> q a n").bitcast(I32))
-        b_rows = after_a.tile([P, P], F32, name="b_rows", offset=6144, align_bytes=64)
+        b_rows = after_a.tile([P, P], F32, name="b_rows", offset=4096, align_bytes=64)
         nc.sync.dma_start(b_rows[STAGE:, :], b.rearrange("(s p) -> s p", p=P).unsqueeze(0).to_broadcast([4, N // P, P]))
         nc.gpsimd.memset(b_rows[0:STAGE, :], 0.0)
         b_turned = psum.tile([P, P], F32, name="b_turned", tag="bank5")
         nc.tensor.transpose(b_turned[:], b_rows[:], identity[:])
         bias = keep.tile([P, N // P], F32, name="bias")
         nc.scalar.copy(bias[:], b_turned[:, STAGE : STAGE + N // P])
-        for rows in (tab2_rows, wb_rows):
-            nc.gpsimd.memset(rows[0:STAGE, :], 0)
-        tab2_win = after_a.tile([P, T], I32, name="tab2_win", offset=0, align_bytes=64)
-        nc.sync.dma_start(tab2_win[:], tab2_words[0].rearrange("p t i -> p (t i)").bitcast(I32))
-        wb_both = after_a.tile([P, 2, 2, PASS], I32, name="wb_both", offset=6656, align_bytes=64)
+        nc.gpsimd.memset(wb_rows[0:STAGE, :], 0)
+        wb_both = after_a.tile([P, 2, 2, PASS], I32, name="wb_both", offset=4608, align_bytes=64)
         wb_raw = [wb_both[:, g] for g in range(2)]
         for g in range(2):
             nc.sync.dma_start(wb_raw[g], wb_hbm[:, :, 4 * PASS * g : 4 * PASS * (g + 1)].bitcast(I32))
@@ -130,24 +131,31 @@ def tile_list_kg_sqd_mix_gelu_kernel(
         nc.vector.tensor_copy(tab_plane[:], tab_rows[:].bitcast(U8).indirect(idx[:]))
         tab_codes = keep.tile([P, J], U32, name="tab_codes", align_bytes=64)
         nc.vector.tensor_copy(tab_codes[:], tab_win[:].bitcast(U32).indirect(idx[:]))
-        wa_t = keep.tile([P, R], U16, name="wa_t", align_bytes=64)
-        nc.vector.tensor_copy(
-            wa_t[:].rearrange("p (g t c i) -> p g c t i", g=2, t=4, i=8),
-            wa_raw[:].bitcast(U16).rearrange("p (g c i t) -> p g c t i", g=2, t=4, i=8),
-        )
 
-        picked2 = after_b.tile([P, J // 4], I32, name="picked2", offset=4096 - 64, align_bytes=64)
-        nc.vector.tensor_copy(picked2[:].bitcast(U8), tab2_rows[:].bitcast(U8).indirect(idx2[:]))
-        deal_scales(staged_b[:, : R // 4], wb_rows[:], 2)
-        nc.vector.tensor_copy(staged_b[:, R // 4 :], picked2[:])
+        def deal_wa(dst, g):
+            nc.vector.tensor_copy(
+                dst[:].rearrange("p (t c i) -> p c t i", t=4, i=8),
+                wa_raw[:].bitcast(U16)[:, g * PASS : (g + 1) * PASS].rearrange("p (c i t) -> p c t i", t=4, i=8),
+            )
+
+        wa_t = [keep.tile([P, PASS], U16, name="wa_first", align_bytes=64)]
+        deal_wa(wa_t[0], 0)
+
+        picked2 = keep.tile([P, J // 4], I32, name="picked2", align_bytes=64)[:]
+        nc.vector.tensor_copy(picked2.bitcast(U8), tab2_rows.bitcast(U8).indirect(idx2[:]))
+        staged_b = after_b.tile([P, SLOT_B // 4], I32, name="staged_b", offset=0, align_bytes=64)
+        deal_scales(staged_b[:, : R // 4], wb_rows, 2)
+        nc.vector.tensor_copy(staged_b[:, R // 4 :], picked2)
         place(planes_b, staged_b[STAGE:, :])
+        wa_t.append(after_a.tile([P, PASS], U16, name="wa_second", offset=24064, align_bytes=64))
+        deal_wa(wa_t[1], 1)
 
-        en_rows = after_a.tile([32, N // 4], I32, name="en_rows", offset=5120, align_bytes=64)
+        en_rows = after_a.tile([32, N // 4], I32, name="en_rows", offset=25088, align_bytes=64)
         nc.sync.dma_start(en_rows[0:32:2, :], en8_scales[0].bitcast(I32))
         nc.sync.dma_start(en_rows[1:32:2, :], en4_scales[0].bitcast(I32))
-        en8_codes = after_b.tile([P, N], I32, name="en8_codes", offset=0, align_bytes=64)
+        en8_codes = after_c.tile([P, N], I32, name="en8_codes", offset=0, align_bytes=64)
         nc.sync.dma_start(en8_codes[:], en8_words[0].rearrange("p n i -> p (n i)").bitcast(I32))
-        en4_codes = after_b.tile([P, N // 2], I32, name="en4_codes", offset=4096 + 128, align_bytes=64)
+        en4_codes = after_c.tile([P, N // 2], I32, name="en4_codes", offset=4096, align_bytes=64)
         nc.sync.dma_start(en4_codes[:], en4_words[0].bitcast(I32))
         place(en_planes, en_rows)
 
@@ -164,7 +172,7 @@ def tile_list_kg_sqd_mix_gelu_kernel(
                 s0 = g * PASS + t * P
                 nc.tensor.matmul_mx(
                     out=ha[:],
-                    lhsT=wa_t[:, s0 : s0 + P].bitcast(FP4X4),
+                    lhsT=wa_t[g][:, t * P : (t + 1) * P].bitcast(FP4X4),
                     lhsT_scale=scale_a[:, s0 : s0 + P],
                     rhs=tab_codes[:].bitcast(FP8X4),
                     rhs_scale=tab_plane[:],
@@ -179,7 +187,7 @@ def tile_list_kg_sqd_mix_gelu_kernel(
 
         def gather_tab2(part):
             cols = slice(part * HALF // 16, (part + 1) * HALF // 16)
-            pairs = keep.tile([P, HALF], U32, name=f"tab2_pairs{part}", align_bytes=64)
+            pairs = after_a.tile([P, HALF], U32, name=f"tab2_pairs{part}", offset=13824 + 1024 * part, align_bytes=64)
             nc.vector.tensor_copy(pairs[:], tab2_win[:].bitcast(U32).indirect(idx2[:, cols]))
             parted = keep.tile([P, 2, HALF], U16, name=f"tab2_codes{part}", align_bytes=64)
             nc.vector.tensor_copy(
@@ -189,7 +197,7 @@ def tile_list_kg_sqd_mix_gelu_kernel(
             tab2_codes.append(parted)
 
         def reorder_wb(g):
-            dealt = keep.tile([P, 2, PASS], I32, name=f"wb_t{g}", align_bytes=64)
+            dealt = after_a.tile([P, 2, PASS], I32, name=f"wb_t{g}", offset=15872 + 4096 * g, align_bytes=64)
             nc.vector.tensor_copy(
                 dealt[:].rearrange("p a (t c i) -> p a c t i", t=4, i=4),
                 wb_raw[g].rearrange("p a (c i t) -> p a c t i", t=4, i=4),
@@ -199,7 +207,6 @@ def tile_list_kg_sqd_mix_gelu_kernel(
         gather_tab2(0)
         reorder_wb(0)
         reorder_wb(1)
-        gather_tab2(1)
 
         ring = []
 
@@ -228,26 +235,32 @@ def tile_list_kg_sqd_mix_gelu_kernel(
             return sums
 
         def difference(sums, j0, width, g):
-            diff = work.tile([P, width // RUN, 4, RUN], F32, name="diff")
+            diff = work.tile([P, 4, width], F32, name="diff")
             for t in range(4):
                 nc.vector.scalar_tensor_tensor(
-                    diff[:, :, t, :], sums[t].rearrange("p (c i) -> p c i", i=RUN), root[:, 4 * g + t : 4 * g + t + 1],
-                    head[g][:, t, j0 : j0 + width].rearrange("p (c i) -> p c i", i=RUN), ALU.mult, ALU.subtract,
+                    diff[:, t, :], sums[t], root[:, 4 * g + t : 4 * g + t + 1],
+                    head[g][:, t, j0 : j0 + width], ALU.mult, ALU.subtract,
                 )
             return diff
 
-        def quantised(diff, width, g, on_vector):
+        def squared(diff, width, on_vector):
             square = work.tile([P, width, 4], BF16, name="square", align_bytes=64)
-            woven = square[:].rearrange("p (c i) t -> p c t i", i=RUN)
-            planar = diff
+            woven = square[:].rearrange("p (c i) t -> p c t i", i=2)
+            planar = diff.rearrange("p t (c i) -> p c t i", i=2)
             if on_vector:
                 nc.vector.tensor_tensor(woven, planar, planar, ALU.mult)
             else:
                 nc.scalar.activation(woven, planar, ACT.Square)
+            return square
+
+        def signed(square, width, g):
             h = work.tile([P, width, 4], BF16, name="h", align_bytes=64)
             nc.vector.tensor_tensor(
                 h[:], square[:], sign[:, 4 * g : 4 * g + 4].unsqueeze(1).to_broadcast([P, width, 4]), ALU.mult
             )
+            return h
+
+        def quantised(h, width):
             codes = work.tile([P, width], U32, name="h_codes", align_bytes=64)
             scales = work.tile([P, width], U8, name="h_scales", align_bytes=64)
             nc.vector.quantize_mx(out=codes[:].bitcast(FP8X4), scales=scales[:], in_=h[:].rearrange("p j t -> p (j t)"))
@@ -256,16 +269,16 @@ def tile_list_kg_sqd_mix_gelu_kernel(
         group_of = {c: (chunks, banks) for chunks, banks in GROUPS for c in chunks}
         sums_of = {}
 
-        def score(c, g, codes, scales):
+        def score(c, g, codes, scales, tiles):
             chunks, banks = group_of[c]
             width = CHUNKS[c][1]
             per_bank = N // P // len(banks)
-            if c == chunks[0] and g == 0:
+            if chunks not in sums_of:
                 sums_of[chunks] = [
                     psum.tile([P, per_bank, len(chunks) * width], F32, name="y", tag=f"bank{bank}") for bank in banks
                 ]
             c0 = (c - chunks[0]) * width
-            for s in range(N // P):
+            for s in tiles:
                 n0 = s * P
                 if g == 0:
                     lhs = en8_codes[:, n0 : n0 + P].bitcast(FP8X4)
@@ -301,18 +314,27 @@ def tile_list_kg_sqd_mix_gelu_kernel(
 
         sums = {u: project(*columns(spans[u][0]), spans[u][1]) for u in range(AHEAD)}
         diffs = {}
-        for step in range(len(spans) + 1):
-            if step < len(spans):
-                chunks, g = spans[step]
-                diffs[step] = difference(sums[step], *columns(chunks), g)
+        for step in range(len(spans)):
+            chunks, g = spans[step]
+            diffs[step] = difference(sums[step], *columns(chunks), g)
+            if step == 0:
+                gather_tab2(1)
             if step + AHEAD < len(spans):
                 chunks, g = spans[step + AHEAD]
                 sums[step + AHEAD] = project(*columns(chunks), g)
-            if step > 0:
+            if 0 < step < len(spans) - 1:
                 chunks, g = spans[step - 1]
                 for i, c in enumerate(chunks):
                     width = CHUNKS[c][1]
-                    part = diffs[step - 1][:, i * width // RUN : (i + 1) * width // RUN]
-                    score(c, g, *quantised(part, width, g, (c, g) in SQUARE_ON_VECTOR))
+                    square = squared(diffs[step - 1][:, :, i * width : (i + 1) * width], width, False)
+                    score(c, g, *quantised(signed(square, width, g), width), range(N // P))
+        last = len(CHUNKS) - 1
+        width = CHUNKS[last][1]
+        squares = [squared(diffs[len(spans) - 2 + g][:], width, True) for g in range(2)]
+        values = [signed(squares[g], width, g) for g in range(2)]
+        packed = [quantised(values[g], width) for g in range(2)]
+        for s0 in range(0, N // P, 2):
+            for g in range(2):
+                score(last, g, *packed[g], range(s0, s0 + 2))
         for chunks, banks in GROUPS:
             finish(chunks)

@@ -23,7 +23,7 @@ BANK = 512
 HALF = J // 2
 RUN = 4
 STAGE = 96
-SLOT_B = 1536
+SLOT = 1024
 AHEAD = 2
 SPANS = [(0, 1), (2,), (3,)]
 CHUNKS = [(0, 128), (128, 128), (256, 128), (384, 128)]
@@ -38,7 +38,6 @@ def tile_list_kg_sqd_mix_gelu_kernel(
     with ExitStack() as ctx:
         keep = ctx.enter_context(tc.tile_pool(name="keep", bufs=1))
         after_a = ctx.enter_context(tc.tile_pool(name="after_a", bufs=1))
-        after_b = ctx.enter_context(tc.tile_pool(name="after_b", bufs=1))
         after_c = ctx.enter_context(tc.tile_pool(name="after_c", bufs=1))
         work = ctx.enter_context(tc.tile_pool(name="work", bufs=4))
         psum = ctx.enter_context(tc.psum_pool(name="psum", bufs=1))
@@ -47,81 +46,69 @@ def tile_list_kg_sqd_mix_gelu_kernel(
         idx2 = keep.tile([P, J // 16], U16, name="idx2")
         tab_rows = keep.tile([P, T // 4], I32, name="tab_rows", align_bytes=64)
         first = after_a.tile([P, 2208], I32, name="first", offset=4096 - 64, align_bytes=64)
-        wa_rows = first[:, : PASS // 4]
-        tab2_rows = after_b.tile([P, T // 4], I32, name="tab2_rows", offset=0, align_bytes=64)[:]
-        staged_a = keep.tile([P, PASS // 4], I32, name="staged_a", align_bytes=64)
+        weight_rows = first[:, : PASS // 4]
+        tab2_rows = keep.tile([P, T // 4], I32, name="tab2_rows", align_bytes=64)
+        staged = keep.tile([P, SLOT // 4], I32, name="staged", align_bytes=64)
+        b_rows = keep.tile([P, P], F32, name="b_rows")
         planes_a = keep.tile([P, R // 4], I32, name="planes_a", align_bytes=64)
-        planes_b = keep.tile([P, 2 * SLOT_B // 4], I32, name="planes_b", align_bytes=64)
+        planes_b = keep.tile([P, SLOT], I32, name="planes_b", align_bytes=64)
         en_planes = keep.tile([P, 2 * N // 4], I32, name="en_planes", align_bytes=64)
         warm = keep.tile([P, 2], F32, name="warm")
         tab_win = keep.tile([P, T], I32, name="tab_win", align_bytes=64)
         wa_raw = after_c.tile([P, R // 2], I32, name="wa_raw", offset=3072, align_bytes=64)
-        vectors = keep.tile([P, PASS], F32, name="vectors")
+        sm_dealt = keep.tile([P, 2, 4], F32, name="sm_dealt")
         identity = keep.tile([P, P], F32, name="identity")
         wb_hbm = wb_words.rearrange("a p n i -> p a (n i)")
 
-        nc.gpsimd.dma_start(tab2_rows[STAGE:, :], tab2_scales.rearrange("a q t -> q a t").bitcast(I32))
+        nc.gpsimd.dma_start(b_rows[STAGE:, :], b.rearrange("(s p) -> s p", p=P).unsqueeze(0).to_broadcast([4, N // P, P]))
+        nc.vector.memset(tab2_rows[:], 0)
         nc.vector.memset(warm[:], 0.0)
-        nc.vector.memset(vectors[0:STAGE, :], 0.0)
-        nc.gpsimd.memset(en_planes[:], 0)
         make_identity(nc, identity[:])
-        nc.vector.memset(wa_rows[0:STAGE, :], 0)
-        nc.vector.memset(tab2_rows[0:STAGE, :], 0)
-        for planes in (planes_a, planes_b):
-            nc.vector.memset(planes[:], 0)
+        nc.gpsimd.memset(b_rows[0:STAGE, :], 0.0)
+        nc.gpsimd.memset(en_planes[:], 0)
+        nc.vector.memset(planes_a[:], 0)
+        nc.vector.memset(planes_b[:].rearrange("p (g n) -> p g n", g=2)[:, :, : (SLOT + PASS) // 4], 0)
         nc.scalar.activation(warm[:, 1:2], warm[:, 0:1], ACT.Sqrt)
 
-        nc.sync.dma_start(wa_rows[STAGE:, :], wa_scales[0].rearrange("q (g n) -> (q g) n", g=2).bitcast(I32))
+        wa_halves = wa_scales[0].rearrange("q (g n) -> (q g) n", g=2).bitcast(I32)
+        nc.sync.dma_start(weight_rows[0::2, :], wa_halves.unsqueeze(1).to_broadcast([32, 2, PASS // 4]))
+        nc.sync.dma_start(weight_rows[1::2, :], wb_scales.rearrange("a q (g n) -> (q g) a n", g=2).bitcast(I32))
         nc.sync.dma_start(idx[:], offs)
-        nc.sync.dma_start(vectors[STAGE:, :PASS], sm.rearrange("(g r) -> g r", g=2).unsqueeze(0).to_broadcast([16, 2, PASS]))
         for q in (0, 2, 1, 3):
             nc.sync.dma_start(
                 tab_rows[32 * q : 32 * q + 32, :],
                 tab_scales[0, 4 * q : 4 * q + 4, :].bitcast(I32).unsqueeze(0).to_broadcast([8, 4, T // 4]),
             )
         nc.sync.dma_start(tab_win[:], tab_words[0].rearrange("p t i -> p (t i)").bitcast(I32))
+        nc.sync.dma_start(sm_dealt[:], sm.rearrange("(g p t) -> p g t", g=2, t=4))
         nc.sync.dma_start(wa_raw[:], wa_words[0].bitcast(I32))
         nc.sync.dma_start(idx2[:], offs2)
+        nc.sync.dma_start(tab2_rows[1::4, :], tab2_scales.rearrange("a q t -> q a t").bitcast(I32))
 
         sign = keep.tile([P, 8], BF16, name="sign")
         size = keep.tile([P, 8], F32, name="size")
         root = keep.tile([P, 8], F32, name="root")
-        sm_turned = psum.tile([P, 4, P], F32, name="sm_turned", tag="bank4")
-        for t in range(4):
-            nc.tensor.transpose(sm_turned[:, t, :], vectors[:, t:PASS:4], identity[:])
-        sm_dealt = sm_turned[:, :, STAGE : STAGE + 2].rearrange("p t g -> p g t")
-        nc.scalar.activation(size[:].rearrange("p (g t) -> p g t", g=2), sm_dealt, ACT.Abs)
+        nc.scalar.activation(size[:].rearrange("p (g t) -> p g t", g=2), sm_dealt[:], ACT.Abs)
         nc.scalar.activation(root[:], size[:], ACT.Sqrt)
-        nc.scalar.activation(sign[:].rearrange("p (g t) -> p g t", g=2), sm_dealt, ACT.Sign)
+        nc.scalar.activation(sign[:].rearrange("p (g t) -> p g t", g=2), sm_dealt[:], ACT.Sign)
         nc.scalar.activation(warm[:, 0:1], root[:, 0:1], ACT.Gelu_apprx_tanh)
 
-        def place(planes, staged):
+        def place(planes, rows, pieces):
             for q in (0, 2, 1, 3):
-                nc.sync.dma_start(
-                    planes[32 * q : 32 * q + 4, :].rearrange("p (k n) -> p k n", k=2), staged[8 * q : 8 * q + 8, :]
-                )
+                nc.sync.dma_start(planes[32 * q : 32 * q + 4, :].rearrange("p (k n) -> p k n", k=pieces), rows(q))
 
-        def deal_scales(dst, src, groups):
-            nc.vector.tensor_copy(
-                dst.bitcast(U8).rearrange("p (g t c i) -> p c g t i", g=groups, t=4, i=16),
-                src.bitcast(U8).rearrange("p (g c i t) -> p c g t i", g=groups, t=4, i=16),
-            )
-
-        deal_scales(staged_a[:], wa_rows, 1)
-        place(planes_a, staged_a[STAGE:, :])
-        tab2_win = after_a.tile([P, T], I32, name="tab2_win", offset=0, align_bytes=64)
-        nc.sync.dma_start(tab2_win[:], tab2_words[0].rearrange("p t i -> p (t i)").bitcast(I32))
-        second = after_a.tile([P, 3328], I32, name="second", offset=12800, align_bytes=64)
-        wb_rows = second[:, : R // 4]
-        nc.sync.dma_start(wb_rows[STAGE:, :], wb_scales.rearrange("a q n -> q a n").bitcast(I32))
-        b_rows = after_a.tile([P, P], F32, name="b_rows", offset=4096, align_bytes=64)
-        nc.sync.dma_start(b_rows[STAGE:, :], b.rearrange("(s p) -> s p", p=P).unsqueeze(0).to_broadcast([4, N // P, P]))
-        nc.gpsimd.memset(b_rows[0:STAGE, :], 0.0)
         b_turned = psum.tile([P, P], F32, name="b_turned", tag="bank5")
         nc.tensor.transpose(b_turned[:], b_rows[:], identity[:])
         bias = keep.tile([P, N // P], F32, name="bias")
         nc.scalar.copy(bias[:], b_turned[:, STAGE : STAGE + N // P])
-        nc.gpsimd.memset(wb_rows[0:STAGE, :], 0)
+
+        nc.vector.tensor_copy(
+            staged[:, : PASS // 4].bitcast(U8).rearrange("p (t c i) -> p c t i", t=4, i=16),
+            weight_rows.bitcast(U8).rearrange("p (c i t) -> p c t i", t=4, i=16),
+        )
+        place(planes_a, lambda q: staged[32 * q : 32 * q + 32 : 4, : PASS // 4], 2)
+        tab2_win = after_a.tile([P, T], I32, name="tab2_win", offset=0, align_bytes=64)
+        nc.sync.dma_start(tab2_win[:], tab2_words[0].rearrange("p t i -> p (t i)").bitcast(I32))
         wb_both = after_a.tile([P, 2, 2, PASS], I32, name="wb_both", offset=4608, align_bytes=64)
         wb_raw = [wb_both[:, g] for g in range(2)]
         for g in range(2):
@@ -141,12 +128,11 @@ def tile_list_kg_sqd_mix_gelu_kernel(
         wa_t = [keep.tile([P, PASS], U16, name="wa_first", align_bytes=64)]
         deal_wa(wa_t[0], 0)
 
-        picked2 = keep.tile([P, J // 4], I32, name="picked2", align_bytes=64)[:]
-        nc.vector.tensor_copy(picked2.bitcast(U8), tab2_rows.bitcast(U8).indirect(idx2[:]))
-        staged_b = after_b.tile([P, SLOT_B // 4], I32, name="staged_b", offset=0, align_bytes=64)
-        deal_scales(staged_b[:, : R // 4], wb_rows, 2)
-        nc.vector.tensor_copy(staged_b[:, R // 4 :], picked2)
-        place(planes_b, staged_b[STAGE:, :])
+        second = after_a.tile([P, 3328], I32, name="second", offset=12800, align_bytes=64)
+        picked2 = second[:, : J // 4]
+        nc.vector.tensor_copy(picked2.bitcast(U8), tab2_rows[:].bitcast(U8).indirect(idx2[:]))
+        nc.vector.tensor_copy(staged[:, PASS // 4 :], picked2)
+        place(planes_b, lambda q: staged[32 * q + 1 : 32 * q + 32 : 2, :], 4)
         wa_t.append(after_a.tile([P, PASS], U16, name="wa_second", offset=24064, align_bytes=64))
         deal_wa(wa_t[1], 1)
 
@@ -157,7 +143,7 @@ def tile_list_kg_sqd_mix_gelu_kernel(
         nc.sync.dma_start(en8_codes[:], en8_words[0].rearrange("p n i -> p (n i)").bitcast(I32))
         en4_codes = after_c.tile([P, N // 2], I32, name="en4_codes", offset=4096, align_bytes=64)
         nc.sync.dma_start(en4_codes[:], en4_words[0].bitcast(I32))
-        place(en_planes, en_rows)
+        place(en_planes, lambda q: en_rows[8 * q : 8 * q + 8, :], 2)
 
         scale_a = planes_a[:].bitcast(U8)
         scale_b = planes_b[:].bitcast(U8)
@@ -220,8 +206,8 @@ def tile_list_kg_sqd_mix_gelu_kernel(
                 for t in range(t0, t0 + per_bank):
                     for n0 in range(0, width, P):
                         for a in range(2):
-                            w0 = a * SLOT_B + g * PASS + t * P
-                            s0 = a * SLOT_B + R + j0 + n0
+                            w0 = (2 * g + a) * SLOT + t * P
+                            s0 = 2 * a * SLOT + PASS + j0 + n0
                             nc.tensor.matmul_mx(
                                 out=hb[:, t - t0, n0 : n0 + P],
                                 lhsT=wb_t[g][:, a, t * P : (t + 1) * P].bitcast(FP8X4),
@@ -294,18 +280,18 @@ def tile_list_kg_sqd_mix_gelu_kernel(
                     stop=(c == chunks[-1] and g == 1 and s % per_bank == per_bank - 1),
                 )
 
-        def finish(chunks):
+        def finish(chunks, pieces):
             j0 = CHUNKS[chunks[0]][0]
             width = len(chunks) * CHUNKS[chunks[0]][1]
             banks = sums_of[chunks]
             per_bank = N // P // len(banks)
-            for s0 in range(0, N // P, 2):
-                res = work.tile([P, 2, width], F32, name="res", bufs=8)
-                for s in range(s0, s0 + 2):
+            for s0, rows in pieces:
+                res = work.tile([P, rows, width], F32, name="res", bufs=12)
+                for s in range(s0, s0 + rows):
                     nc.scalar.activation(
                         res[:, s - s0, :], banks[s // per_bank][:, s % per_bank, :], ACT.Gelu_apprx_tanh, bias=bias[:, s : s + 1]
                     )
-                nc.sync.dma_start(out_v[:, s0 : s0 + 2, j0 : j0 + width], res[:])
+                nc.sync.dma_start(out_v[:, s0 : s0 + rows, j0 : j0 + width], res[:])
 
         spans = [(chunks, g) for chunks in SPANS for g in range(2)]
 
@@ -337,4 +323,7 @@ def tile_list_kg_sqd_mix_gelu_kernel(
             for g in range(2):
                 score(last, g, *packed[g], range(s0, s0 + 2))
         for chunks, banks in GROUPS:
-            finish(chunks)
+            pieces = [(s0, 2) for s0 in range(0, N // P, 2)]
+            if last in chunks:
+                pieces[-1:] = [(N // P - 2, 1), (N // P - 1, 1)]
+            finish(chunks, pieces)

@@ -23,7 +23,6 @@ BANK = 512
 HALF = J // 2
 RUN = 4
 STAGE = 96
-SLOT = 1024
 AHEAD = 2
 SPANS = [(0, 1), (2,), (3,)]
 CHUNKS = [(0, 128), (128, 128), (256, 128), (384, 128)]
@@ -45,13 +44,14 @@ def tile_list_kg_sqd_mix_gelu_kernel(
         idx = keep.tile([P, J // 16], U16, name="idx")
         idx2 = keep.tile([P, J // 16], U16, name="idx2")
         tab_rows = keep.tile([P, T // 4], I32, name="tab_rows", align_bytes=64)
-        first = after_a.tile([P, 2208], I32, name="first", offset=4096 - 64, align_bytes=64)
+        first = after_a.tile([P, 2192], I32, name="first", offset=4096 - 64, align_bytes=64)
         weight_rows = first[:, : PASS // 4]
-        tab2_rows = keep.tile([P, T // 4], I32, name="tab2_rows", align_bytes=64)
-        staged = keep.tile([P, SLOT // 4], I32, name="staged", align_bytes=64)
+        second = after_a.tile([P, 3328], I32, name="second", offset=12800, align_bytes=64)
+        tab2_rows = second[:, : T // 4]
+        staged = keep.tile([P, PASS // 4], I32, name="staged", align_bytes=64)
         b_rows = keep.tile([P, P], F32, name="b_rows")
-        planes_a = keep.tile([P, R // 4], I32, name="planes_a", align_bytes=64)
-        planes_b = keep.tile([P, SLOT], I32, name="planes_b", align_bytes=64)
+        planes_a = keep.tile([P, 2, 4, PASS // 4], I32, name="planes_a", align_bytes=64)
+        planes_b = keep.tile([P, 2 * J // 4], I32, name="planes_b", align_bytes=64)
         en_planes = keep.tile([P, 2 * N // 4], I32, name="en_planes", align_bytes=64)
         warm = keep.tile([P, 2], F32, name="warm")
         tab_win = keep.tile([P, T], I32, name="tab_win", align_bytes=64)
@@ -61,13 +61,13 @@ def tile_list_kg_sqd_mix_gelu_kernel(
         wb_hbm = wb_words.rearrange("a p n i -> p a (n i)")
 
         nc.gpsimd.dma_start(b_rows[STAGE:, :], b.rearrange("(s p) -> s p", p=P).unsqueeze(0).to_broadcast([4, N // P, P]))
-        nc.vector.memset(tab2_rows[:], 0)
+        nc.vector.memset(tab2_rows, 0)
         nc.vector.memset(warm[:], 0.0)
         make_identity(nc, identity[:])
-        nc.gpsimd.memset(b_rows[0:STAGE, :], 0.0)
-        nc.gpsimd.memset(en_planes[:], 0)
-        nc.vector.memset(planes_a[:], 0)
-        nc.vector.memset(planes_b[:].rearrange("p (g n) -> p g n", g=2)[:, :, : (SLOT + PASS) // 4], 0)
+        nc.vector.memset(planes_a[:, :, 1:, :], 0)
+        nc.vector.memset(b_rows[0:STAGE, :], 0.0)
+        nc.vector.memset(planes_b[:], 0)
+        nc.vector.memset(en_planes[:], 0)
         nc.scalar.activation(warm[:, 1:2], warm[:, 0:1], ACT.Sqrt)
 
         wa_halves = wa_scales[0].rearrange("q (g n) -> (q g) n", g=2).bitcast(I32)
@@ -95,7 +95,7 @@ def tile_list_kg_sqd_mix_gelu_kernel(
 
         def place(planes, rows, pieces):
             for q in (0, 2, 1, 3):
-                nc.sync.dma_start(planes[32 * q : 32 * q + 4, :].rearrange("p (k n) -> p k n", k=pieces), rows(q))
+                nc.sync.dma_start(planes[32 * q : 32 * q + 4].rearrange("p (k n) -> p k n", k=pieces), rows(q))
 
         b_turned = psum.tile([P, P], F32, name="b_turned", tag="bank5")
         nc.tensor.transpose(b_turned[:], b_rows[:], identity[:])
@@ -103,10 +103,10 @@ def tile_list_kg_sqd_mix_gelu_kernel(
         nc.scalar.copy(bias[:], b_turned[:, STAGE : STAGE + N // P])
 
         nc.vector.tensor_copy(
-            staged[:, : PASS // 4].bitcast(U8).rearrange("p (t c i) -> p c t i", t=4, i=16),
+            staged[:].bitcast(U8).rearrange("p (t c i) -> p c t i", t=4, i=16),
             weight_rows.bitcast(U8).rearrange("p (c i t) -> p c t i", t=4, i=16),
         )
-        place(planes_a, lambda q: staged[32 * q : 32 * q + 32 : 4, : PASS // 4], 2)
+        place(planes_a[:].rearrange("p g k n -> p (g k n)"), lambda q: staged[32 * q : 32 * q + 32, :], 8)
         tab2_win = after_a.tile([P, T], I32, name="tab2_win", offset=0, align_bytes=64)
         nc.sync.dma_start(tab2_win[:], tab2_words[0].rearrange("p t i -> p (t i)").bitcast(I32))
         wb_both = after_a.tile([P, 2, 2, PASS], I32, name="wb_both", offset=4608, align_bytes=64)
@@ -128,11 +128,9 @@ def tile_list_kg_sqd_mix_gelu_kernel(
         wa_t = [keep.tile([P, PASS], U16, name="wa_first", align_bytes=64)]
         deal_wa(wa_t[0], 0)
 
-        second = after_a.tile([P, 3328], I32, name="second", offset=12800, align_bytes=64)
-        picked2 = second[:, : J // 4]
-        nc.vector.tensor_copy(picked2.bitcast(U8), tab2_rows[:].bitcast(U8).indirect(idx2[:]))
-        nc.vector.tensor_copy(staged[:, PASS // 4 :], picked2)
-        place(planes_b, lambda q: staged[32 * q + 1 : 32 * q + 32 : 2, :], 4)
+        picked2 = keep.tile([P, J // 4], I32, name="picked2", align_bytes=64)
+        nc.vector.tensor_copy(picked2[:].bitcast(U8), tab2_rows.bitcast(U8).indirect(idx2[:]))
+        place(planes_b, lambda q: picked2[32 * q + 1 : 32 * q + 32 : 4, :], 2)
         wa_t.append(after_a.tile([P, PASS], U16, name="wa_second", offset=24064, align_bytes=64))
         deal_wa(wa_t[1], 1)
 
@@ -145,7 +143,7 @@ def tile_list_kg_sqd_mix_gelu_kernel(
         nc.sync.dma_start(en4_codes[:], en4_words[0].bitcast(I32))
         place(en_planes, lambda q: en_rows[8 * q : 8 * q + 8, :], 2)
 
-        scale_a = planes_a[:].bitcast(U8)
+        scale_a = planes_a[:].rearrange("p g k n -> p (g k n)").bitcast(U8)
         scale_b = planes_b[:].bitcast(U8)
         en_scale = en_planes[:].bitcast(U8)
         out_v = out.rearrange("(s p) j -> p s j", p=P)
@@ -155,7 +153,7 @@ def tile_list_kg_sqd_mix_gelu_kernel(
             rows = keep.tile([P, 4, J], F32, name=f"head{g}")
             for t in range(4):
                 ha = psum.tile([P, BANK], F32, name="ha", tag=f"bank{t}")
-                s0 = g * PASS + t * P
+                s0 = (4 * g + 2) * PASS + t * P
                 nc.tensor.matmul_mx(
                     out=ha[:],
                     lhsT=wa_t[g][:, t * P : (t + 1) * P].bitcast(FP4X4),
@@ -206,12 +204,12 @@ def tile_list_kg_sqd_mix_gelu_kernel(
                 for t in range(t0, t0 + per_bank):
                     for n0 in range(0, width, P):
                         for a in range(2):
-                            w0 = (2 * g + a) * SLOT + t * P
-                            s0 = 2 * a * SLOT + PASS + j0 + n0
+                            w0 = (4 * g + 2 * a + 1) * PASS + t * P
+                            s0 = a * J + j0 + n0
                             nc.tensor.matmul_mx(
                                 out=hb[:, t - t0, n0 : n0 + P],
                                 lhsT=wb_t[g][:, a, t * P : (t + 1) * P].bitcast(FP8X4),
-                                lhsT_scale=scale_b[:, w0 : w0 + P],
+                                lhsT_scale=scale_a[:, w0 : w0 + P],
                                 rhs=tab2_codes[part][:, a, c0 + n0 : c0 + n0 + P].bitcast(FP4X4),
                                 rhs_scale=scale_b[:, s0 : s0 + P],
                                 start=(a == 0),

@@ -21,8 +21,6 @@ P = 128
 PASS = 512
 BANK = 512
 HALF = J // 2
-RUN = 4
-STAGE = 96
 AHEAD = 2
 SPANS = [(0, 1), (2,), (3,)]
 CHUNKS = [(0, 128), (128, 128), (256, 128), (384, 128)]
@@ -49,7 +47,6 @@ def tile_list_kg_sqd_mix_gelu_kernel(
         second = after_a.tile([P, 3328], I32, name="second", offset=12800, align_bytes=64)
         tab2_rows = second[:, : T // 4]
         staged = keep.tile([P, PASS // 4], I32, name="staged", align_bytes=64)
-        b_rows = keep.tile([P, P], F32, name="b_rows")
         planes_a = keep.tile([P, 2, 4, PASS // 4], I32, name="planes_a", align_bytes=64)
         planes_b = keep.tile([P, 2 * J // 4], I32, name="planes_b", align_bytes=64)
         en_planes = keep.tile([P, 2 * N // 4], I32, name="en_planes", align_bytes=64)
@@ -60,12 +57,10 @@ def tile_list_kg_sqd_mix_gelu_kernel(
         identity = keep.tile([P, P], F32, name="identity")
         wb_hbm = wb_words.rearrange("a p n i -> p a (n i)")
 
-        nc.gpsimd.dma_start(b_rows[STAGE:, :], b.rearrange("(s p) -> s p", p=P).unsqueeze(0).to_broadcast([4, N // P, P]))
         nc.vector.memset(tab2_rows, 0)
         nc.vector.memset(warm[:], 0.0)
         make_identity(nc, identity[:])
         nc.vector.memset(planes_a[:, :, 1:, :], 0)
-        nc.vector.memset(b_rows[0:STAGE, :], 0.0)
         nc.vector.memset(planes_b[:], 0)
         nc.vector.memset(en_planes[:], 0)
         nc.scalar.activation(warm[:, 1:2], warm[:, 0:1], ACT.Sqrt)
@@ -96,11 +91,6 @@ def tile_list_kg_sqd_mix_gelu_kernel(
         def place(planes, rows, pieces):
             for q in (0, 2, 1, 3):
                 nc.sync.dma_start(planes[32 * q : 32 * q + 4].rearrange("p (k n) -> p k n", k=pieces), rows(q))
-
-        b_turned = psum.tile([P, P], F32, name="b_turned", tag="bank5")
-        nc.tensor.transpose(b_turned[:], b_rows[:], identity[:])
-        bias = keep.tile([P, N // P], F32, name="bias")
-        nc.scalar.copy(bias[:], b_turned[:, STAGE : STAGE + N // P])
 
         nc.vector.tensor_copy(
             staged[:].bitcast(U8).rearrange("p (t c i) -> p c t i", t=4, i=16),
@@ -134,6 +124,8 @@ def tile_list_kg_sqd_mix_gelu_kernel(
         wa_t.append(after_a.tile([P, PASS], U16, name="wa_second", offset=24064, align_bytes=64))
         deal_wa(wa_t[1], 1)
 
+        b_rows = after_a.tile([P, P], F32, name="b_rows", offset=12800, align_bytes=64)
+        nc.sync.dma_start(b_rows[:], b.rearrange("(s p) -> s p", p=P).unsqueeze(0).to_broadcast([16, N // P, P]))
         en_rows = after_a.tile([32, N // 4], I32, name="en_rows", offset=25088, align_bytes=64)
         nc.sync.dma_start(en_rows[0:32:2, :], en8_scales[0].bitcast(I32))
         nc.sync.dma_start(en_rows[1:32:2, :], en4_scales[0].bitcast(I32))
@@ -297,6 +289,11 @@ def tile_list_kg_sqd_mix_gelu_kernel(
             return CHUNKS[chunks[0]][0], len(chunks) * CHUNKS[chunks[0]][1]
 
         sums = {u: project(*columns(spans[u][0]), spans[u][1]) for u in range(AHEAD)}
+        b_turned = psum.tile([P, P], F32, name="b_turned", tag="bank3")
+        nc.tensor.transpose(b_turned[:], b_rows[:], identity[:])
+        bias = keep.tile([P, N // P], F32, name="bias")
+        nc.scalar.copy(bias[:], b_turned[:, : N // P])
+
         diffs = {}
         for step in range(len(spans)):
             chunks, g = spans[step]

@@ -319,6 +319,8 @@ def tile_list_kg_sqd_mix_gelu_kernel(
                 score(last, g, *packed[g], range(s0, s0 + 2))
         for chunks, banks in GROUPS:
             pieces = [(s0, 2) for s0 in range(0, N // P, 2)]
+            if chunks == (last - 1,):
+                pieces = [(s0, min(3, N // P - s0)) for s0 in range(0, N // P, 3)]
             if last in chunks:
                 pieces[-1:] = [(N // P - 2, 1), (N // P - 1, 1)]
             finish(chunks, pieces)

@@ -194,19 +194,18 @@ def tile_list_kg_sqd_mix_gelu_kernel(
                 hb = psum.tile([P, per_bank, width], F32, name="hb", tag=f"bank{4 + len(ring) % 4}")
                 ring.append(hb)
                 for t in range(t0, t0 + per_bank):
-                    for n0 in range(0, width, P):
-                        for a in range(2):
-                            w0 = (4 * g + 2 * a + 1) * PASS + t * P
-                            s0 = a * J + j0 + n0
-                            nc.tensor.matmul_mx(
-                                out=hb[:, t - t0, n0 : n0 + P],
-                                lhsT=wb_t[g][:, a, t * P : (t + 1) * P].bitcast(FP8X4),
-                                lhsT_scale=scale_a[:, w0 : w0 + P],
-                                rhs=tab2_codes[part][:, a, c0 + n0 : c0 + n0 + P].bitcast(FP4X4),
-                                rhs_scale=scale_b[:, s0 : s0 + P],
-                                start=(a == 0),
-                                stop=(a == 1),
-                            )
+                    for a in range(2):
+                        w0 = (4 * g + 2 * a + 1) * PASS + t * P
+                        s0 = a * J + j0
+                        nc.tensor.matmul_mx(
+                            out=hb[:, t - t0, :],
+                            lhsT=wb_t[g][:, a, t * P : (t + 1) * P].bitcast(FP8X4),
+                            lhsT_scale=scale_a[:, w0 : w0 + P],
+                            rhs=tab2_codes[part][:, a, c0 : c0 + width].bitcast(FP4X4),
+                            rhs_scale=scale_b[:, s0 : s0 + width],
+                            start=(a == 0),
+                            stop=(a == 1),
+                        )
                 sums.extend(hb[:, t - t0, :] for t in range(t0, t0 + per_bank))
             return sums
 

@@ -57,6 +57,7 @@ def tile_list_kg_sqd_mix_gelu_kernel(
         identity = keep.tile([P, P], F32, name="identity")
         wb_hbm = wb_words.rearrange("a p n i -> p a (n i)")
 
+        nc.gpsimd.memset(tab_rows[:], 0)
         nc.vector.memset(tab2_rows, 0)
         nc.vector.memset(warm[:], 0.0)
         make_identity(nc, identity[:])
@@ -70,10 +71,7 @@ def tile_list_kg_sqd_mix_gelu_kernel(
         nc.sync.dma_start(weight_rows[1::2, :], wb_scales.rearrange("a q (g n) -> (q g) a n", g=2).bitcast(I32))
         nc.sync.dma_start(idx[:], offs)
         for q in (0, 2, 1, 3):
-            nc.sync.dma_start(
-                tab_rows[32 * q : 32 * q + 32, :],
-                tab_scales[0, 4 * q : 4 * q + 4, :].bitcast(I32).unsqueeze(0).to_broadcast([8, 4, T // 4]),
-            )
+            nc.sync.dma_start(tab_rows[32 * q : 32 * q + 4, :], tab_scales[0, 4 * q : 4 * q + 4, :].bitcast(I32))
         nc.sync.dma_start(tab_win[:], tab_words[0].rearrange("p t i -> p (t i)").bitcast(I32))
         nc.sync.dma_start(sm_dealt[:], sm.rearrange("(g p t) -> p g t", g=2, t=4))
         nc.sync.dma_start(wa_raw[:], wa_words[0].bitcast(I32))

@@ -70,8 +70,8 @@ def tile_list_kg_sqd_mix_gelu_kernel(
         nc.sync.dma_start(weight_rows[0::2, :], wa_halves.unsqueeze(1).to_broadcast([32, 2, PASS // 4]))
         nc.sync.dma_start(weight_rows[1::2, :], wb_scales.rearrange("a q (g n) -> (q g) a n", g=2).bitcast(I32))
         nc.sync.dma_start(idx[:], offs)
-        for q in (0, 2, 1, 3):
-            nc.sync.dma_start(tab_rows[32 * q : 32 * q + 4, :], tab_scales[0, 4 * q : 4 * q + 4, :].bitcast(I32))
+        for r in range(4):
+            nc.sync.dma_start(tab_rows[r::32, :], tab_scales[0, r::4, :].bitcast(I32))
         nc.sync.dma_start(tab_win[:], tab_words[0].rearrange("p t i -> p (t i)").bitcast(I32))
         nc.sync.dma_start(sm_dealt[:], sm.rearrange("(g p t) -> p g t", g=2, t=4))
         nc.sync.dma_start(wa_raw[:], wa_words[0].bitcast(I32))
@@ -125,13 +125,14 @@ def tile_list_kg_sqd_mix_gelu_kernel(
         b_rows = after_a.tile([P, P], F32, name="b_rows", offset=12800, align_bytes=64)
         nc.sync.dma_start(b_rows[:], b.rearrange("(s p) -> s p", p=P).unsqueeze(0).to_broadcast([16, N // P, P]))
         en_rows = after_a.tile([32, N // 4], I32, name="en_rows", offset=25088, align_bytes=64)
-        nc.sync.dma_start(en_rows[0:32:2, :], en8_scales[0].bitcast(I32))
-        nc.sync.dma_start(en_rows[1:32:2, :], en4_scales[0].bitcast(I32))
+        nc.sync.dma_start(en_rows[0:32:2, :], en8_scales[0].rearrange("(q r) n -> r q n", r=4).bitcast(I32))
+        nc.sync.dma_start(en_rows[1:32:2, :], en4_scales[0].rearrange("(q r) n -> r q n", r=4).bitcast(I32))
         en8_codes = after_c.tile([P, N], I32, name="en8_codes", offset=0, align_bytes=64)
         nc.sync.dma_start(en8_codes[:], en8_words[0].rearrange("p n i -> p (n i)").bitcast(I32))
         en4_codes = after_c.tile([P, N // 2], I32, name="en4_codes", offset=4096, align_bytes=64)
         nc.sync.dma_start(en4_codes[:], en4_words[0].bitcast(I32))
-        place(en_planes, lambda q: en_rows[8 * q : 8 * q + 8, :], 2)
+        for r in range(4):
+            nc.sync.dma_start(en_planes[r::32].rearrange("p (k n) -> p k n", k=2), en_rows[8 * r : 8 * r + 8, :])
 
         scale_a = planes_a[:].rearrange("p g k n -> p (g k n)").bitcast(U8)
         scale_b = planes_b[:].bitcast(U8)

@@ -41,7 +41,7 @@ def tile_list_kg_sqd_mix_gelu_kernel(
 
         idx = keep.tile([P, J // 16], U16, name="idx")
         idx2 = keep.tile([P, J // 16], U16, name="idx2")
-        tab_rows = keep.tile([P, T // 4], I32, name="tab_rows", align_bytes=64)
+        tab_rows = keep.tile([P, 2, T // 4], I32, name="tab_rows", align_bytes=64)
         first = after_a.tile([P, 2192], I32, name="first", offset=4096 - 64, align_bytes=64)
         weight_rows = first[:, : PASS // 4]
         second = after_a.tile([P, 3328], I32, name="second", offset=12800, align_bytes=64)
@@ -57,7 +57,7 @@ def tile_list_kg_sqd_mix_gelu_kernel(
         identity = keep.tile([P, P], F32, name="identity")
         wb_hbm = wb_words.rearrange("a p n i -> p a (n i)")
 
-        nc.gpsimd.memset(tab_rows[:], 0)
+        nc.gpsimd.memset(tab_rows[:, 0, :], 0)
         nc.vector.memset(tab2_rows, 0)
         nc.vector.memset(warm[:], 0.0)
         make_identity(nc, identity[:])
@@ -70,10 +70,11 @@ def tile_list_kg_sqd_mix_gelu_kernel(
         nc.sync.dma_start(weight_rows[0::2, :], wa_halves.unsqueeze(1).to_broadcast([32, 2, PASS // 4]))
         nc.sync.dma_start(weight_rows[1::2, :], wb_scales.rearrange("a q (g n) -> (q g) a n", g=2).bitcast(I32))
         nc.sync.dma_start(idx[:], offs)
-        for r in range(4):
-            nc.sync.dma_start(tab_rows[r::32, :], tab_scales[0, r::4, :].bitcast(I32))
-        nc.sync.dma_start(tab_win[:], tab_words[0].rearrange("p t i -> p (t i)").bitcast(I32))
+        nc.sync.dma_start(tab_rows[0:4], tab_scales[0, 0:8, :].rearrange("(q r) t -> r q t", q=2).bitcast(I32))
+        for q in (2, 3):
+            nc.sync.dma_start(tab_rows[32 * q : 32 * q + 4, 0, :], tab_scales[0, 4 * q : 4 * q + 4, :].bitcast(I32))
         nc.sync.dma_start(sm_dealt[:], sm.rearrange("(g p t) -> p g t", g=2, t=4))
+        nc.sync.dma_start(tab_win[:], tab_words[0].rearrange("p t i -> p (t i)").bitcast(I32))
         nc.sync.dma_start(wa_raw[:], wa_words[0].bitcast(I32))
         nc.sync.dma_start(idx2[:], offs2)
         nc.sync.dma_start(tab2_rows[1::4, :], tab2_scales.rearrange("a q t -> q a t").bitcast(I32))
@@ -84,7 +85,7 @@ def tile_list_kg_sqd_mix_gelu_kernel(
         nc.scalar.activation(size[:].rearrange("p (g t) -> p g t", g=2), sm_dealt[:], ACT.Abs)
         nc.scalar.activation(root[:], size[:], ACT.Sqrt)
         nc.scalar.activation(sign[:].rearrange("p (g t) -> p g t", g=2), sm_dealt[:], ACT.Sign)
-        nc.scalar.activation(warm[:, 0:1], root[:, 0:1], ACT.Gelu_apprx_tanh)
+        nc.scalar.activation(size[:, 0:1], warm[:, 0:1], ACT.Gelu_apprx_tanh)
 
         def place(planes, rows, pieces):
             for q in (0, 2, 1, 3):
@@ -103,7 +104,8 @@ def tile_list_kg_sqd_mix_gelu_kernel(
             nc.sync.dma_start(wb_raw[g], wb_hbm[:, :, 4 * PASS * g : 4 * PASS * (g + 1)].bitcast(I32))
 
         tab_plane = keep.tile([P, J], U8, name="tab_plane", align_bytes=64)
-        nc.vector.tensor_copy(tab_plane[:], tab_rows[:].bitcast(U8).indirect(idx[:]))
+        nc.vector.tensor_copy(tab_rows[32:36, 0, :], tab_rows[0:4, 1, :])
+        nc.vector.tensor_copy(tab_plane[:], tab_rows[:, 0, :].bitcast(U8).indirect(idx[:]))
         tab_codes = keep.tile([P, J], U32, name="tab_codes", align_bytes=64)
         nc.vector.tensor_copy(tab_codes[:], tab_win[:].bitcast(U32).indirect(idx[:]))
 

@@ -23,6 +23,7 @@ BANK = 512
 HALF = J // 2
 AHEAD = 2
 SPANS = [(0, 1), (2,), (3,)]
+HB_BANKS = [(4, 5, 6, 7), (0, 1), (4,), (5,), (6,), (7,)]
 CHUNKS = [(0, 128), (128, 128), (256, 128), (384, 128)]
 GROUPS = [((0, 1), (0, 1, 2, 3)), ((2,), (4, 5)), ((3,), (6, 0, 1, 7))]
 
@@ -35,24 +36,24 @@ def tile_list_kg_sqd_mix_gelu_kernel(
     with ExitStack() as ctx:
         keep = ctx.enter_context(tc.tile_pool(name="keep", bufs=1))
         after_a = ctx.enter_context(tc.tile_pool(name="after_a", bufs=1))
-        after_c = ctx.enter_context(tc.tile_pool(name="after_c", bufs=1))
         work = ctx.enter_context(tc.tile_pool(name="work", bufs=4))
+        words = ctx.enter_context(tc.tile_pool(name="words", bufs=1))
         psum = ctx.enter_context(tc.psum_pool(name="psum", bufs=1))
 
         idx = keep.tile([P, J // 16], U16, name="idx")
         idx2 = keep.tile([P, J // 16], U16, name="idx2")
-        tab_rows = keep.tile([P, 2, T // 4], I32, name="tab_rows", align_bytes=64)
-        first = after_a.tile([P, 2192], I32, name="first", offset=4096 - 64, align_bytes=64)
+        tab_rows = keep.tile([P, 2, T // 4], I32, name="tab_rows", align_bytes=256)
+        first = after_a.tile([P, 2240], I32, name="first", offset=4096 - 256, align_bytes=256)
         weight_rows = first[:, : PASS // 4]
-        second = after_a.tile([P, 3328], I32, name="second", offset=12800, align_bytes=64)
+        second = after_a.tile([P, 4864], I32, name="second", offset=12800, align_bytes=256)
         tab2_rows = second[:, : T // 4]
-        staged = keep.tile([P, PASS // 4], I32, name="staged", align_bytes=64)
-        planes_a = keep.tile([P, 2, 4, PASS // 4], I32, name="planes_a", align_bytes=64)
-        planes_b = keep.tile([P, 2 * J // 4], I32, name="planes_b", align_bytes=64)
-        en_planes = keep.tile([P, 2 * N // 4], I32, name="en_planes", align_bytes=64)
+        staged = keep.tile([P, PASS // 4], I32, name="staged", align_bytes=256)
+        planes_a = keep.tile([P, 2, 4, PASS // 4], I32, name="planes_a", align_bytes=256)
+        planes_b = keep.tile([P, 2 * J // 4], I32, name="planes_b", align_bytes=256)
+        en_planes = keep.tile([P, 2 * N // 4], I32, name="en_planes", align_bytes=256)
         warm = keep.tile([P, 2], F32, name="warm")
-        tab_win = keep.tile([P, T], I32, name="tab_win", align_bytes=64)
-        wa_raw = after_c.tile([P, R // 2], I32, name="wa_raw", offset=3072, align_bytes=64)
+        tab_win = keep.tile([P, T], I32, name="tab_win", align_bytes=256)
+        wa_raw = words.tile([P, R // 2], I32, name="wa_raw", align_bytes=256)
         sm_dealt = keep.tile([P, 2, 4], F32, name="sm_dealt")
         identity = keep.tile([P, P], F32, name="identity")
         wb_hbm = wb_words.rearrange("a p n i -> p a (n i)")
@@ -96,42 +97,42 @@ def tile_list_kg_sqd_mix_gelu_kernel(
             weight_rows.bitcast(U8).rearrange("p (c i t) -> p c t i", t=4, i=16),
         )
         place(planes_a[:].rearrange("p g k n -> p (g k n)"), lambda q: staged[32 * q : 32 * q + 32, :], 8)
-        tab2_win = after_a.tile([P, T], I32, name="tab2_win", offset=0, align_bytes=64)
+        tab2_win = after_a.tile([P, T], I32, name="tab2_win", offset=0, align_bytes=256)
         nc.sync.dma_start(tab2_win[:], tab2_words[0].rearrange("p t i -> p (t i)").bitcast(I32))
-        wb_both = after_a.tile([P, 2, 2, PASS], I32, name="wb_both", offset=4608, align_bytes=64)
+        wb_both = after_a.tile([P, 2, 2, PASS], I32, name="wb_both", offset=4608, align_bytes=256)
         wb_raw = [wb_both[:, g] for g in range(2)]
         for g in range(2):
             nc.sync.dma_start(wb_raw[g], wb_hbm[:, :, 4 * PASS * g : 4 * PASS * (g + 1)].bitcast(I32))
 
-        tab_plane = keep.tile([P, J], U8, name="tab_plane", align_bytes=64)
+        tab_plane = keep.tile([P, J], U8, name="tab_plane", align_bytes=256)
         nc.vector.tensor_copy(tab_rows[32:36, 0, :], tab_rows[0:4, 1, :])
         nc.vector.tensor_copy(tab_plane[:], tab_rows[:, 0, :].bitcast(U8).indirect(idx[:]))
-        tab_codes = keep.tile([P, J], U32, name="tab_codes", align_bytes=64)
+        tab_codes = keep.tile([P, J], U32, name="tab_codes", align_bytes=256)
         nc.vector.tensor_copy(tab_codes[:], tab_win[:].bitcast(U32).indirect(idx[:]))
 
-        def deal_wa(dst, g):
-            nc.vector.tensor_copy(
+        def deal_wa(copy, dst, g):
+            copy(
                 dst[:].rearrange("p (t c i) -> p c t i", t=4, i=8),
                 wa_raw[:].bitcast(U16)[:, g * PASS : (g + 1) * PASS].rearrange("p (c i t) -> p c t i", t=4, i=8),
             )
 
-        wa_t = [keep.tile([P, PASS], U16, name="wa_first", align_bytes=64)]
-        deal_wa(wa_t[0], 0)
+        wa_t = [keep.tile([P, PASS], U16, name="wa_first", align_bytes=256)]
+        deal_wa(nc.vector.tensor_copy, wa_t[0], 0)
 
-        picked2 = keep.tile([P, J // 4], I32, name="picked2", align_bytes=64)
+        picked2 = keep.tile([P, J // 4], I32, name="picked2", align_bytes=256)
         nc.vector.tensor_copy(picked2[:].bitcast(U8), tab2_rows.bitcast(U8).indirect(idx2[:]))
         place(planes_b, lambda q: picked2[32 * q + 1 : 32 * q + 32 : 4, :], 2)
-        wa_t.append(after_a.tile([P, PASS], U16, name="wa_second", offset=24064, align_bytes=64))
-        deal_wa(wa_t[1], 1)
+        wa_t.append(words.tile([P, PASS], U16, name="wa_second", align_bytes=256))
+        deal_wa(nc.scalar.copy, wa_t[1], 1)
 
         b_rows = after_a.tile([P, P], F32, name="b_rows", offset=12800, align_bytes=64)
         nc.sync.dma_start(b_rows[:], b.rearrange("(s p) -> s p", p=P).unsqueeze(0).to_broadcast([16, N // P, P]))
-        en_rows = after_a.tile([32, N // 4], I32, name="en_rows", offset=25088, align_bytes=64)
+        en_rows = after_a.tile([32, N // 4], I32, name="en_rows", offset=25088, align_bytes=256)
         nc.sync.dma_start(en_rows[0:32:2, :], en8_scales[0].rearrange("(q r) n -> r q n", r=4).bitcast(I32))
         nc.sync.dma_start(en_rows[1:32:2, :], en4_scales[0].rearrange("(q r) n -> r q n", r=4).bitcast(I32))
-        en8_codes = after_c.tile([P, N], I32, name="en8_codes", offset=0, align_bytes=64)
+        en8_codes = after_a.tile([P, N], I32, name="en8_codes", offset=26112, align_bytes=256)
         nc.sync.dma_start(en8_codes[:], en8_words[0].rearrange("p n i -> p (n i)").bitcast(I32))
-        en4_codes = after_c.tile([P, N // 2], I32, name="en4_codes", offset=4096, align_bytes=64)
+        en4_codes = after_a.tile([P, N // 2], I32, name="en4_codes", offset=30208, align_bytes=256)
         nc.sync.dma_start(en4_codes[:], en4_words[0].bitcast(I32))
         for r in range(4):
             nc.sync.dma_start(en_planes[r::32].rearrange("p (k n) -> p k n", k=2), en_rows[8 * r : 8 * r + 8, :])
@@ -143,7 +144,7 @@ def tile_list_kg_sqd_mix_gelu_kernel(
 
         head = []
         for g in range(2):
-            rows = keep.tile([P, 4, J], F32, name=f"head{g}")
+            rows = keep.tile([P, 4, J], F32, name=f"head{g}", align_bytes=256)
             for t in range(4):
                 ha = psum.tile([P, BANK], F32, name="ha", tag=f"bank{t}")
                 s0 = (4 * g + 2) * PASS + t * P
@@ -164,9 +165,9 @@ def tile_list_kg_sqd_mix_gelu_kernel(
 
         def gather_tab2(part):
             cols = slice(part * HALF // 16, (part + 1) * HALF // 16)
-            pairs = after_a.tile([P, HALF], U32, name=f"tab2_pairs{part}", offset=13824 + 1024 * part, align_bytes=64)
+            pairs = after_a.tile([P, HALF], U32, name=f"tab2_pairs{part}", offset=13824 + 1024 * part, align_bytes=256)
             nc.vector.tensor_copy(pairs[:], tab2_win[:].bitcast(U32).indirect(idx2[:, cols]))
-            parted = keep.tile([P, 2, HALF], U16, name=f"tab2_codes{part}", align_bytes=64)
+            parted = keep.tile([P, 2, HALF], U16, name=f"tab2_codes{part}", align_bytes=256)
             nc.vector.tensor_copy(
                 parted[:].rearrange("p d (c i) -> p c d i", i=8),
                 pairs[:].bitcast(U16).rearrange("p (c i d) -> p c d i", d=2, i=8),
@@ -174,7 +175,7 @@ def tile_list_kg_sqd_mix_gelu_kernel(
             tab2_codes.append(parted)
 
         def reorder_wb(g):
-            dealt = after_a.tile([P, 2, PASS], I32, name=f"wb_t{g}", offset=15872 + 4096 * g, align_bytes=64)
+            dealt = after_a.tile([P, 2, PASS], I32, name=f"wb_t{g}", offset=15872 + 4096 * g, align_bytes=256)
             nc.vector.tensor_copy(
                 dealt[:].rearrange("p a (t c i) -> p a c t i", t=4, i=4),
                 wb_raw[g].rearrange("p a (c i t) -> p a c t i", t=4, i=4),
@@ -185,15 +186,12 @@ def tile_list_kg_sqd_mix_gelu_kernel(
         reorder_wb(0)
         reorder_wb(1)
 
-        ring = []
-
-        def project(j0, width, g):
+        def project(j0, width, g, banks):
             part, c0 = divmod(j0, HALF)
-            per_bank = BANK // width
+            per_bank = 4 // len(banks)
             sums = []
             for t0 in range(0, 4, per_bank):
-                hb = psum.tile([P, per_bank, width], F32, name="hb", tag=f"bank{4 + len(ring) % 4}")
-                ring.append(hb)
+                hb = psum.tile([P, per_bank, width], F32, name="hb", tag=f"bank{banks[t0 // per_bank]}")
                 for t in range(t0, t0 + per_bank):
                     for a in range(2):
                         w0 = (4 * g + 2 * a + 1) * PASS + t * P
@@ -211,7 +209,7 @@ def tile_list_kg_sqd_mix_gelu_kernel(
             return sums
 
         def difference(sums, j0, width, g):
-            diff = work.tile([P, 4, width], F32, name="diff")
+            diff = work.tile([P, 4, width], F32, name="diff", align_bytes=256)
             for t in range(4):
                 nc.vector.scalar_tensor_tensor(
                     diff[:, t, :], sums[t], root[:, 4 * g + t : 4 * g + t + 1],
@@ -220,7 +218,7 @@ def tile_list_kg_sqd_mix_gelu_kernel(
             return diff
 
         def squared(diff, width, on_vector):
-            square = work.tile([P, width, 4], BF16, name="square", align_bytes=64)
+            square = work.tile([P, width, 4], BF16, name="square", align_bytes=256)
             woven = square[:].rearrange("p (c i) t -> p c t i", i=2)
             planar = diff.rearrange("p t (c i) -> p c t i", i=2)
             if on_vector:
@@ -230,15 +228,15 @@ def tile_list_kg_sqd_mix_gelu_kernel(
             return square
 
         def signed(square, width, g):
-            h = work.tile([P, width, 4], BF16, name="h", align_bytes=64)
+            h = work.tile([P, width, 4], BF16, name="h", align_bytes=256)
             nc.vector.tensor_tensor(
                 h[:], square[:], sign[:, 4 * g : 4 * g + 4].unsqueeze(1).to_broadcast([P, width, 4]), ALU.mult
             )
             return h
 
         def quantised(h, width):
-            codes = work.tile([P, width], U32, name="h_codes", align_bytes=64)
-            scales = work.tile([P, width], U8, name="h_scales", align_bytes=64)
+            codes = work.tile([P, width], U32, name="h_codes", align_bytes=256)
+            scales = work.tile([P, width], U8, name="h_scales", align_bytes=256)
             nc.vector.quantize_mx(out=codes[:].bitcast(FP8X4), scales=scales[:], in_=h[:].rearrange("p j t -> p (j t)"))
             return codes, scales
 
@@ -276,7 +274,7 @@ def tile_list_kg_sqd_mix_gelu_kernel(
             banks = sums_of[chunks]
             per_bank = N // P // len(banks)
             for s0, rows in pieces:
-                res = work.tile([P, rows, width], F32, name="res", bufs=12)
+                res = work.tile([P, rows, width], F32, name="res", bufs=12, align_bytes=256)
                 for s in range(s0, s0 + rows):
                     nc.scalar.activation(
                         res[:, s - s0, :], banks[s // per_bank][:, s % per_bank, :], ACT.Gelu_apprx_tanh, bias=bias[:, s : s + 1]
@@ -288,7 +286,7 @@ def tile_list_kg_sqd_mix_gelu_kernel(
         def columns(chunks):
             return CHUNKS[chunks[0]][0], len(chunks) * CHUNKS[chunks[0]][1]
 
-        sums = {u: project(*columns(spans[u][0]), spans[u][1]) for u in range(AHEAD)}
+        sums = {u: project(*columns(spans[u][0]), spans[u][1], HB_BANKS[u]) for u in range(AHEAD)}
         b_turned = psum.tile([P, P], F32, name="b_turned", tag="bank3")
         nc.tensor.transpose(b_turned[:], b_rows[:], identity[:])
         bias = keep.tile([P, N // P], F32, name="bias")
@@ -302,7 +300,7 @@ def tile_list_kg_sqd_mix_gelu_kernel(
                 gather_tab2(1)
             if step + AHEAD < len(spans):
                 chunks, g = spans[step + AHEAD]
-                sums[step + AHEAD] = project(*columns(chunks), g)
+                sums[step + AHEAD] = project(*columns(chunks), g, HB_BANKS[step + AHEAD])
             if 0 < step < len(spans) - 1:
                 chunks, g = spans[step - 1]
                 for i, c in enumerate(chunks):

@@ -127,10 +127,10 @@ def tile_list_kg_sqd_mix_gelu_kernel(
 
         b_rows = after_a.tile([P, P], F32, name="b_rows", offset=12800, align_bytes=64)
         nc.sync.dma_start(b_rows[:], b.rearrange("(s p) -> s p", p=P).unsqueeze(0).to_broadcast([16, N // P, P]))
-        en_rows = after_a.tile([32, N // 4], I32, name="en_rows", offset=25088, align_bytes=256)
+        en_rows = after_a.tile([32, N // 4], I32, name="en_rows", offset=24064, align_bytes=256)
         nc.sync.dma_start(en_rows[0:32:2, :], en8_scales[0].rearrange("(q r) n -> r q n", r=4).bitcast(I32))
         nc.sync.dma_start(en_rows[1:32:2, :], en4_scales[0].rearrange("(q r) n -> r q n", r=4).bitcast(I32))
-        en8_codes = after_a.tile([P, N], I32, name="en8_codes", offset=26112, align_bytes=256)
+        en8_codes = after_a.tile([P, N], I32, name="en8_codes", offset=25344, align_bytes=256)
         nc.sync.dma_start(en8_codes[:], en8_words[0].rearrange("p n i -> p (n i)").bitcast(I32))
         en4_codes = after_a.tile([P, N // 2], I32, name="en4_codes", offset=30208, align_bytes=256)
         nc.sync.dma_start(en4_codes[:], en4_words[0].bitcast(I32))
@@ -235,7 +235,7 @@ def tile_list_kg_sqd_mix_gelu_kernel(
             return h
 
         def quantised(h, width):
-            codes = work.tile([P, width], U32, name="h_codes", align_bytes=256)
+            codes = after_a.tile([P, width], U32, name="h_codes", bufs=4, offset=32256, align_bytes=256)
             scales = work.tile([P, width], U8, name="h_scales", align_bytes=256)
             nc.vector.quantize_mx(out=codes[:].bitcast(FP8X4), scales=scales[:], in_=h[:].rearrange("p j t -> p (j t)"))
             return codes, scales

from contextlib import ExitStack

import concourse.mybir as mybir
from concourse.masks import make_identity

K, L, R, N, T, J = 512, 1024, 1024, 1024, 1024, 512
FLOPS = 2 * J * (K * R + L * R + R * N)

F32 = mybir.dt.float32
BF16 = mybir.dt.bfloat16
I32 = mybir.dt.int32
U32 = mybir.dt.uint32
U16 = mybir.dt.uint16
U8 = mybir.dt.uint8
FP8X4 = mybir.dt.float8_e4m3fn_x4
FP4X4 = mybir.dt.float4_e2m1fn_x4
ACT = mybir.ActivationFunctionType
ALU = mybir.AluOpType

P = 128
PASS = 512
BANK = 512
HALF = J // 2
AHEAD = 2
SPANS = [(0, 1), (2,), (3,)]
HB_BANKS = [(4, 5, 6, 7), (0, 1), (4,), (5,), (6,), (7,)]
CHUNKS = [(0, 128), (128, 128), (256, 128), (384, 128)]
GROUPS = [((0, 1), (0, 1, 2, 3)), ((2,), (4, 5)), ((3,), (6, 0, 1, 7))]


def tile_list_kg_sqd_mix_gelu_kernel(
    tc, tab_words, tab_scales, tab2_words, tab2_scales, wa_words, wa_scales, wb_words, wb_scales,
    sm, en8_words, en8_scales, en4_words, en4_scales, b, offs, offs2, out,
):
    nc = tc.nc
    with ExitStack() as ctx:
        keep = ctx.enter_context(tc.tile_pool(name="keep", bufs=1))
        after_a = ctx.enter_context(tc.tile_pool(name="after_a", bufs=1))
        work = ctx.enter_context(tc.tile_pool(name="work", bufs=4))
        words = ctx.enter_context(tc.tile_pool(name="words", bufs=1))
        psum = ctx.enter_context(tc.psum_pool(name="psum", bufs=1))

        idx = keep.tile([P, J // 16], U16, name="idx")
        idx2 = keep.tile([P, J // 16], U16, name="idx2")
        tab_rows = keep.tile([P, 2, T // 4], I32, name="tab_rows", align_bytes=256)
        first = after_a.tile([P, 2240], I32, name="first", offset=4096 - 256, align_bytes=256)
        weight_rows = first[:, : PASS // 4]
        second = after_a.tile([P, 4864], I32, name="second", offset=12800, align_bytes=256)
        tab2_rows = second[:, : T // 4]
        staged = keep.tile([P, PASS // 4], I32, name="staged", align_bytes=256)
        planes_a = keep.tile([P, 2, 4, PASS // 4], I32, name="planes_a", align_bytes=256)
        planes_b = keep.tile([P, 2 * J // 4], I32, name="planes_b", align_bytes=256)
        en_planes = keep.tile([P, 2 * N // 4], I32, name="en_planes", align_bytes=256)
        warm = keep.tile([P, 2], F32, name="warm")
        tab_win = keep.tile([P, T], I32, name="tab_win", align_bytes=256)
        wa_raw = words.tile([P, R // 2], I32, name="wa_raw", align_bytes=256)
        sm_dealt = keep.tile([P, 2, 4], F32, name="sm_dealt")
        identity = keep.tile([P, P], F32, name="identity")
        wb_hbm = wb_words.rearrange("a p n i -> p a (n i)")

        nc.gpsimd.memset(tab_rows[:, 0, :], 0)
        nc.vector.memset(tab2_rows, 0)
        nc.vector.memset(warm[:], 0.0)
        make_identity(nc, identity[:])
        nc.vector.memset(planes_a[:, :, 1:, :], 0)
        nc.vector.memset(planes_b[:], 0)
        nc.vector.memset(en_planes[:], 0)
        nc.scalar.activation(warm[:, 1:2], warm[:, 0:1], ACT.Sqrt)

        wa_halves = wa_scales[0].rearrange("q (g n) -> (q g) n", g=2).bitcast(I32)
        nc.sync.dma_start(weight_rows[0::2, :], wa_halves.unsqueeze(1).to_broadcast([32, 2, PASS // 4]))
        nc.sync.dma_start(weight_rows[1::2, :], wb_scales.rearrange("a q (g n) -> (q g) a n", g=2).bitcast(I32))
        nc.sync.dma_start(idx[:], offs)
        nc.sync.dma_start(tab_rows[0:4], tab_scales[0, 0:8, :].rearrange("(q r) t -> r q t", q=2).bitcast(I32))
        for q in (2, 3):
            nc.sync.dma_start(tab_rows[32 * q : 32 * q + 4, 0, :], tab_scales[0, 4 * q : 4 * q + 4, :].bitcast(I32))
        nc.sync.dma_start(sm_dealt[:], sm.rearrange("(g p t) -> p g t", g=2, t=4))
        nc.sync.dma_start(tab_win[:], tab_words[0].rearrange("p t i -> p (t i)").bitcast(I32))
        nc.sync.dma_start(wa_raw[:], wa_words[0].bitcast(I32))
        nc.sync.dma_start(idx2[:], offs2)
        nc.sync.dma_start(tab2_rows[1::4, :], tab2_scales.rearrange("a q t -> q a t").bitcast(I32))

        sign = keep.tile([P, 8], BF16, name="sign")
        size = keep.tile([P, 8], F32, name="size")
        root = keep.tile([P, 8], F32, name="root")
        nc.scalar.activation(size[:].rearrange("p (g t) -> p g t", g=2), sm_dealt[:], ACT.Abs)
        nc.scalar.activation(root[:], size[:], ACT.Sqrt)
        nc.scalar.activation(sign[:].rearrange("p (g t) -> p g t", g=2), sm_dealt[:], ACT.Sign)
        nc.scalar.activation(size[:, 0:1], warm[:, 0:1], ACT.Gelu_apprx_tanh)

        def place(planes, rows, pieces):
            for q in (0, 2, 1, 3):
                nc.sync.dma_start(planes[32 * q : 32 * q + 4].rearrange("p (k n) -> p k n", k=pieces), rows(q))

        nc.vector.tensor_copy(
            staged[:].bitcast(U8).rearrange("p (t c i) -> p c t i", t=4, i=16),
            weight_rows.bitcast(U8).rearrange("p (c i t) -> p c t i", t=4, i=16),
        )
        place(planes_a[:].rearrange("p g k n -> p (g k n)"), lambda q: staged[32 * q : 32 * q + 32, :], 8)
        tab2_win = after_a.tile([P, T], I32, name="tab2_win", offset=0, align_bytes=256)
        nc.sync.dma_start(tab2_win[:], tab2_words[0].rearrange("p t i -> p (t i)").bitcast(I32))
        wb_both = after_a.tile([P, 2, 2, PASS], I32, name="wb_both", offset=4608, align_bytes=256)
        wb_raw = [wb_both[:, g] for g in range(2)]
        for g in range(2):
            nc.sync.dma_start(wb_raw[g], wb_hbm[:, :, 4 * PASS * g : 4 * PASS * (g + 1)].bitcast(I32))

        tab_plane = keep.tile([P, J], U8, name="tab_plane", align_bytes=256)
        nc.vector.tensor_copy(tab_rows[32:36, 0, :], tab_rows[0:4, 1, :])
        nc.vector.tensor_copy(tab_plane[:], tab_rows[:, 0, :].bitcast(U8).indirect(idx[:]))
        tab_codes = keep.tile([P, J], U32, name="tab_codes", align_bytes=256)
        nc.vector.tensor_copy(tab_codes[:], tab_win[:].bitcast(U32).indirect(idx[:]))

        def deal_wa(copy, dst, g):
            copy(
                dst[:].rearrange("p (t c i) -> p c t i", t=4, i=8),
                wa_raw[:].bitcast(U16)[:, g * PASS : (g + 1) * PASS].rearrange("p (c i t) -> p c t i", t=4, i=8),
            )

        wa_t = [keep.tile([P, PASS], U16, name="wa_first", align_bytes=256)]
        deal_wa(nc.vector.tensor_copy, wa_t[0], 0)

        picked2 = keep.tile([P, J // 4], I32, name="picked2", align_bytes=256)
        nc.vector.tensor_copy(picked2[:].bitcast(U8), tab2_rows.bitcast(U8).indirect(idx2[:]))
        place(planes_b, lambda q: picked2[32 * q + 1 : 32 * q + 32 : 4, :], 2)
        wa_t.append(words.tile([P, PASS], U16, name="wa_second", align_bytes=256))
        deal_wa(nc.scalar.copy, wa_t[1], 1)

        b_rows = after_a.tile([P, P], F32, name="b_rows", offset=12800, align_bytes=64)
        nc.sync.dma_start(b_rows[:], b.rearrange("(s p) -> s p", p=P).unsqueeze(0).to_broadcast([16, N // P, P]))
        en_rows = after_a.tile([32, N // 4], I32, name="en_rows", offset=24064, align_bytes=256)
        nc.sync.dma_start(en_rows[0:32:2, :], en8_scales[0].rearrange("(q r) n -> r q n", r=4).bitcast(I32))
        nc.sync.dma_start(en_rows[1:32:2, :], en4_scales[0].rearrange("(q r) n -> r q n", r=4).bitcast(I32))
        en8_codes = after_a.tile([P, N], I32, name="en8_codes", offset=25344, align_bytes=256)
        nc.sync.dma_start(en8_codes[:], en8_words[0].rearrange("p n i -> p (n i)").bitcast(I32))
        en4_codes = after_a.tile([P, N // 2], I32, name="en4_codes", offset=30208, align_bytes=256)
        nc.sync.dma_start(en4_codes[:], en4_words[0].bitcast(I32))
        for r in range(4):
            nc.sync.dma_start(en_planes[r::32].rearrange("p (k n) -> p k n", k=2), en_rows[8 * r : 8 * r + 8, :])

        scale_a = planes_a[:].rearrange("p g k n -> p (g k n)").bitcast(U8)
        scale_b = planes_b[:].bitcast(U8)
        en_scale = en_planes[:].bitcast(U8)
        out_v = out.rearrange("(s p) j -> p s j", p=P)

        head = []
        for g in range(2):
            rows = keep.tile([P, 4, J], F32, name=f"head{g}", align_bytes=256)
            for t in range(4):
                ha = psum.tile([P, BANK], F32, name="ha", tag=f"bank{t}")
                s0 = (4 * g + 2) * PASS + t * P
                nc.tensor.matmul_mx(
                    out=ha[:],
                    lhsT=wa_t[g][:, t * P : (t + 1) * P].bitcast(FP4X4),
                    lhsT_scale=scale_a[:, s0 : s0 + P],
                    rhs=tab_codes[:].bitcast(FP8X4),
                    rhs_scale=tab_plane[:],
                    start=True,
                    stop=True,
                )
                nc.scalar.activation(rows[:, t, :], ha[:], ACT.Copy, scale=root[:, 4 * g + t : 4 * g + t + 1])
            head.append(rows)

        tab2_codes = []
        wb_t = []

        def gather_tab2(part):
            cols = slice(part * HALF // 16, (part + 1) * HALF // 16)
            pairs = after_a.tile([P, HALF], U32, name=f"tab2_pairs{part}", offset=13824 + 1024 * part, align_bytes=256)
            nc.vector.tensor_copy(pairs[:], tab2_win[:].bitcast(U32).indirect(idx2[:, cols]))
            parted = keep.tile([P, 2, HALF], U16, name=f"tab2_codes{part}", align_bytes=256)
            nc.vector.tensor_copy(
                parted[:].rearrange("p d (c i) -> p c d i", i=8),
                pairs[:].bitcast(U16).rearrange("p (c i d) -> p c d i", d=2, i=8),
            )
            tab2_codes.append(parted)

        def reorder_wb(g):
            dealt = after_a.tile([P, 2, PASS], I32, name=f"wb_t{g}", offset=15872 + 4096 * g, align_bytes=256)
            nc.vector.tensor_copy(
                dealt[:].rearrange("p a (t c i) -> p a c t i", t=4, i=4),
                wb_raw[g].rearrange("p a (c i t) -> p a c t i", t=4, i=4),
            )
            wb_t.append(dealt)

        gather_tab2(0)
        reorder_wb(0)
        reorder_wb(1)

        def project(j0, width, g, banks):
            part, c0 = divmod(j0, HALF)
            per_bank = 4 // len(banks)
            sums = []
            for t0 in range(0, 4, per_bank):
                hb = psum.tile([P, per_bank, width], F32, name="hb", tag=f"bank{banks[t0 // per_bank]}")
                for t in range(t0, t0 + per_bank):
                    for a in range(2):
                        w0 = (4 * g + 2 * a + 1) * PASS + t * P
                        s0 = a * J + j0
                        nc.tensor.matmul_mx(
                            out=hb[:, t - t0, :],
                            lhsT=wb_t[g][:, a, t * P : (t + 1) * P].bitcast(FP8X4),
                            lhsT_scale=scale_a[:, w0 : w0 + P],
                            rhs=tab2_codes[part][:, a, c0 : c0 + width].bitcast(FP4X4),
                            rhs_scale=scale_b[:, s0 : s0 + width],
                            start=(a == 0),
                            stop=(a == 1),
                        )
                sums.extend(hb[:, t - t0, :] for t in range(t0, t0 + per_bank))
            return sums

        def difference(sums, j0, width, g):
            diff = work.tile([P, 4, width], F32, name="diff", align_bytes=256)
            for t in range(4):
                nc.vector.scalar_tensor_tensor(
                    diff[:, t, :], sums[t], root[:, 4 * g + t : 4 * g + t + 1],
                    head[g][:, t, j0 : j0 + width], ALU.mult, ALU.subtract,
                )
            return diff

        def squared(diff, width, on_vector):
            square = work.tile([P, width, 4], BF16, name="square", align_bytes=256)
            woven = square[:].rearrange("p (c i) t -> p c t i", i=2)
            planar = diff.rearrange("p t (c i) -> p c t i", i=2)
            if on_vector:
                nc.vector.tensor_tensor(woven, planar, planar, ALU.mult)
            else:
                nc.scalar.activation(woven, planar, ACT.Square)
            return square

        def signed(square, width, g):
            h = work.tile([P, width, 4], BF16, name="h", align_bytes=256)
            nc.vector.tensor_tensor(
                h[:], square[:], sign[:, 4 * g : 4 * g + 4].unsqueeze(1).to_broadcast([P, width, 4]), ALU.mult
            )
            return h

        def quantised(h, width):
            codes = after_a.tile([P, width], U32, name="h_codes", bufs=4, offset=32256, align_bytes=256)
            scales = work.tile([P, width], U8, name="h_scales", align_bytes=256)
            nc.vector.quantize_mx(out=codes[:].bitcast(FP8X4), scales=scales[:], in_=h[:].rearrange("p j t -> p (j t)"))
            return codes, scales

        group_of = {c: (chunks, banks) for chunks, banks in GROUPS for c in chunks}
        sums_of = {}

        def score(c, g, codes, scales, tiles):
            chunks, banks = group_of[c]
            width = CHUNKS[c][1]
            per_bank = N // P // len(banks)
            if chunks not in sums_of:
                sums_of[chunks] = [
                    psum.tile([P, per_bank, len(chunks) * width], F32, name="y", tag=f"bank{bank}") for bank in banks
                ]
            c0 = (c - chunks[0]) * width
            for s in tiles:
                n0 = s * P
                if g == 0:
                    lhs = en8_codes[:, n0 : n0 + P].bitcast(FP8X4)
                else:
                    lhs = en4_codes[:].bitcast(U16)[:, n0 : n0 + P].bitcast(FP4X4)
                nc.tensor.matmul_mx(
                    out=sums_of[chunks][s // per_bank][:, s % per_bank, c0 : c0 + width],
                    lhsT=lhs,
                    lhsT_scale=en_scale[:, g * N + n0 : g * N + n0 + P],
                    rhs=codes[:].bitcast(FP8X4),
                    rhs_scale=scales[:],
                    start=(c == chunks[0] and g == 0 and s % per_bank == 0),
                    stop=(c == chunks[-1] and g == 1 and s % per_bank == per_bank - 1),
                )

        def finish(chunks, pieces):
            j0 = CHUNKS[chunks[0]][0]
            width = len(chunks) * CHUNKS[chunks[0]][1]
            banks = sums_of[chunks]
            per_bank = N // P // len(banks)
            for s0, rows in pieces:
                res = work.tile([P, rows, width], F32, name="res", bufs=12, align_bytes=256)
                for s in range(s0, s0 + rows):
                    nc.scalar.activation(
                        res[:, s - s0, :], banks[s // per_bank][:, s % per_bank, :], ACT.Gelu_apprx_tanh, bias=bias[:, s : s + 1]
                    )
                nc.sync.dma_start(out_v[:, s0 : s0 + rows, j0 : j0 + width], res[:])

        spans = [(chunks, g) for chunks in SPANS for g in range(2)]

        def columns(chunks):
            return CHUNKS[chunks[0]][0], len(chunks) * CHUNKS[chunks[0]][1]

        sums = {u: project(*columns(spans[u][0]), spans[u][1], HB_BANKS[u]) for u in range(AHEAD)}
        b_turned = psum.tile([P, P], F32, name="b_turned", tag="bank3")
        nc.tensor.transpose(b_turned[:], b_rows[:], identity[:])
        bias = keep.tile([P, N // P], F32, name="bias")
        nc.scalar.copy(bias[:], b_turned[:, : N // P])

        diffs = {}
        for step in range(len(spans)):
            chunks, g = spans[step]
            diffs[step] = difference(sums[step], *columns(chunks), g)
            if step == 0:
                gather_tab2(1)
            if step + AHEAD < len(spans):
                chunks, g = spans[step + AHEAD]
                sums[step + AHEAD] = project(*columns(chunks), g, HB_BANKS[step + AHEAD])
            if 0 < step < len(spans) - 1:
                chunks, g = spans[step - 1]
                for i, c in enumerate(chunks):
                    width = CHUNKS[c][1]
                    square = squared(diffs[step - 1][:, :, i * width : (i + 1) * width], width, False)
                    score(c, g, *quantised(signed(square, width, g), width), range(N // P))
        last = len(CHUNKS) - 1
        width = CHUNKS[last][1]
        squares = [squared(diffs[len(spans) - 2 + g][:], width, True) for g in range(2)]
        values = [signed(squares[g], width, g) for g in range(2)]
        packed = [quantised(values[g], width) for g in range(2)]
        for s0 in range(0, N // P, 2):
            for g in range(2):
                score(last, g, *packed[g], range(s0, s0 + 2))
        for chunks, banks in GROUPS:
            pieces = [(s0, 2) for s0 in range(0, N // P, 2)]
            if chunks == (last - 1,):
                pieces = [(s0, min(3, N // P - s0)) for s0 in range(0, N // P, 3)]
            if last in chunks:
                pieces[-1:] = [(N // P - 2, 1), (N // P - 1, 1)]
            finish(chunks, pieces)
